import numpy as np
import ml_dtypes


def mxq(x, axis, fmt="e4m3"):
    dtype, down = {"e4m3": (ml_dtypes.float8_e4m3fn, 7), "e5m2": (ml_dtypes.float8_e5m2, 14)}[fmt]
    v = np.moveaxis(np.asarray(x, np.float32).astype(ml_dtypes.bfloat16).astype(np.float64), axis, -1)
    blocks = v.reshape(v.shape[:-1] + (-1, 32))
    amax = np.abs(blocks).max(-1, keepdims=True)
    byte = np.maximum(np.where(amax > 0, np.frexp(amax)[1] - 1 + 127, 0) - down, 1)
    scale = np.exp2(byte - 127.0)
    codes = (blocks / scale).astype(np.float32).astype(dtype).astype(np.float64)
    return np.moveaxis((codes * scale).reshape(v.shape), -1, axis)


WIDE = False


def mx_kscale(k):
    if not WIDE:
        return np.ones(k)
    levels = np.array([24, -24, 12, -12, 0])
    if k % 512:
        return np.exp2(np.random.permutation(np.resize(levels, k // 32))).repeat(32)
    a = np.empty((k // 512, 16))
    for p in range(k // 512):
        a[p, :8] = np.random.permutation(np.resize(levels, 8))
        for g in range(8):
            far = levels[np.abs(levels - a[p, g]) >= 10]
            a[p, g + 8] = far[np.random.randint(len(far))]
    return np.exp2(a.ravel()).repeat(32)


def f64(x):
    return np.asarray(x).astype(np.float64)


def striped8(idx):
    return np.concatenate([v.reshape(-1, 16).T for v in idx]).astype(np.uint16)


def unstriped8(offs):
    return np.stack([offs[16 * g:16 * g + 16].T.reshape(-1) for g in range(8)]).astype(np.int64)


E2M1 = np.array([0.0, 0.5, 1.0, 1.5, 2.0, 3.0, 4.0, 6.0, -0.0, -0.5, -1.0, -1.5, -2.0, -3.0, -4.0, -6.0])


def pack_weight(w, fmt):
    k, n = w.shape
    w = f64(np.asarray(w, np.float32).astype(ml_dtypes.bfloat16)).reshape(k // 32, 32, n)
    amax = np.abs(w).max(1)
    if fmt == "e4m3":
        byte = np.frexp(amax)[1] - 1 + 127 - 7
    else:
        mant, ex = np.frexp(amax / 6.0)
        byte = np.where(mant > 0.5, ex, ex - 1) + 127
    byte = np.clip(np.where(amax > 0, byte, 1), 1, 254)
    scaled = (w * np.exp2(127.0 - byte)[:, None, :]).reshape(k, n).astype(np.float32)
    by_word = np.ascontiguousarray(scaled.reshape(k // 512, 128, 4, n).transpose(0, 1, 3, 2))
    if fmt == "e4m3":
        words = by_word.astype(ml_dtypes.float8_e4m3fn).view(np.uint8)
    else:
        c = by_word.astype(ml_dtypes.float4_e2m1fn).view(np.uint8) & 0xF
        words = (c[..., 0::2] | (c[..., 1::2] << 4)).reshape(k // 512, 128, 2 * n)
    return np.ascontiguousarray(words), np.ascontiguousarray(byte.astype(np.uint8).reshape(k // 512, 16, n))


def unpack_weight(words, scales, fmt):
    g, _, n = scales.shape
    words = np.ascontiguousarray(words).reshape(g, 128, n, -1)
    if fmt == "e4m3":
        vals = words.view(ml_dtypes.float8_e4m3fn).astype(np.float64)
    else:
        nib = np.empty((g, 128, n, 4), np.uint8)
        nib[..., 0::2] = words & 0xF
        nib[..., 1::2] = words >> 4
        vals = E2M1[nib]
    vals = vals * np.repeat(np.exp2(scales.astype(np.float64) - 127.0), 8, axis=1)[..., None]
    return vals.transpose(0, 1, 3, 2).reshape(g * 512, n)


def gelu(f):
    return 0.5 * f * (1.0 + np.tanh(np.sqrt(2.0 / np.pi) * (f + 0.044715 * f**3)))


K, R, N, T, J = 512, 1024, 512, 2048, 1024


def setup_inputs():
    n = np.random.standard_normal
    s = mx_kscale(K)[:, None]
    u = mx_kscale(R)[:, None]
    p_wg = pack_weight(n((K, R)) / np.sqrt(K) / s, "e2m1")
    p_wu = pack_weight(n((K, R)) / np.sqrt(K) / s * u.T, "e2m1")
    return {
        "xT": (n((K, T)) * s).astype(np.float32),
        "wgt": np.repeat(np.random.uniform(0.5, 2.0, (8, J)), 16, axis=0).astype(np.float32),
        "wg_words": p_wg[0],
        "wg_scales": p_wg[1],
        "wu_words": p_wu[0],
        "wu_scales": p_wu[1],
        "wd": (n((R, N)) / np.sqrt(R) / u).astype(np.float32),
        "offs": striped8(np.stack([np.random.permutation(T)[:J] for _ in range(8)])),
    }


def reference(xT, wgt, wg_words, wg_scales, wu_words, wu_scales, wd, offs):
    idx = unstriped8(offs)
    rows = np.arange(K)
    xg = f64(wgt)[rows // 4 % 128] * f64(xT)[rows[:, None], idx[rows % 512 // 64]]
    xT_ = mxq(xg, 0, "e4m3")
    wg_ = unpack_weight(wg_words, wg_scales, "e2m1")
    wu_ = unpack_weight(wu_words, wu_scales, "e2m1")
    ga = wg_.T @ xT_
    ub = wu_.T @ xT_
    h = gelu(ga) * ub
    h_ = mxq(h, 0, "e4m3")
    wd_ = mxq(f64(wd), 0, "e4m3")
    y = wd_.T @ h_
    return y

@@ -1,0 +1,252 @@
+from contextlib import ExitStack
+
+import concourse.mybir as mybir
+
+K, R, N, T, J = 512, 1024, 512, 2048, 1024
+FLOPS = 2 * K * R * J * 2 + 2 * R * N * J
+
+F32 = mybir.dt.float32
+BF16 = mybir.dt.bfloat16
+I32 = mybir.dt.int32
+U32 = mybir.dt.uint32
+U16 = mybir.dt.uint16
+U8 = mybir.dt.uint8
+FP8X4 = mybir.dt.float8_e4m3fn_x4
+FP4X4 = mybir.dt.float4_e2m1fn_x4
+MULT = mybir.AluOpType.mult
+GELU = mybir.ActivationFunctionType.Gelu_apprx_tanh
+
+P = 128
+PACK = 4
+PASSES = R // (P * PACK)
+GROUP = 256
+GROUPS = J // GROUP
+CHUNK = 128
+N_TILES = N // P
+
+
+def tile_list_gelu_none_kernel(
+    tc, xT, wgt, wg_words, wg_scales, wu_words, wu_scales, wd, offs, out
+):
+    nc = tc.nc
+    with ExitStack() as ctx:
+        keep = ctx.enter_context(tc.tile_pool(name="keep", bufs=1))
+        ring = ctx.enter_context(tc.tile_pool(name="ring", bufs=3))
+        psum = ctx.enter_context(tc.psum_pool(name="psum", bufs=1))
+
+        offsets = keep.tile([P, J // 16], U16, name="offsets")
+        nc.sync.dma_start(offsets[:], offs)
+
+        warm_in = keep.tile([P, 8], F32, name="warm_in")
+        warm_out = keep.tile([P, 8], F32, name="warm_out")
+        nc.vector.memset(warm_in[:], 0.0)
+
+        w_scales = keep.tile([P, 2 * R], U8, name="w_scales", align_bytes=64)
+        nc.vector.memset(w_scales[:].bitcast(I32), 0)
+        for g, src in enumerate((wg_scales, wu_scales)):
+            scales_raw = keep.tile([P, R // 4], I32, name=f"scales_raw{g}")
+            for q in range(4):
+                rows = slice(32 * q, 32 * q + 4)
+                nc.scalar.dma_start(scales_raw[rows, :], src[0, 4 * q : 4 * q + 4, :].bitcast(I32))
+                nc.vector.tensor_copy(
+                    w_scales[rows, g * R : (g + 1) * R].bitcast(I32).rearrange("p (b t s) -> p b t s", t=PACK, s=32),
+                    scales_raw[rows, :].rearrange("p (b s t) -> p b t s", t=PACK, s=32),
+                )
+
+        nc.scalar.activation(warm_out[:], warm_in[:], GELU)
+
+        x_planes = xT.rearrange("(p i) t -> i p t", i=PACK)
+        planes = [keep.tile([P, T], F32, name=f"plane{i}") for i in range(PACK)]
+        weight = keep.tile([P, J], F32, name="weight")
+        nc.sync.dma_start(planes[0][:], x_planes[0])
+        nc.sync.dma_start(weight[:, : J // 2], wgt[:, : J // 2])
+        nc.sync.dma_start(weight[:, J // 2 :], wgt[:, J // 2 :])
+        for i in range(1, PACK):
+            nc.sync.dma_start(planes[i][:], x_planes[i])
+
+        words_raw = keep.tile([P, R], I32, name="words_raw")
+        for g, src in enumerate((wg_words, wu_words)):
+            nc.sync.dma_start(words_raw[:, g * R // 2 : (g + 1) * R // 2], src[0].bitcast(I32))
+
+        wd_rows = wd.rearrange("(b s t e) n -> b e s t n", b=PASSES, t=PACK, e=4)
+        wd_raw = [keep.tile([P, PACK, N], F32, name=f"wd_raw{b}") for b in range(PASSES)]
+        for b in range(PASSES):
+            for e in range(4):
+                nc.sync.dma_start(wd_raw[b][e:P:4, :, :], wd_rows[b, e])
+
+        picked = [keep.tile([P, PACK, 2 * GROUP], F32, name=f"picked{h}") for h in range(GROUPS // 2)]
+        x_bf = [keep.tile([P, GROUP, PACK], BF16, name=f"x_bf{q}", align_bytes=64) for q in range(GROUPS)]
+        x_codes = [keep.tile([P, GROUP], U32, name=f"x_codes{q}", align_bytes=64) for q in range(GROUPS)]
+        x_scales = [keep.tile([P, GROUP], U8, name=f"x_scales{q}", align_bytes=64) for q in range(GROUPS)]
+
+        def gather(i, start, width):
+            h, c = divmod(start, 2 * GROUP)
+            cols = offsets[:, start // 16 : (start + width) // 16]
+            nc.vector.tensor_tensor(
+                picked[h][:, i, c : c + width], planes[i][:].indirect(cols), weight[:, start : start + width], MULT
+            )
+
+        def weave_pair(u, q):
+            h, c = divmod(q * GROUP, 2 * GROUP)
+            nc.scalar.copy(
+                x_bf[q][:, :, 2 * u : 2 * u + 2],
+                picked[h][:, 2 * u : 2 * u + 2, c : c + GROUP].rearrange("p i j -> p j i"),
+            )
+
+        def quantize_x(q):
+            nc.vector.quantize_mx(
+                out=x_codes[q][:].bitcast(FP8X4), scales=x_scales[q][:], in_=x_bf[q][:].rearrange("p j i -> p (j i)")
+            )
+
+        for i in range(PACK - 1):
+            for h in range(GROUPS // 2):
+                gather(i, h * 2 * GROUP, 2 * GROUP)
+                if i == 1:
+                    weave_pair(0, 2 * h)
+                    weave_pair(0, 2 * h + 1)
+        for q in range(GROUPS):
+            gather(PACK - 1, q * GROUP, GROUP)
+            weave_pair(1, q)
+
+        w_codes = keep.tile([P, 4 * R], U8, name="w_codes", align_bytes=64)
+        nc.vector.tensor_copy(
+            w_codes[:].bitcast(I32).rearrange("p (g t s w) -> p g t s w", t=PACK, s=32, w=2),
+            words_raw[:].rearrange("p (g s t w) -> p g t s w", t=PACK, s=32, w=2),
+        )
+
+        wd_bf = [keep.tile([P, N, PACK], BF16, name=f"wd_bf{b}", align_bytes=64) for b in range(PASSES)]
+        wd_codes = [keep.tile([P, N], U32, name=f"wd_codes{b}", align_bytes=64) for b in range(PASSES)]
+        wd_scales = [keep.tile([P, N], U8, name=f"wd_scales{b}", align_bytes=64) for b in range(PASSES)]
+
+        def weave_wd(b):
+            dst = wd_bf[b][:].rearrange("p (c i) t -> p c t i", i=4)
+            src = wd_raw[b][:].rearrange("p t (c i) -> p c t i", i=4)
+            if b == 0:
+                nc.vector.tensor_copy(dst, src)
+            else:
+                nc.scalar.copy(dst, src)
+
+        def quantize_wd(b):
+            nc.vector.quantize_mx(
+                out=wd_codes[b][:].bitcast(FP8X4), scales=wd_scales[b][:], in_=wd_bf[b][:].rearrange("p n t -> p (n t)")
+            )
+
+        def first_product(g, b, q, c, bank):
+            cols = slice(c * CHUNK, (c + 1) * CHUNK)
+            for t in range(PACK):
+                s = (g * PASSES + b) * PACK + t
+                nc.tensor.matmul_mx(
+                    out=bank[:, t, :],
+                    lhsT=w_codes[:, 2 * P * s : 2 * P * (s + 1)].bitcast(FP4X4),
+                    lhsT_scale=w_scales[:, P * s : P * (s + 1)],
+                    rhs=x_codes[q][:, cols].bitcast(FP8X4),
+                    rhs_scale=x_scales[q][:, cols],
+                    start=True,
+                    stop=True,
+                )
+
+        taken = []
+
+        def next_bank(shape):
+            taken.append(shape)
+            return psum.tile(shape, F32, name=f"bank{len(taken) % 8}")
+
+        spans = [(0, 256), (256, 256), (512, 256), (768, 128), (896, 128)]
+        h_bf = {}
+        h_codes = {}
+        h_scales = {}
+
+        def hidden(u, b, c):
+            start, width = spans[u]
+            if c == 0:
+                h_bf[u, b] = keep.tile([P, width, PACK], BF16, name=f"h_bf{u}_{b}", align_bytes=64)
+            q, cq = divmod(start // CHUNK + c, GROUP // CHUNK)
+            gate = next_bank([P, PACK, CHUNK])
+            up = next_bank([P, PACK, CHUNK])
+            first_product(0, b, q, cq, gate)
+            first_product(1, b, q, cq, up)
+            act = ring.tile([P, CHUNK, PACK], F32, name="act")
+            nc.scalar.activation(act[:], gate[:].rearrange("p t j -> p j t"), GELU)
+            nc.vector.tensor_tensor(
+                h_bf[u, b][:, c * CHUNK : (c + 1) * CHUNK, :], up[:].rearrange("p t j -> p j t"), act[:], MULT
+            )
+
+        def quantize_h(u, b):
+            width = spans[u][1]
+            h_codes[u, b] = keep.tile([P, width], U32, name=f"h_codes{u}_{b}", align_bytes=64)
+            h_scales[u, b] = keep.tile([P, width], U8, name=f"h_scales{u}_{b}", align_bytes=64)
+            nc.vector.quantize_mx(
+                out=h_codes[u, b][:].bitcast(FP8X4),
+                scales=h_scales[u, b][:],
+                in_=h_bf[u, b][:].rearrange("p j t -> p (j t)"),
+            )
+
+        out_rows = out.rearrange("(m p) j -> p m j", p=P)
+
+        def down_pass(acc, m, u, b):
+            n_cols = slice(m * P, (m + 1) * P)
+            nc.tensor.matmul_mx(
+                out=acc,
+                lhsT=wd_codes[b][:, n_cols].bitcast(FP8X4),
+                lhsT_scale=wd_scales[b][:, n_cols],
+                rhs=h_codes[u, b][:].bitcast(FP8X4),
+                rhs_scale=h_scales[u, b][:],
+                start=(b == 0),
+                stop=(b == PASSES - 1),
+            )
+
+        def second_product(u):
+            start, width = spans[u]
+            per_bank = 512 // width
+            for first in range(0, N_TILES, per_bank):
+                acc = next_bank([P, per_bank, width])
+                for mm in range(per_bank):
+                    for b in range(PASSES):
+                        down_pass(acc[:, mm, :], first + mm, u, b)
+                result = keep.tile([P, per_bank, width], F32, name=f"result{u}_{first}")
+                if u == 1 and first > 0:
+                    nc.vector.tensor_copy(result[:], acc[:])
+                else:
+                    nc.scalar.copy(result[:], acc[:])
+                nc.sync.dma_start(out_rows[:, first : first + per_bank, start : start + width], result[:])
+
+        def last_product(u):
+            start, width = spans[u]
+            accs = [next_bank([P, width]) for m in range(N_TILES)]
+            for m in range(N_TILES):
+                down_pass(accs[m][:], m, u, 0)
+            quantize_h(u, 1)
+            for m in range(N_TILES):
+                down_pass(accs[m][:], m, u, 1)
+            for half in range(2):
+                result = keep.tile([P, 2, width], F32, name=f"result{u}_{half}")
+                for mm in range(2):
+                    if half == 0:
+                        nc.scalar.copy(result[:, mm, :], accs[mm][:])
+                    else:
+                        nc.vector.tensor_copy(result[:, mm, :], accs[2 + mm][:])
+                queue = nc.scalar if half == 0 else nc.sync
+                queue.dma_start(out_rows[:, 2 * half : 2 * half + 2, start : start + width], result[:])
+
+        steps = [(u, b, c) for u in range(len(spans)) for b in range(PASSES) for c in range(spans[u][1] // CHUNK)]
+        extra = {
+            1: [lambda: quantize_x(1)],
+            2: [lambda: weave_wd(0), lambda: quantize_x(2)],
+            3: [lambda: quantize_x(3), lambda: quantize_wd(0)],
+            5: [lambda: weave_wd(1)],
+            7: [lambda: quantize_wd(1)],
+            8: [lambda: second_product(0)],
+            10: [lambda: second_product(1)],
+            12: [lambda: second_product(2)],
+            14: [lambda: second_product(3)],
+        }
+        quantize_x(0)
+        waiting = None
+        for n, (u, b, c) in enumerate(steps):
+            hidden(u, b, c)
+            if waiting is not None:
+                quantize_h(*waiting)
+            waiting = (u, b) if (c + 1) * CHUNK == spans[u][1] else None
+            for work in extra.get(n, []):
+                work()
+        last_product(len(spans) - 1)

@@ -31,7 +31,7 @@ def tile_list_gelu_none_kernel(
     nc = tc.nc
     with ExitStack() as ctx:
         keep = ctx.enter_context(tc.tile_pool(name="keep", bufs=1))
-        ring = ctx.enter_context(tc.tile_pool(name="ring", bufs=3))
+        ring = ctx.enter_context(tc.tile_pool(name="ring", bufs=4))
         psum = ctx.enter_context(tc.psum_pool(name="psum", bufs=1))
 
         offsets = keep.tile([P, J // 16], U16, name="offsets")
@@ -74,23 +74,21 @@ def tile_list_gelu_none_kernel(
             for e in range(4):
                 nc.sync.dma_start(wd_raw[b][e:P:4, :, :], wd_rows[b, e])
 
-        picked = [keep.tile([P, PACK, 2 * GROUP], F32, name=f"picked{h}") for h in range(GROUPS // 2)]
+        picked = {}
         x_bf = [keep.tile([P, GROUP, PACK], BF16, name=f"x_bf{q}", align_bytes=64) for q in range(GROUPS)]
         x_codes = [keep.tile([P, GROUP], U32, name=f"x_codes{q}", align_bytes=64) for q in range(GROUPS)]
         x_scales = [keep.tile([P, GROUP], U8, name=f"x_scales{q}", align_bytes=64) for q in range(GROUPS)]
 
-        def gather(i, start, width):
-            h, c = divmod(start, 2 * GROUP)
-            cols = offsets[:, start // 16 : (start + width) // 16]
+        def gather(i, q):
+            cols = offsets[:, q * GROUP // 16 : (q + 1) * GROUP // 16]
             nc.vector.tensor_tensor(
-                picked[h][:, i, c : c + width], planes[i][:].indirect(cols), weight[:, start : start + width], MULT
+                picked[q][:, i, :], planes[i][:].indirect(cols), weight[:, q * GROUP : (q + 1) * GROUP], MULT
             )
 
-        def weave_pair(u, q):
-            h, c = divmod(q * GROUP, 2 * GROUP)
+        def weave_x(q):
             nc.scalar.copy(
-                x_bf[q][:, :, 2 * u : 2 * u + 2],
-                picked[h][:, 2 * u : 2 * u + 2, c : c + GROUP].rearrange("p i j -> p j i"),
+                x_bf[q][:].rearrange("p (c e) i -> p c i e", e=4),
+                picked[q][:].rearrange("p i (c e) -> p c i e", e=4),
             )
 
         def quantize_x(q):
@@ -98,15 +96,20 @@ def tile_list_gelu_none_kernel(
                 out=x_codes[q][:].bitcast(FP8X4), scales=x_scales[q][:], in_=x_bf[q][:].rearrange("p j i -> p (j i)")
             )
 
+        early = range(GROUPS - 1)
+        for q in early:
+            picked[q] = keep.tile([P, PACK, GROUP], F32, name=f"picked{q}")
         for i in range(PACK - 1):
-            for h in range(GROUPS // 2):
-                gather(i, h * 2 * GROUP, 2 * GROUP)
-                if i == 1:
-                    weave_pair(0, 2 * h)
-                    weave_pair(0, 2 * h + 1)
-        for q in range(GROUPS):
-            gather(PACK - 1, q * GROUP, GROUP)
-            weave_pair(1, q)
+            for q in early:
+                gather(i, q)
+        for q in early:
+            gather(PACK - 1, q)
+            weave_x(q)
+
+        def gather_late(i):
+            if i == 0:
+                picked[GROUPS - 1] = keep.tile([P, PACK, GROUP], F32, name="picked0")
+            gather(i, GROUPS - 1)
 
         w_codes = keep.tile([P, 4 * R], U8, name="w_codes", align_bytes=64)
         nc.vector.tensor_copy(
@@ -204,10 +207,7 @@ def tile_list_gelu_none_kernel(
                     for b in range(PASSES):
                         down_pass(acc[:, mm, :], first + mm, u, b)
                 result = keep.tile([P, per_bank, width], F32, name=f"result{u}_{first}")
-                if u == 1 and first > 0:
-                    nc.vector.tensor_copy(result[:], acc[:])
-                else:
-                    nc.scalar.copy(result[:], acc[:])
+                nc.scalar.copy(result[:], acc[:])
                 nc.sync.dma_start(out_rows[:, first : first + per_bank, start : start + width], result[:])
 
         def last_product(u):
@@ -230,10 +230,13 @@ def tile_list_gelu_none_kernel(
 
         steps = [(u, b, c) for u in range(len(spans)) for b in range(PASSES) for c in range(spans[u][1] // CHUNK)]
         extra = {
-            1: [lambda: quantize_x(1)],
-            2: [lambda: weave_wd(0), lambda: quantize_x(2)],
-            3: [lambda: quantize_x(3), lambda: quantize_wd(0)],
+            0: [lambda: gather_late(0), lambda: quantize_x(1)],
+            1: [lambda: gather_late(1)],
+            2: [lambda: gather_late(2), lambda: quantize_x(2)],
+            3: [lambda: gather_late(3), lambda: weave_wd(0), lambda: weave_x(3)],
+            4: [lambda: quantize_wd(0)],
             5: [lambda: weave_wd(1)],
+            6: [lambda: quantize_x(3)],
             7: [lambda: quantize_wd(1)],
             8: [lambda: second_product(0)],
             10: [lambda: second_product(1)],

@@ -14,6 +14,7 @@ U8 = mybir.dt.uint8
 FP8X4 = mybir.dt.float8_e4m3fn_x4
 FP4X4 = mybir.dt.float4_e2m1fn_x4
 MULT = mybir.AluOpType.mult
+ADD = mybir.AluOpType.add
 GELU = mybir.ActivationFunctionType.Gelu_apprx_tanh
 
 P = 128
@@ -43,30 +44,38 @@ def tile_list_gelu_none_kernel(
 
         w_scales = keep.tile([P, 2 * R], U8, name="w_scales", align_bytes=64)
         nc.vector.memset(w_scales[:].bitcast(I32), 0)
-        for g, src in enumerate((wg_scales, wu_scales)):
-            scales_raw = keep.tile([P, R // 4], I32, name=f"scales_raw{g}")
-            for q in range(4):
-                rows = slice(32 * q, 32 * q + 4)
-                nc.scalar.dma_start(scales_raw[rows, :], src[0, 4 * q : 4 * q + 4, :].bitcast(I32))
-                nc.vector.tensor_copy(
-                    w_scales[rows, g * R : (g + 1) * R].bitcast(I32).rearrange("p (b t s) -> p b t s", t=PACK, s=32),
-                    scales_raw[rows, :].rearrange("p (b s t) -> p b t s", t=PACK, s=32),
-                )
+        scales_raw = [keep.tile([P, R // 4], I32, name=f"scales_raw{g}") for g in range(2)]
 
-        nc.scalar.activation(warm_out[:], warm_in[:], GELU)
+        def load_scales(queue, g, q):
+            rows = slice(32 * q, 32 * q + 4)
+            queue.dma_start(scales_raw[g][rows, :], (wg_scales, wu_scales)[g][0, 4 * q : 4 * q + 4, :].bitcast(I32))
+            nc.vector.tensor_copy(
+                w_scales[rows, g * R : (g + 1) * R].bitcast(I32).rearrange("p (b t s) -> p b t s", t=PACK, s=32),
+                scales_raw[g][rows, :].rearrange("p (b s t) -> p b t s", t=PACK, s=32),
+            )
 
         x_planes = xT.rearrange("(p i) t -> i p t", i=PACK)
         planes = [keep.tile([P, T], F32, name=f"plane{i}") for i in range(PACK)]
-        weight = keep.tile([P, J], F32, name="weight")
+        early_width = J - GROUP
+        weight_early = keep.tile([P, early_width], F32, name="weight_early")
+        weight_late = keep.tile([P, GROUP], F32, name="weight_late")
+        for q in range(3):
+            load_scales(nc.scalar, 0, q)
+        nc.scalar.activation(warm_out[:], warm_in[:], GELU)
+        load_scales(nc.sync, 0, 3)
+        load_scales(nc.sync, 1, 0)
         nc.sync.dma_start(planes[0][:], x_planes[0])
-        nc.sync.dma_start(weight[:, : J // 2], wgt[:, : J // 2])
-        nc.sync.dma_start(weight[:, J // 2 :], wgt[:, J // 2 :])
+        nc.sync.dma_start(weight_early[:], wgt[:, :early_width])
+        for q in range(1, 4):
+            load_scales(nc.sync, 1, q)
         for i in range(1, PACK):
             nc.sync.dma_start(planes[i][:], x_planes[i])
 
-        words_raw = keep.tile([P, R], I32, name="words_raw")
+        words_raw = keep.tile([P, R], I32, name="words_raw", align_bytes=64)
         for g, src in enumerate((wg_words, wu_words)):
             nc.sync.dma_start(words_raw[:, g * R // 2 : (g + 1) * R // 2], src[0].bitcast(I32))
+
+        nc.sync.dma_start(weight_late[:], wgt[:, early_width:])
 
         wd_rows = wd.rearrange("(b s t e) n -> b e s t n", b=PASSES, t=PACK, e=4)
         wd_raw = [keep.tile([P, PACK, N], F32, name=f"wd_raw{b}") for b in range(PASSES)]
@@ -74,21 +83,19 @@ def tile_list_gelu_none_kernel(
             for e in range(4):
                 nc.sync.dma_start(wd_raw[b][e:P:4, :, :], wd_rows[b, e])
 
-        picked = {}
+        picked_early = keep.tile([P, PACK, early_width], F32, name="picked_early")
         x_bf = [keep.tile([P, GROUP, PACK], BF16, name=f"x_bf{q}", align_bytes=64) for q in range(GROUPS)]
         x_codes = [keep.tile([P, GROUP], U32, name=f"x_codes{q}", align_bytes=64) for q in range(GROUPS)]
         x_scales = [keep.tile([P, GROUP], U8, name=f"x_scales{q}", align_bytes=64) for q in range(GROUPS)]
 
-        def gather(i, q):
-            cols = offsets[:, q * GROUP // 16 : (q + 1) * GROUP // 16]
-            nc.vector.tensor_tensor(
-                picked[q][:, i, :], planes[i][:].indirect(cols), weight[:, q * GROUP : (q + 1) * GROUP], MULT
-            )
+        def gather(dst, i, start, weight):
+            width = weight.shape[1]
+            cols = offsets[:, start // 16 : (start + width) // 16]
+            nc.vector.tensor_tensor(dst, planes[i][:].indirect(cols), weight, MULT)
 
-        def weave_x(q):
+        def weave_x(q, src):
             nc.scalar.copy(
-                x_bf[q][:].rearrange("p (c e) i -> p c i e", e=4),
-                picked[q][:].rearrange("p i (c e) -> p c i e", e=4),
+                x_bf[q][:].rearrange("p (c e) i -> p c i e", e=4), src.rearrange("p i (c e) -> p c i e", e=4)
             )
 
         def quantize_x(q):
@@ -96,20 +103,12 @@ def tile_list_gelu_none_kernel(
                 out=x_codes[q][:].bitcast(FP8X4), scales=x_scales[q][:], in_=x_bf[q][:].rearrange("p j i -> p (j i)")
             )
 
-        early = range(GROUPS - 1)
-        for q in early:
-            picked[q] = keep.tile([P, PACK, GROUP], F32, name=f"picked{q}")
         for i in range(PACK - 1):
-            for q in early:
-                gather(i, q)
-        for q in early:
-            gather(PACK - 1, q)
-            weave_x(q)
-
-        def gather_late(i):
-            if i == 0:
-                picked[GROUPS - 1] = keep.tile([P, PACK, GROUP], F32, name="picked0")
-            gather(i, GROUPS - 1)
+            gather(picked_early[:, i, :], i, 0, weight_early[:])
+        for q in range(GROUPS - 1):
+            cols = slice(q * GROUP, (q + 1) * GROUP)
+            gather(picked_early[:, PACK - 1, cols], PACK - 1, q * GROUP, weight_early[:, cols])
+            weave_x(q, picked_early[:, :, cols])
 
         w_codes = keep.tile([P, 4 * R], U8, name="w_codes", align_bytes=64)
         nc.vector.tensor_copy(
@@ -117,17 +116,22 @@ def tile_list_gelu_none_kernel(
             words_raw[:].rearrange("p (g s t w) -> p g t s w", t=PACK, s=32, w=2),
         )
 
-        wd_bf = [keep.tile([P, N, PACK], BF16, name=f"wd_bf{b}", align_bytes=64) for b in range(PASSES)]
+        picked_late = keep.tile([P, PACK, GROUP], F32, name="words_raw", align_bytes=64)
+
+        def gather_late(i):
+            gather(picked_late[:, i, :], i, early_width, weight_late[:])
+
+        wd_bf = {}
         wd_codes = [keep.tile([P, N], U32, name=f"wd_codes{b}", align_bytes=64) for b in range(PASSES)]
         wd_scales = [keep.tile([P, N], U8, name=f"wd_scales{b}", align_bytes=64) for b in range(PASSES)]
 
         def weave_wd(b):
-            dst = wd_bf[b][:].rearrange("p (c i) t -> p c t i", i=4)
-            src = wd_raw[b][:].rearrange("p t (c i) -> p c t i", i=4)
-            if b == 0:
-                nc.vector.tensor_copy(dst, src)
-            else:
-                nc.scalar.copy(dst, src)
+            wd_bf[b] = keep.tile([P, N, PACK], BF16, name=("words_raw", "wd_bf1")[b], align_bytes=64)
+            for m in range(N_TILES):
+                cols = slice(m * P, (m + 1) * P)
+                nc.gpsimd.tensor_scalar(
+                    wd_bf[b][:, cols, :], wd_raw[b][:, :, cols].rearrange("p t n -> p n t"), 1.0, 0.0, MULT, ADD
+                )
 
         def quantize_wd(b):
             nc.vector.quantize_mx(
@@ -231,17 +235,15 @@ def tile_list_gelu_none_kernel(
         steps = [(u, b, c) for u in range(len(spans)) for b in range(PASSES) for c in range(spans[u][1] // CHUNK)]
         extra = {
             0: [lambda: gather_late(0), lambda: quantize_x(1)],
-            1: [lambda: gather_late(1)],
-            2: [lambda: gather_late(2), lambda: quantize_x(2)],
-            3: [lambda: gather_late(3), lambda: weave_wd(0), lambda: weave_x(3)],
-            4: [lambda: quantize_wd(0)],
-            5: [lambda: weave_wd(1)],
-            6: [lambda: quantize_x(3)],
-            7: [lambda: quantize_wd(1)],
-            8: [lambda: second_product(0)],
-            10: [lambda: second_product(1)],
+            1: [lambda: gather_late(1), lambda: gather_late(2)],
+            2: [lambda: gather_late(3), lambda: quantize_x(2), lambda: weave_x(3, picked_late[:]), lambda: weave_wd(0)],
+            4: [lambda: weave_wd(1), lambda: quantize_wd(0)],
+            5: [lambda: quantize_x(3)],
+            6: [lambda: quantize_wd(1)],
+            7: [lambda: second_product(0)],
+            9: [lambda: second_product(1)],
             12: [lambda: second_product(2)],
-            14: [lambda: second_product(3)],
+            15: [lambda: second_product(3)],
         }
         quantize_x(0)
         waiting = None

@@ -32,7 +32,7 @@ def tile_list_gelu_none_kernel(
     nc = tc.nc
     with ExitStack() as ctx:
         keep = ctx.enter_context(tc.tile_pool(name="keep", bufs=1))
-        ring = ctx.enter_context(tc.tile_pool(name="ring", bufs=4))
+        ring = ctx.enter_context(tc.tile_pool(name="ring", bufs=3))
         psum = ctx.enter_context(tc.psum_pool(name="psum", bufs=1))
 
         offsets = keep.tile([P, J // 16], U16, name="offsets")
@@ -58,7 +58,7 @@ def tile_list_gelu_none_kernel(
         planes = [keep.tile([P, T], F32, name=f"plane{i}") for i in range(PACK)]
         early_width = J - GROUP
         weight_early = keep.tile([P, early_width], F32, name="weight_early")
-        weight_late = keep.tile([P, GROUP], F32, name="weight_late")
+        weight_late = keep.tile([P, GROUP], F32, name="weight_late", align_bytes=64)
         for q in range(3):
             load_scales(nc.scalar, 0, q)
         nc.scalar.activation(warm_out[:], warm_in[:], GELU)
@@ -71,7 +71,7 @@ def tile_list_gelu_none_kernel(
         for i in range(1, PACK):
             nc.sync.dma_start(planes[i][:], x_planes[i])
 
-        words_raw = keep.tile([P, R], I32, name="words_raw", align_bytes=64)
+        words_raw = keep.tile([P, R], I32, name="words_raw")
         for g, src in enumerate((wg_words, wu_words)):
             nc.sync.dma_start(words_raw[:, g * R // 2 : (g + 1) * R // 2], src[0].bitcast(I32))
 
@@ -84,7 +84,7 @@ def tile_list_gelu_none_kernel(
                 nc.sync.dma_start(wd_raw[b][e:P:4, :, :], wd_rows[b, e])
 
         picked_early = keep.tile([P, PACK, early_width], F32, name="picked_early")
-        x_bf = [keep.tile([P, GROUP, PACK], BF16, name=f"x_bf{q}", align_bytes=64) for q in range(GROUPS)]
+        x_bf = {}
         x_codes = [keep.tile([P, GROUP], U32, name=f"x_codes{q}", align_bytes=64) for q in range(GROUPS)]
         x_scales = [keep.tile([P, GROUP], U8, name=f"x_scales{q}", align_bytes=64) for q in range(GROUPS)]
 
@@ -94,8 +94,9 @@ def tile_list_gelu_none_kernel(
             nc.vector.tensor_tensor(dst, planes[i][:].indirect(cols), weight, MULT)
 
         def weave_x(q, src):
+            x_bf[q] = keep.tile([P, GROUP, PACK], BF16, name="h_bf0_0" if q == GROUPS - 1 else f"x_bf{q}", align_bytes=64)
             nc.scalar.copy(
-                x_bf[q][:].rearrange("p (c e) i -> p c i e", e=4), src.rearrange("p i (c e) -> p c i e", e=4)
+                x_bf[q][:].rearrange("p (c e) i -> p c i e", e=2), src.rearrange("p i (c e) -> p c i e", e=2)
             )
 
         def quantize_x(q):
@@ -116,41 +117,43 @@ def tile_list_gelu_none_kernel(
             words_raw[:].rearrange("p (g s t w) -> p g t s w", t=PACK, s=32, w=2),
         )
 
-        picked_late = keep.tile([P, PACK, GROUP], F32, name="words_raw", align_bytes=64)
-
-        def gather_late(i):
-            gather(picked_late[:, i, :], i, early_width, weight_late[:])
-
         wd_bf = {}
         wd_codes = [keep.tile([P, N], U32, name=f"wd_codes{b}", align_bytes=64) for b in range(PASSES)]
         wd_scales = [keep.tile([P, N], U8, name=f"wd_scales{b}", align_bytes=64) for b in range(PASSES)]
 
-        def weave_wd(b):
-            wd_bf[b] = keep.tile([P, N, PACK], BF16, name=("words_raw", "wd_bf1")[b], align_bytes=64)
-            for m in range(N_TILES):
-                cols = slice(m * P, (m + 1) * P)
+        def weave_wd(b, half, slot):
+            wd_bf[b, half] = keep.tile([P, N // 2, PACK], BF16, name=slot, align_bytes=64)
+            for m in range(2):
+                cols = slice((2 * half + m) * P, (2 * half + m + 1) * P)
                 nc.gpsimd.tensor_scalar(
-                    wd_bf[b][:, cols, :], wd_raw[b][:, :, cols].rearrange("p t n -> p n t"), 1.0, 0.0, MULT, ADD
+                    wd_bf[b, half][:, m * P : (m + 1) * P, :],
+                    wd_raw[b][:, :, cols].rearrange("p t n -> p n t"),
+                    1.0,
+                    0.0,
+                    MULT,
+                    ADD,
                 )
 
-        def quantize_wd(b):
+        def quantize_wd(b, half):
+            cols = slice(half * N // 2, (half + 1) * N // 2)
             nc.vector.quantize_mx(
-                out=wd_codes[b][:].bitcast(FP8X4), scales=wd_scales[b][:], in_=wd_bf[b][:].rearrange("p n t -> p (n t)")
+                out=wd_codes[b][:, cols].bitcast(FP8X4),
+                scales=wd_scales[b][:, cols],
+                in_=wd_bf[b, half][:].rearrange("p n t -> p (n t)"),
             )
 
-        def first_product(g, b, q, c, bank):
-            cols = slice(c * CHUNK, (c + 1) * CHUNK)
-            for t in range(PACK):
-                s = (g * PASSES + b) * PACK + t
-                nc.tensor.matmul_mx(
-                    out=bank[:, t, :],
-                    lhsT=w_codes[:, 2 * P * s : 2 * P * (s + 1)].bitcast(FP4X4),
-                    lhsT_scale=w_scales[:, P * s : P * (s + 1)],
-                    rhs=x_codes[q][:, cols].bitcast(FP8X4),
-                    rhs_scale=x_scales[q][:, cols],
-                    start=True,
-                    stop=True,
-                )
+        def first_product(dst, g, b, t, start, width):
+            q, c = divmod(start, GROUP)
+            s = (g * PASSES + b) * PACK + t
+            nc.tensor.matmul_mx(
+                out=dst,
+                lhsT=w_codes[:, 2 * P * s : 2 * P * (s + 1)].bitcast(FP4X4),
+                lhsT_scale=w_scales[:, P * s : P * (s + 1)],
+                rhs=x_codes[q][:, c : c + width].bitcast(FP8X4),
+                rhs_scale=x_scales[q][:, c : c + width],
+                start=True,
+                stop=True,
+            )
 
         taken = []
 
@@ -158,100 +161,121 @@ def tile_list_gelu_none_kernel(
             taken.append(shape)
             return psum.tile(shape, F32, name=f"bank{len(taken) % 8}")
 
-        spans = [(0, 256), (256, 256), (512, 256), (768, 128), (896, 128)]
+        act = {}
         h_bf = {}
         h_codes = {}
         h_scales = {}
+        h_slot = {(1, 1): "stage1", (2, 0): "stage2", (2, 1): "stage3", (3, 0): "stage2", (3, 1): "stage3"}
 
-        def hidden(u, b, c):
-            start, width = spans[u]
+        def hidden(q, b, c):
             if c == 0:
-                h_bf[u, b] = keep.tile([P, width, PACK], BF16, name=f"h_bf{u}_{b}", align_bytes=64)
-            q, cq = divmod(start // CHUNK + c, GROUP // CHUNK)
-            gate = next_bank([P, PACK, CHUNK])
+                act[q, b] = ring.tile([P, PACK, GROUP], F32, name="act")
+                for first in range(0, PACK, 2):
+                    gate = next_bank([P, 2, GROUP])
+                    for t in range(2):
+                        first_product(gate[:, t, :], 0, b, first + t, q * GROUP, GROUP)
+                    nc.scalar.activation(act[q, b][:, first : first + 2, :], gate[:], GELU)
+                h_codes[q, b] = keep.tile([P, GROUP], U32, name=f"h_codes{q}_{b}", align_bytes=64)
+                h_scales[q, b] = keep.tile([P, GROUP], U8, name=f"h_scales{q}_{b}", align_bytes=64)
+            if c == 0 or (q, b) == (GROUPS - 1, PASSES - 1):
+                slot = h_slot.get((q, b), f"h_bf{q}_{b}")
+                h_bf[q, b] = keep.tile([P, GROUP, PACK], BF16, name=slot, align_bytes=64)
             up = next_bank([P, PACK, CHUNK])
-            first_product(0, b, q, cq, gate)
-            first_product(1, b, q, cq, up)
-            act = ring.tile([P, CHUNK, PACK], F32, name="act")
-            nc.scalar.activation(act[:], gate[:].rearrange("p t j -> p j t"), GELU)
+            for t in range(PACK):
+                first_product(up[:, t, :], 1, b, t, q * GROUP + c * CHUNK, CHUNK)
+            cols = slice(c * CHUNK, (c + 1) * CHUNK)
             nc.vector.tensor_tensor(
-                h_bf[u, b][:, c * CHUNK : (c + 1) * CHUNK, :], up[:].rearrange("p t j -> p j t"), act[:], MULT
+                h_bf[q, b][:, cols, :].rearrange("p (c e) t -> p c t e", e=2),
+                up[:].rearrange("p t (c e) -> p c t e", e=2),
+                act[q, b][:, :, cols].rearrange("p t (c e) -> p c t e", e=2),
+                MULT,
             )
 
-        def quantize_h(u, b):
-            width = spans[u][1]
-            h_codes[u, b] = keep.tile([P, width], U32, name=f"h_codes{u}_{b}", align_bytes=64)
-            h_scales[u, b] = keep.tile([P, width], U8, name=f"h_scales{u}_{b}", align_bytes=64)
+        def quantize_h(q, b, cols):
             nc.vector.quantize_mx(
-                out=h_codes[u, b][:].bitcast(FP8X4),
-                scales=h_scales[u, b][:],
-                in_=h_bf[u, b][:].rearrange("p j t -> p (j t)"),
+                out=h_codes[q, b][:, cols].bitcast(FP8X4),
+                scales=h_scales[q, b][:, cols],
+                in_=h_bf[q, b][:, cols, :].rearrange("p j t -> p (j t)"),
             )
 
         out_rows = out.rearrange("(m p) j -> p m j", p=P)
 
-        def down_pass(acc, m, u, b):
+        def down_pass(acc, m, q, b, cols):
             n_cols = slice(m * P, (m + 1) * P)
             nc.tensor.matmul_mx(
                 out=acc,
                 lhsT=wd_codes[b][:, n_cols].bitcast(FP8X4),
                 lhsT_scale=wd_scales[b][:, n_cols],
-                rhs=h_codes[u, b][:].bitcast(FP8X4),
-                rhs_scale=h_scales[u, b][:],
+                rhs=h_codes[q, b][:, cols].bitcast(FP8X4),
+                rhs_scale=h_scales[q, b][:, cols],
                 start=(b == 0),
                 stop=(b == PASSES - 1),
             )
 
-        def second_product(u):
-            start, width = spans[u]
+        def second_product(q, cols):
+            width = cols.stop - cols.start
+            tokens = slice(q * GROUP + cols.start, q * GROUP + cols.stop)
             per_bank = 512 // width
             for first in range(0, N_TILES, per_bank):
                 acc = next_bank([P, per_bank, width])
                 for mm in range(per_bank):
                     for b in range(PASSES):
-                        down_pass(acc[:, mm, :], first + mm, u, b)
-                result = keep.tile([P, per_bank, width], F32, name=f"result{u}_{first}")
+                        down_pass(acc[:, mm, :], first + mm, q, b, cols)
+                result = keep.tile([P, per_bank, width], F32, name=f"result{q}_{first}")
                 nc.scalar.copy(result[:], acc[:])
-                nc.sync.dma_start(out_rows[:, first : first + per_bank, start : start + width], result[:])
+                nc.sync.dma_start(out_rows[:, first : first + per_bank, tokens], result[:])
 
-        def last_product(u):
-            start, width = spans[u]
-            accs = [next_bank([P, width]) for m in range(N_TILES)]
+        def last_product(q, cols):
+            tokens = slice(q * GROUP + cols.start, q * GROUP + cols.stop)
+            accs = [next_bank([P, CHUNK]) for m in range(N_TILES)]
             for m in range(N_TILES):
-                down_pass(accs[m][:], m, u, 0)
-            quantize_h(u, 1)
+                down_pass(accs[m][:], m, q, 0, cols)
+            quantize_h(q, 1, cols)
             for m in range(N_TILES):
-                down_pass(accs[m][:], m, u, 1)
+                down_pass(accs[m][:], m, q, 1, cols)
             for half in range(2):
-                result = keep.tile([P, 2, width], F32, name=f"result{u}_{half}")
+                result = keep.tile([P, 2, CHUNK], F32, name=f"last_result{half}")
                 for mm in range(2):
                     if half == 0:
-                        nc.scalar.copy(result[:, mm, :], accs[mm][:])
+                        nc.vector.tensor_copy(result[:, mm, :], accs[mm][:])
                     else:
-                        nc.vector.tensor_copy(result[:, mm, :], accs[2 + mm][:])
-                queue = nc.scalar if half == 0 else nc.sync
-                queue.dma_start(out_rows[:, 2 * half : 2 * half + 2, start : start + width], result[:])
+                        nc.scalar.copy(result[:, mm, :], accs[2 + mm][:])
+                queue = nc.sync if half == 0 else nc.scalar
+                queue.dma_start(out_rows[:, 2 * half : 2 * half + 2, tokens], result[:])
 
-        steps = [(u, b, c) for u in range(len(spans)) for b in range(PASSES) for c in range(spans[u][1] // CHUNK)]
-        extra = {
-            0: [lambda: gather_late(0), lambda: quantize_x(1)],
-            1: [lambda: gather_late(1), lambda: gather_late(2)],
-            2: [lambda: gather_late(3), lambda: quantize_x(2), lambda: weave_x(3, picked_late[:]), lambda: weave_wd(0)],
-            4: [lambda: weave_wd(1), lambda: quantize_wd(0)],
-            5: [lambda: quantize_x(3)],
-            6: [lambda: quantize_wd(1)],
-            7: [lambda: second_product(0)],
-            9: [lambda: second_product(1)],
-            12: [lambda: second_product(2)],
-            15: [lambda: second_product(3)],
-        }
+        whole = slice(0, GROUP)
+        chunks = [slice(0, CHUNK), slice(CHUNK, GROUP)]
+        last = GROUPS - 1
         quantize_x(0)
-        waiting = None
-        for n, (u, b, c) in enumerate(steps):
-            hidden(u, b, c)
-            if waiting is not None:
-                quantize_h(*waiting)
-            waiting = (u, b) if (c + 1) * CHUNK == spans[u][1] else None
-            for work in extra.get(n, []):
-                work()
-        last_product(len(spans) - 1)
+        picked_late = keep.tile([P, PACK, GROUP], F32, name="x_bf0", align_bytes=64)
+        for i in range(PACK):
+            gather(picked_late[:, i, :], i, early_width, weight_late[:])
+        weave_wd(0, 0, "weight_late")
+        weave_wd(0, 1, "stage1")
+        weave_wd(1, 0, "stage2")
+        weave_wd(1, 1, "stage3")
+        for q in range(GROUPS):
+            hidden(q, 0, 0)
+            if q > 0:
+                quantize_h(q - 1, 1, whole)
+            hidden(q, 0, 1)
+            if q == 1:
+                quantize_wd(0, 0)
+                quantize_wd(0, 1)
+            if q > 1:
+                second_product(q - 2, whole)
+            hidden(q, 1, 0)
+            quantize_h(q, 0, whole)
+            if q == 1:
+                weave_x(last, picked_late[:])
+            if q < last:
+                quantize_x(q + 1)
+            if q == last:
+                quantize_h(last, 1, chunks[0])
+            hidden(q, 1, 1)
+            if q == 1:
+                quantize_wd(1, 0)
+                quantize_wd(1, 1)
+        second_product(last - 1, whole)
+        second_product(last, chunks[0])
+        last_product(last, chunks[1])

@@ -20,10 +20,12 @@ GELU = mybir.ActivationFunctionType.Gelu_apprx_tanh
 P = 128
 PACK = 4
 PASSES = R // (P * PACK)
-GROUP = 256
-GROUPS = J // GROUP
+BANK = 512
 CHUNK = 128
 N_TILES = N // P
+WIDTHS = (128, 256, 256, 256, 128)
+STARTS = tuple(sum(WIDTHS[:q]) for q in range(len(WIDTHS)))
+GROUPS = len(WIDTHS)
 
 
 def tile_list_gelu_none_kernel(
@@ -32,107 +34,101 @@ def tile_list_gelu_none_kernel(
     nc = tc.nc
     with ExitStack() as ctx:
         keep = ctx.enter_context(tc.tile_pool(name="keep", bufs=1))
-        ring = ctx.enter_context(tc.tile_pool(name="ring", bufs=3))
         psum = ctx.enter_context(tc.psum_pool(name="psum", bufs=1))
 
         offsets = keep.tile([P, J // 16], U16, name="offsets")
         nc.sync.dma_start(offsets[:], offs)
 
-        warm_in = keep.tile([P, 8], F32, name="warm_in")
-        warm_out = keep.tile([P, 8], F32, name="warm_out")
-        nc.vector.memset(warm_in[:], 0.0)
-
         w_scales = keep.tile([P, 2 * R], U8, name="w_scales", align_bytes=64)
         nc.vector.memset(w_scales[:].bitcast(I32), 0)
         scales_raw = [keep.tile([P, R // 4], I32, name=f"scales_raw{g}") for g in range(2)]
+        for g, src in enumerate((wg_scales, wu_scales)):
+            for q in range(4):
+                rows = slice(32 * q, 32 * q + 4)
+                nc.scalar.dma_start(scales_raw[g][rows, :], src[0, 4 * q : 4 * q + 4, :].bitcast(I32))
+                nc.vector.tensor_copy(
+                    w_scales[rows, g * R : (g + 1) * R].bitcast(I32).rearrange("p (b t s) -> p b t s", t=PACK, s=32),
+                    scales_raw[g][rows, :].rearrange("p (b s t) -> p b t s", t=PACK, s=32),
+                )
 
-        def load_scales(queue, g, q):
-            rows = slice(32 * q, 32 * q + 4)
-            queue.dma_start(scales_raw[g][rows, :], (wg_scales, wu_scales)[g][0, 4 * q : 4 * q + 4, :].bitcast(I32))
-            nc.vector.tensor_copy(
-                w_scales[rows, g * R : (g + 1) * R].bitcast(I32).rearrange("p (b t s) -> p b t s", t=PACK, s=32),
-                scales_raw[g][rows, :].rearrange("p (b s t) -> p b t s", t=PACK, s=32),
-            )
+        warm_in = keep.tile([P, 8], F32, name="warm_in")
+        warm_out = keep.tile([P, 8], F32, name="warm_out")
+        nc.vector.memset(warm_in[:], 0.0)
+        nc.scalar.activation(warm_out[:], warm_in[:], GELU)
 
         x_planes = xT.rearrange("(p i) t -> i p t", i=PACK)
         planes = [keep.tile([P, T], F32, name=f"plane{i}") for i in range(PACK)]
-        early_width = J - GROUP
-        weight_early = keep.tile([P, early_width], F32, name="weight_early")
-        weight_late = keep.tile([P, GROUP], F32, name="weight_late", align_bytes=64)
-        for q in range(3):
-            load_scales(nc.scalar, 0, q)
-        nc.scalar.activation(warm_out[:], warm_in[:], GELU)
-        load_scales(nc.sync, 0, 3)
-        load_scales(nc.sync, 1, 0)
+        weight = keep.tile([P, J], F32, name="weight")
         nc.sync.dma_start(planes[0][:], x_planes[0])
-        nc.sync.dma_start(weight_early[:], wgt[:, :early_width])
-        for q in range(1, 4):
-            load_scales(nc.sync, 1, q)
+        nc.sync.dma_start(weight[:], wgt)
         for i in range(1, PACK):
             nc.sync.dma_start(planes[i][:], x_planes[i])
 
-        words_raw = keep.tile([P, R], I32, name="words_raw")
+        words_raw = [keep.tile([P, R // 2], I32, name=f"words_raw{g}") for g in range(2)]
         for g, src in enumerate((wg_words, wu_words)):
-            nc.sync.dma_start(words_raw[:, g * R // 2 : (g + 1) * R // 2], src[0].bitcast(I32))
+            nc.sync.dma_start(words_raw[g][:], src[0].bitcast(I32))
 
-        nc.sync.dma_start(weight_late[:], wgt[:, early_width:])
-
-        wd_rows = wd.rearrange("(b s t e) n -> b e s t n", b=PASSES, t=PACK, e=4)
+        wd_rows = wd.rearrange("(b s t e) n -> b t s (e n)", b=PASSES, t=PACK, e=4)
         wd_raw = [keep.tile([P, PACK, N], F32, name=f"wd_raw{b}") for b in range(PASSES)]
         for b in range(PASSES):
-            for e in range(4):
-                nc.sync.dma_start(wd_raw[b][e:P:4, :, :], wd_rows[b, e])
+            for t in range(PACK):
+                nc.sync.dma_start(wd_raw[b][:, t, :], wd_rows[b, t])
 
-        picked_early = keep.tile([P, PACK, early_width], F32, name="picked_early")
-        x_bf = {}
-        x_codes = [keep.tile([P, GROUP], U32, name=f"x_codes{q}", align_bytes=64) for q in range(GROUPS)]
-        x_scales = [keep.tile([P, GROUP], U8, name=f"x_scales{q}", align_bytes=64) for q in range(GROUPS)]
-
-        def gather(dst, i, start, weight):
-            width = weight.shape[1]
+        def gather(dst, i, start, width):
             cols = offsets[:, start // 16 : (start + width) // 16]
-            nc.vector.tensor_tensor(dst, planes[i][:].indirect(cols), weight, MULT)
+            nc.vector.tensor_tensor(dst, planes[i][:].indirect(cols), weight[:, start : start + width], MULT)
 
-        def weave_x(q, src):
-            x_bf[q] = keep.tile([P, GROUP, PACK], BF16, name="h_bf0_0" if q == GROUPS - 1 else f"x_bf{q}", align_bytes=64)
+        picked_low = keep.tile([P, 2, J], F32, name="picked_low")
+        picked_high = [keep.tile([P, 2, w], F32, name=f"picked_high{q}") for q, w in enumerate(WIDTHS)]
+        x_bf = [keep.tile([P, w, PACK], BF16, name=f"x_bf{q}", align_bytes=64) for q, w in enumerate(WIDTHS)]
+        x_codes = [keep.tile([P, w], U32, name=f"x_codes{q}", align_bytes=64) for q, w in enumerate(WIDTHS)]
+        x_scales = [keep.tile([P, w], U8, name=f"x_scales{q}", align_bytes=64) for q, w in enumerate(WIDTHS)]
+
+        def weave_pair(q, first, src):
             nc.scalar.copy(
-                x_bf[q][:].rearrange("p (c e) i -> p c i e", e=2), src.rearrange("p i (c e) -> p c i e", e=2)
+                x_bf[q][:, :, first : first + 2].rearrange("p (c e) i -> p c i e", e=2),
+                src.rearrange("p i (c e) -> p c i e", e=2),
             )
+
+        for i in range(2):
+            gather(picked_low[:, i, :], i, 0, J)
+        for q in range(GROUPS):
+            weave_pair(q, 0, picked_low[:, :, STARTS[q] : STARTS[q] + WIDTHS[q]])
+        for q in range(GROUPS):
+            gather(picked_high[q][:, 0, :], 2, STARTS[q], WIDTHS[q])
+
+        def finish_x(q):
+            gather(picked_high[q][:, 1, :], 3, STARTS[q], WIDTHS[q])
+            weave_pair(q, 2, picked_high[q][:])
 
         def quantize_x(q):
             nc.vector.quantize_mx(
                 out=x_codes[q][:].bitcast(FP8X4), scales=x_scales[q][:], in_=x_bf[q][:].rearrange("p j i -> p (j i)")
             )
 
-        for i in range(PACK - 1):
-            gather(picked_early[:, i, :], i, 0, weight_early[:])
-        for q in range(GROUPS - 1):
-            cols = slice(q * GROUP, (q + 1) * GROUP)
-            gather(picked_early[:, PACK - 1, cols], PACK - 1, q * GROUP, weight_early[:, cols])
-            weave_x(q, picked_early[:, :, cols])
+        w_codes = [keep.tile([P, 2 * R], U8, name=f"w_codes{g}", align_bytes=64) for g in range(2)]
 
-        w_codes = keep.tile([P, 4 * R], U8, name="w_codes", align_bytes=64)
-        nc.vector.tensor_copy(
-            w_codes[:].bitcast(I32).rearrange("p (g t s w) -> p g t s w", t=PACK, s=32, w=2),
-            words_raw[:].rearrange("p (g s t w) -> p g t s w", t=PACK, s=32, w=2),
-        )
+        def order_words(g):
+            nc.vector.tensor_copy(
+                w_codes[g][:].bitcast(I32).rearrange("p (b t s w) -> p b t s w", t=PACK, s=32, w=2),
+                words_raw[g][:].rearrange("p (b s t w) -> p b t s w", t=PACK, s=32, w=2),
+            )
 
         wd_bf = {}
         wd_codes = [keep.tile([P, N], U32, name=f"wd_codes{b}", align_bytes=64) for b in range(PASSES)]
         wd_scales = [keep.tile([P, N], U8, name=f"wd_scales{b}", align_bytes=64) for b in range(PASSES)]
 
-        def weave_wd(b, half, slot):
-            wd_bf[b, half] = keep.tile([P, N // 2, PACK], BF16, name=slot, align_bytes=64)
-            for m in range(2):
-                cols = slice((2 * half + m) * P, (2 * half + m + 1) * P)
-                nc.gpsimd.tensor_scalar(
-                    wd_bf[b, half][:, m * P : (m + 1) * P, :],
-                    wd_raw[b][:, :, cols].rearrange("p t n -> p n t"),
-                    1.0,
-                    0.0,
-                    MULT,
-                    ADD,
-                )
+        def weave_wd(b, half):
+            wd_bf[b, half] = keep.tile([P, N // 2, PACK], BF16, name=f"wd_bf{b}_{half}", align_bytes=64)
+            cols = slice(half * N // 2, (half + 1) * N // 2)
+            nc.gpsimd.tensor_scalar(
+                wd_bf[b, half][:],
+                wd_raw[b][:, :, cols].rearrange("p t n -> p n t"),
+                1.0,
+                0.0,
+                MULT,
+                ADD,
+            )
 
         def quantize_wd(b, half):
             cols = slice(half * N // 2, (half + 1) * N // 2)
@@ -142,140 +138,122 @@ def tile_list_gelu_none_kernel(
                 in_=wd_bf[b, half][:].rearrange("p n t -> p (n t)"),
             )
 
-        def first_product(dst, g, b, t, start, width):
-            q, c = divmod(start, GROUP)
-            s = (g * PASSES + b) * PACK + t
+        def first_product(dst, g, b, t, q, cols):
+            s = b * PACK + t
             nc.tensor.matmul_mx(
                 out=dst,
-                lhsT=w_codes[:, 2 * P * s : 2 * P * (s + 1)].bitcast(FP4X4),
-                lhsT_scale=w_scales[:, P * s : P * (s + 1)],
-                rhs=x_codes[q][:, c : c + width].bitcast(FP8X4),
-                rhs_scale=x_scales[q][:, c : c + width],
+                lhsT=w_codes[g][:, 2 * P * s : 2 * P * (s + 1)].bitcast(FP4X4),
+                lhsT_scale=w_scales[:, g * R + P * s : g * R + P * (s + 1)],
+                rhs=x_codes[q][:, cols].bitcast(FP8X4),
+                rhs_scale=x_scales[q][:, cols],
                 start=True,
                 stop=True,
             )
-
-        taken = []
-
-        def next_bank(shape):
-            taken.append(shape)
-            return psum.tile(shape, F32, name=f"bank{len(taken) % 8}")
 
         act = {}
         h_bf = {}
         h_codes = {}
         h_scales = {}
-        h_slot = {(1, 1): "stage1", (2, 0): "stage2", (2, 1): "stage3", (3, 0): "stage2", (3, 1): "stage3"}
 
-        def hidden(q, b, c):
-            if c == 0:
-                act[q, b] = ring.tile([P, PACK, GROUP], F32, name="act")
-                for first in range(0, PACK, 2):
-                    gate = next_bank([P, 2, GROUP])
-                    for t in range(2):
-                        first_product(gate[:, t, :], 0, b, first + t, q * GROUP, GROUP)
-                    nc.scalar.activation(act[q, b][:, first : first + 2, :], gate[:], GELU)
-                h_codes[q, b] = keep.tile([P, GROUP], U32, name=f"h_codes{q}_{b}", align_bytes=64)
-                h_scales[q, b] = keep.tile([P, GROUP], U8, name=f"h_scales{q}_{b}", align_bytes=64)
-            if c == 0 or (q, b) == (GROUPS - 1, PASSES - 1):
-                slot = h_slot.get((q, b), f"h_bf{q}_{b}")
-                h_bf[q, b] = keep.tile([P, GROUP, PACK], BF16, name=slot, align_bytes=64)
-            up = next_bank([P, PACK, CHUNK])
-            for t in range(PACK):
-                first_product(up[:, t, :], 1, b, t, q * GROUP + c * CHUNK, CHUNK)
+        def gate(q, b):
+            width = WIDTHS[q]
+            per_bank = BANK // width
+            act[q, b] = keep.tile([P, PACK, width], F32, name=f"act{q}_{b}")
+            h_bf[q, b] = keep.tile([P, width, PACK], BF16, name=f"h_bf{q}_{b}", align_bytes=64)
+            h_codes[q, b] = keep.tile([P, width], U32, name=f"h_codes{q}_{b}", align_bytes=64)
+            h_scales[q, b] = keep.tile([P, width], U8, name=f"h_scales{q}_{b}", align_bytes=64)
+            for first in range(0, PACK, per_bank):
+                bank = psum.tile([P, per_bank, width], F32, name="gate_bank", bufs=3)
+                for t in range(per_bank):
+                    first_product(bank[:, t, :], 0, b, first + t, q, slice(0, width))
+                nc.scalar.activation(act[q, b][:, first : first + per_bank, :], bank[:], GELU)
+
+        def up(q, b, c):
             cols = slice(c * CHUNK, (c + 1) * CHUNK)
+            bank = psum.tile([P, PACK, CHUNK], F32, name="up_bank", bufs=3)
+            for t in range(PACK):
+                first_product(bank[:, t, :], 1, b, t, q, cols)
             nc.vector.tensor_tensor(
                 h_bf[q, b][:, cols, :].rearrange("p (c e) t -> p c t e", e=2),
-                up[:].rearrange("p t (c e) -> p c t e", e=2),
+                bank[:].rearrange("p t (c e) -> p c t e", e=2),
                 act[q, b][:, :, cols].rearrange("p t (c e) -> p c t e", e=2),
                 MULT,
             )
 
-        def quantize_h(q, b, cols):
+        def quantize_h(q, b):
             nc.vector.quantize_mx(
-                out=h_codes[q, b][:, cols].bitcast(FP8X4),
-                scales=h_scales[q, b][:, cols],
-                in_=h_bf[q, b][:, cols, :].rearrange("p j t -> p (j t)"),
+                out=h_codes[q, b][:].bitcast(FP8X4),
+                scales=h_scales[q, b][:],
+                in_=h_bf[q, b][:].rearrange("p j t -> p (j t)"),
             )
 
         out_rows = out.rearrange("(m p) j -> p m j", p=P)
 
-        def down_pass(acc, m, q, b, cols):
+        def down_pass(acc, m, q, b, start, stop):
             n_cols = slice(m * P, (m + 1) * P)
             nc.tensor.matmul_mx(
                 out=acc,
                 lhsT=wd_codes[b][:, n_cols].bitcast(FP8X4),
                 lhsT_scale=wd_scales[b][:, n_cols],
-                rhs=h_codes[q, b][:, cols].bitcast(FP8X4),
-                rhs_scale=h_scales[q, b][:, cols],
-                start=(b == 0),
-                stop=(b == PASSES - 1),
+                rhs=h_codes[q, b][:].bitcast(FP8X4),
+                rhs_scale=h_scales[q, b][:],
+                start=start,
+                stop=stop,
             )
 
-        def second_product(q, cols):
-            width = cols.stop - cols.start
-            tokens = slice(q * GROUP + cols.start, q * GROUP + cols.stop)
-            per_bank = 512 // width
+        def down(q):
+            width = WIDTHS[q]
+            tokens = slice(STARTS[q], STARTS[q] + width)
+            per_bank = BANK // width
             for first in range(0, N_TILES, per_bank):
-                acc = next_bank([P, per_bank, width])
+                acc = psum.tile([P, per_bank, width], F32, name="down_bank", bufs=2)
                 for mm in range(per_bank):
                     for b in range(PASSES):
-                        down_pass(acc[:, mm, :], first + mm, q, b, cols)
+                        down_pass(acc[:, mm, :], first + mm, q, b, b == 0, b == PASSES - 1)
                 result = keep.tile([P, per_bank, width], F32, name=f"result{q}_{first}")
                 nc.scalar.copy(result[:], acc[:])
                 nc.sync.dma_start(out_rows[:, first : first + per_bank, tokens], result[:])
 
-        def last_product(q, cols):
-            tokens = slice(q * GROUP + cols.start, q * GROUP + cols.stop)
-            accs = [next_bank([P, CHUNK]) for m in range(N_TILES)]
-            for m in range(N_TILES):
-                down_pass(accs[m][:], m, q, 0, cols)
-            quantize_h(q, 1, cols)
-            for m in range(N_TILES):
-                down_pass(accs[m][:], m, q, 1, cols)
+        def last_down(q):
+            width = WIDTHS[q]
+            tokens = slice(STARTS[q], STARTS[q] + width)
+            accs = [psum.tile([P, 2, width], F32, name="down_bank", bufs=2) for half in range(2)]
+            for b in range(PASSES):
+                if b == PASSES - 1:
+                    quantize_h(q, b)
+                for m in range(N_TILES):
+                    down_pass(accs[m // 2][:, m % 2, :], m, q, b, b == 0 and m % 2 == 0, b == PASSES - 1 and m % 2 == 1)
             for half in range(2):
-                result = keep.tile([P, 2, CHUNK], F32, name=f"last_result{half}")
-                for mm in range(2):
-                    if half == 0:
-                        nc.vector.tensor_copy(result[:, mm, :], accs[mm][:])
-                    else:
-                        nc.scalar.copy(result[:, mm, :], accs[2 + mm][:])
+                result = keep.tile([P, 2, width], F32, name=f"last_result{half}")
+                if half == 0:
+                    nc.vector.tensor_copy(result[:], accs[half][:])
+                else:
+                    nc.scalar.copy(result[:], accs[half][:])
                 queue = nc.sync if half == 0 else nc.scalar
                 queue.dma_start(out_rows[:, 2 * half : 2 * half + 2, tokens], result[:])
 
-        whole = slice(0, GROUP)
-        chunks = [slice(0, CHUNK), slice(CHUNK, GROUP)]
         last = GROUPS - 1
+        finish_x(0)
+        order_words(0)
         quantize_x(0)
-        picked_late = keep.tile([P, PACK, GROUP], F32, name="x_bf0", align_bytes=64)
-        for i in range(PACK):
-            gather(picked_late[:, i, :], i, early_width, weight_late[:])
-        weave_wd(0, 0, "weight_late")
-        weave_wd(0, 1, "stage1")
-        weave_wd(1, 0, "stage2")
-        weave_wd(1, 1, "stage3")
+        order_words(1)
+        pending = []
         for q in range(GROUPS):
-            hidden(q, 0, 0)
-            if q > 0:
-                quantize_h(q - 1, 1, whole)
-            hidden(q, 0, 1)
-            if q == 1:
-                quantize_wd(0, 0)
-                quantize_wd(0, 1)
-            if q > 1:
-                second_product(q - 2, whole)
-            hidden(q, 1, 0)
-            quantize_h(q, 0, whole)
-            if q == 1:
-                weave_x(last, picked_late[:])
             if q < last:
-                quantize_x(q + 1)
-            if q == last:
-                quantize_h(last, 1, chunks[0])
-            hidden(q, 1, 1)
-            if q == 1:
-                quantize_wd(1, 0)
-                quantize_wd(1, 1)
-        second_product(last - 1, whole)
-        second_product(last, chunks[0])
-        last_product(last, chunks[1])
+                finish_x(q + 1)
+            for b in range(PASSES):
+                gate(q, b)
+                for c in range(WIDTHS[q] // CHUNK):
+                    up(q, b, c)
+                    if c == 0 and pending:
+                        quantize_h(*pending.pop())
+                pending.append((q, b))
+                if b == 0 and q < last:
+                    quantize_x(q + 1)
+                if q in (1, 2):
+                    weave_wd(q - 1, b)
+                    quantize_wd(q - 1, b)
+            if q >= 3:
+                down(2 * (q - 3))
+                down(2 * (q - 3) + 1)
+        last_down(last)

@@ -14,7 +14,6 @@ U8 = mybir.dt.uint8
 FP8X4 = mybir.dt.float8_e4m3fn_x4
 FP4X4 = mybir.dt.float4_e2m1fn_x4
 MULT = mybir.AluOpType.mult
-ADD = mybir.AluOpType.add
 GELU = mybir.ActivationFunctionType.Gelu_apprx_tanh
 
 P = 128
@@ -121,14 +120,12 @@ def tile_list_gelu_none_kernel(
         def weave_wd(b, half):
             wd_bf[b, half] = keep.tile([P, N // 2, PACK], BF16, name=f"wd_bf{b}_{half}", align_bytes=64)
             cols = slice(half * N // 2, (half + 1) * N // 2)
-            nc.gpsimd.tensor_scalar(
-                wd_bf[b, half][:],
-                wd_raw[b][:, :, cols].rearrange("p t n -> p n t"),
-                1.0,
-                0.0,
-                MULT,
-                ADD,
-            )
+            dst = wd_bf[b, half][:].rearrange("p (c e) t -> p c t e", e=4)
+            src = wd_raw[b][:, :, cols].rearrange("p t (c e) -> p c t e", e=4)
+            if half == 0:
+                nc.scalar.copy(dst, src)
+            else:
+                nc.vector.tensor_copy(dst, src)
 
         def quantize_wd(b, half):
             cols = slice(half * N // 2, (half + 1) * N // 2)

@@ -25,6 +25,10 @@ N_TILES = N // P
 WIDTHS = (128, 256, 256, 256, 128)
 STARTS = tuple(sum(WIDTHS[:q]) for q in range(len(WIDTHS)))
 GROUPS = len(WIDTHS)
+EARLY = 3
+HEAD = 256
+LATE_SLOT = {3: "x_bf1", 4: "act0_0"}
+WD_ON_VECTOR = ((0, 1), (1, 1))
 
 
 def tile_list_gelu_none_kernel(
@@ -38,48 +42,66 @@ def tile_list_gelu_none_kernel(
         offsets = keep.tile([P, J // 16], U16, name="offsets")
         nc.sync.dma_start(offsets[:], offs)
 
-        w_scales = keep.tile([P, 2 * R], U8, name="w_scales", align_bytes=64)
-        nc.vector.memset(w_scales[:].bitcast(I32), 0)
-        scales_raw = [keep.tile([P, R // 4], I32, name=f"scales_raw{g}") for g in range(2)]
-        for g, src in enumerate((wg_scales, wu_scales)):
-            for q in range(4):
-                rows = slice(32 * q, 32 * q + 4)
-                nc.scalar.dma_start(scales_raw[g][rows, :], src[0, 4 * q : 4 * q + 4, :].bitcast(I32))
-                nc.vector.tensor_copy(
-                    w_scales[rows, g * R : (g + 1) * R].bitcast(I32).rearrange("p (b t s) -> p b t s", t=PACK, s=32),
-                    scales_raw[g][rows, :].rearrange("p (b s t) -> p b t s", t=PACK, s=32),
-                )
-
         warm_in = keep.tile([P, 8], F32, name="warm_in")
         warm_out = keep.tile([P, 8], F32, name="warm_out")
         nc.vector.memset(warm_in[:], 0.0)
+
+        w_scales = [keep.tile([P, R], U8, name=f"w_scales{g}", align_bytes=64) for g in range(2)]
+        scales_raw = [keep.tile([P, R // 4], I32, name=f"scales_raw{g}") for g in range(2)]
+        nc.vector.memset(w_scales[0][:].bitcast(I32), 0)
+        nc.vector.memset(scales_raw[1][:], 0)
+
+        def order_scales(g, rows):
+            nc.vector.tensor_copy(
+                w_scales[g][rows, :].bitcast(I32).rearrange("p (b t s) -> p b t s", t=PACK, s=32),
+                scales_raw[g][rows, :].rearrange("p (b s t) -> p b t s", t=PACK, s=32),
+            )
+
+        def load_scales(queue, g, q):
+            rows = slice(32 * q, 32 * q + 4)
+            queue.dma_start(scales_raw[g][rows, :], (wg_scales, wu_scales)[g][0, 4 * q : 4 * q + 4, :].bitcast(I32))
+
+        for q in range(3):
+            load_scales(nc.scalar, 0, q)
+            order_scales(0, slice(32 * q, 32 * q + 4))
         nc.scalar.activation(warm_out[:], warm_in[:], GELU)
 
         x_planes = xT.rearrange("(p i) t -> i p t", i=PACK)
         planes = [keep.tile([P, T], F32, name=f"plane{i}") for i in range(PACK)]
         weight = keep.tile([P, J], F32, name="weight")
         nc.sync.dma_start(planes[0][:], x_planes[0])
-        nc.sync.dma_start(weight[:], wgt)
-        for i in range(1, PACK):
-            nc.sync.dma_start(planes[i][:], x_planes[i])
+        nc.sync.dma_start(weight[:, :HEAD], wgt[:, :HEAD])
+        nc.sync.dma_start(weight[:, HEAD:], wgt[:, HEAD:])
+        wd_rows = wd.rearrange("(b s t e) n -> b t s (e n)", b=PASSES, t=PACK, e=4)
+        wd_raw = [keep.tile([P, PACK, N], F32, name=f"wd_raw{b}") for b in range(PASSES)]
+
+        def load_wd(b):
+            for t in range(PACK):
+                nc.sync.dma_start(wd_raw[b][:, t, :], wd_rows[b, t])
+
+        nc.sync.dma_start(planes[1][:], x_planes[1])
+        load_scales(nc.sync, 0, 3)
+        load_scales(nc.sync, 1, 0)
+        nc.sync.dma_start(planes[2][:], x_planes[2])
+        for q in range(1, 4):
+            load_scales(nc.sync, 1, q)
+        nc.sync.dma_start(planes[3][:], x_planes[3])
 
         words_raw = [keep.tile([P, R // 2], I32, name=f"words_raw{g}") for g in range(2)]
         for g, src in enumerate((wg_words, wu_words)):
             nc.sync.dma_start(words_raw[g][:], src[0].bitcast(I32))
 
-        wd_rows = wd.rearrange("(b s t e) n -> b t s (e n)", b=PASSES, t=PACK, e=4)
-        wd_raw = [keep.tile([P, PACK, N], F32, name=f"wd_raw{b}") for b in range(PASSES)]
         for b in range(PASSES):
-            for t in range(PACK):
-                nc.sync.dma_start(wd_raw[b][:, t, :], wd_rows[b, t])
+            load_wd(b)
 
         def gather(dst, i, start, width):
             cols = offsets[:, start // 16 : (start + width) // 16]
             nc.vector.tensor_tensor(dst, planes[i][:].indirect(cols), weight[:, start : start + width], MULT)
 
         picked_low = keep.tile([P, 2, J], F32, name="picked_low")
-        picked_high = [keep.tile([P, 2, w], F32, name=f"picked_high{q}") for q, w in enumerate(WIDTHS)]
-        x_bf = [keep.tile([P, w, PACK], BF16, name=f"x_bf{q}", align_bytes=64) for q, w in enumerate(WIDTHS)]
+        picked_high = {q: keep.tile([P, 2 * WIDTHS[q]], F32, name=f"picked_high{q}", align_bytes=64) for q in range(EARLY)}
+        x_bf = [picked_high[2][:, WIDTHS[2] :].bitcast(BF16).rearrange("p (j i) -> p j i", i=PACK)]
+        x_bf.extend(keep.tile([P, WIDTHS[q], PACK], BF16, name=f"x_bf{q}", align_bytes=64)[:] for q in range(1, GROUPS))
         x_codes = [keep.tile([P, w], U32, name=f"x_codes{q}", align_bytes=64) for q, w in enumerate(WIDTHS)]
         x_scales = [keep.tile([P, w], U8, name=f"x_scales{q}", align_bytes=64) for q, w in enumerate(WIDTHS)]
 
@@ -89,20 +111,31 @@ def tile_list_gelu_none_kernel(
                 src.rearrange("p i (c e) -> p c i e", e=2),
             )
 
-        for i in range(2):
-            gather(picked_low[:, i, :], i, 0, J)
+        gather(picked_low[:, 0, :HEAD], 0, 0, HEAD)
+        gather(picked_low[:, 0, HEAD:], 0, HEAD, J - HEAD)
         for q in range(GROUPS):
-            weave_pair(q, 0, picked_low[:, :, STARTS[q] : STARTS[q] + WIDTHS[q]])
-        for q in range(GROUPS):
-            gather(picked_high[q][:, 0, :], 2, STARTS[q], WIDTHS[q])
+            cols = slice(STARTS[q], STARTS[q] + WIDTHS[q])
+            gather(picked_low[:, 1, cols], 1, STARTS[q], WIDTHS[q])
+            weave_pair(q, 0, picked_low[:, :, cols])
+        for q in range(EARLY):
+            gather(picked_high[q][:, : WIDTHS[q]], 2, STARTS[q], WIDTHS[q])
+
+        order_scales(0, slice(96, 100))
+        order_scales(1, slice(0, P))
 
         def finish_x(q):
-            gather(picked_high[q][:, 1, :], 3, STARTS[q], WIDTHS[q])
-            weave_pair(q, 2, picked_high[q][:])
+            width = WIDTHS[q]
+            if q >= EARLY:
+                picked_high[q] = keep.tile([P, 2 * width], F32, name=LATE_SLOT[q], align_bytes=64)
+                gather(picked_high[q][:, :width], 2, STARTS[q], width)
+            gather(picked_high[q][:, width:], 3, STARTS[q], width)
+
+        def weave_x(q):
+            weave_pair(q, 2, picked_high[q][:].rearrange("p (i j) -> p i j", i=2))
 
         def quantize_x(q):
             nc.vector.quantize_mx(
-                out=x_codes[q][:].bitcast(FP8X4), scales=x_scales[q][:], in_=x_bf[q][:].rearrange("p j i -> p (j i)")
+                out=x_codes[q][:].bitcast(FP8X4), scales=x_scales[q][:], in_=x_bf[q].rearrange("p j i -> p (j i)")
             )
 
         w_codes = [keep.tile([P, 2 * R], U8, name=f"w_codes{g}", align_bytes=64) for g in range(2)]
@@ -122,10 +155,10 @@ def tile_list_gelu_none_kernel(
             cols = slice(half * N // 2, (half + 1) * N // 2)
             dst = wd_bf[b, half][:].rearrange("p (c e) t -> p c t e", e=4)
             src = wd_raw[b][:, :, cols].rearrange("p t (c e) -> p c t e", e=4)
-            if half == 0:
-                nc.scalar.copy(dst, src)
-            else:
+            if (b, half) in WD_ON_VECTOR:
                 nc.vector.tensor_copy(dst, src)
+            else:
+                nc.scalar.copy(dst, src)
 
         def quantize_wd(b, half):
             cols = slice(half * N // 2, (half + 1) * N // 2)
@@ -140,7 +173,7 @@ def tile_list_gelu_none_kernel(
             nc.tensor.matmul_mx(
                 out=dst,
                 lhsT=w_codes[g][:, 2 * P * s : 2 * P * (s + 1)].bitcast(FP4X4),
-                lhsT_scale=w_scales[:, g * R + P * s : g * R + P * (s + 1)],
+                lhsT_scale=w_scales[g][:, P * s : P * (s + 1)],
                 rhs=x_codes[q][:, cols].bitcast(FP8X4),
                 rhs_scale=x_scales[q][:, cols],
                 start=True,
@@ -155,7 +188,7 @@ def tile_list_gelu_none_kernel(
         def gate(q, b):
             width = WIDTHS[q]
             per_bank = BANK // width
-            act[q, b] = keep.tile([P, PACK, width], F32, name=f"act{q}_{b}")
+            act[q, b] = keep.tile([P, PACK, width], F32, name=f"act{q}_{b}", align_bytes=64)
             h_bf[q, b] = keep.tile([P, width, PACK], BF16, name=f"h_bf{q}_{b}", align_bytes=64)
             h_codes[q, b] = keep.tile([P, width], U32, name=f"h_codes{q}_{b}", align_bytes=64)
             h_scales[q, b] = keep.tile([P, width], U8, name=f"h_scales{q}_{b}", align_bytes=64)
@@ -198,15 +231,15 @@ def tile_list_gelu_none_kernel(
                 stop=stop,
             )
 
-        def down(q):
+        def down(q, tag, bufs):
             width = WIDTHS[q]
             tokens = slice(STARTS[q], STARTS[q] + width)
             per_bank = BANK // width
             for first in range(0, N_TILES, per_bank):
-                acc = psum.tile([P, per_bank, width], F32, name="down_bank", bufs=2)
+                acc = psum.tile([P, per_bank, width], F32, name=tag, bufs=bufs)
                 for mm in range(per_bank):
-                    for b in range(PASSES):
-                        down_pass(acc[:, mm, :], first + mm, q, b, b == 0, b == PASSES - 1)
+                    for b in reversed(range(PASSES)):
+                        down_pass(acc[:, mm, :], first + mm, q, b, b == PASSES - 1, b == 0)
                 result = keep.tile([P, per_bank, width], F32, name=f"result{q}_{first}")
                 nc.scalar.copy(result[:], acc[:])
                 nc.sync.dma_start(out_rows[:, first : first + per_bank, tokens], result[:])
@@ -214,7 +247,7 @@ def tile_list_gelu_none_kernel(
         def last_down(q):
             width = WIDTHS[q]
             tokens = slice(STARTS[q], STARTS[q] + width)
-            accs = [psum.tile([P, 2, width], F32, name="down_bank", bufs=2) for half in range(2)]
+            accs = [psum.tile([P, 2, width], F32, name="up_bank", bufs=3) for half in range(2)]
             for b in range(PASSES):
                 if b == PASSES - 1:
                     quantize_h(q, b)
@@ -230,27 +263,44 @@ def tile_list_gelu_none_kernel(
                 queue.dma_start(out_rows[:, 2 * half : 2 * half + 2, tokens], result[:])
 
         last = GROUPS - 1
-        finish_x(0)
+        for q in range(2):
+            finish_x(q)
+            weave_x(q)
         order_words(0)
         quantize_x(0)
+        finish_x(2)
+        weave_x(2)
         order_words(1)
-        pending = []
-        for q in range(GROUPS):
-            if q < last:
-                finish_x(q + 1)
+        quantize_x(1)
+        gate(0, 0)
+        gate(0, 1)
+        finish_x(3)
+        up(0, 0, 0)
+        quantize_x(2)
+        up(0, 1, 0)
+        quantize_h(0, 0)
+        weave_x(3)
+        finish_x(4)
+        pending = [(0, 1)]
+        for q in range(1, GROUPS):
             for b in range(PASSES):
                 gate(q, b)
+                if q == 1:
+                    weave_wd(b, 0)
                 for c in range(WIDTHS[q] // CHUNK):
                     up(q, b, c)
-                    if c == 0 and pending:
+                    if c == 0:
                         quantize_h(*pending.pop())
                 pending.append((q, b))
-                if b == 0 and q < last:
-                    quantize_x(q + 1)
-                if q in (1, 2):
-                    weave_wd(q - 1, b)
-                    quantize_wd(q - 1, b)
-            if q >= 3:
-                down(2 * (q - 3))
-                down(2 * (q - 3) + 1)
+                if q == 1:
+                    quantize_x(3 + b)
+                    weave_wd(b, 1)
+                    if b == 0:
+                        weave_x(4)
+                if (q, b) in ((1, 1), (2, 0)):
+                    for half in range(2):
+                        quantize_wd(q - 1, half)
+        for q in range(last - 1):
+            down(q, "down_bank", 2)
+        down(last - 1, "gate_bank", 3)
         last_down(last)

@@ -25,9 +25,9 @@ N_TILES = N // P
 WIDTHS = (128, 256, 256, 256, 128)
 STARTS = tuple(sum(WIDTHS[:q]) for q in range(len(WIDTHS)))
 GROUPS = len(WIDTHS)
-EARLY = 3
+EARLY = 2
 HEAD = 256
-LATE_SLOT = {3: "x_bf1", 4: "act0_0"}
+LATE_SLOT = {2: "x_bf0", 3: "act1_0", 4: "act2_0"}
 WD_ON_VECTOR = ((0, 1), (1, 1))
 
 
@@ -66,6 +66,12 @@ def tile_list_gelu_none_kernel(
             order_scales(0, slice(32 * q, 32 * q + 4))
         nc.scalar.activation(warm_out[:], warm_in[:], GELU)
 
+        warm_zero = keep.tile([P, PACK * BANK], BF16, name="warm_zero", align_bytes=64)
+        warm_codes = keep.tile([P, BANK], U32, name="warm_codes", align_bytes=64)
+        warm_scales = keep.tile([P, BANK], U8, name="warm_scales", align_bytes=64)
+        nc.vector.memset(warm_zero[:], 0.0)
+        nc.vector.quantize_mx(out=warm_codes[:].bitcast(FP8X4), scales=warm_scales[:], in_=warm_zero[:])
+
         x_planes = xT.rearrange("(p i) t -> i p t", i=PACK)
         planes = [keep.tile([P, T], F32, name=f"plane{i}") for i in range(PACK)]
         weight = keep.tile([P, J], F32, name="weight")
@@ -87,7 +93,7 @@ def tile_list_gelu_none_kernel(
             load_scales(nc.sync, 1, q)
         nc.sync.dma_start(planes[3][:], x_planes[3])
 
-        words_raw = [keep.tile([P, R // 2], I32, name=f"words_raw{g}") for g in range(2)]
+        words_raw = [keep.tile([P, R // 2], I32, name=f"words_raw{g}", align_bytes=64) for g in range(2)]
         for g, src in enumerate((wg_words, wu_words)):
             nc.sync.dma_start(words_raw[g][:], src[0].bitcast(I32))
 
@@ -99,9 +105,8 @@ def tile_list_gelu_none_kernel(
             nc.vector.tensor_tensor(dst, planes[i][:].indirect(cols), weight[:, start : start + width], MULT)
 
         picked_low = keep.tile([P, 2, J], F32, name="picked_low")
-        picked_high = {q: keep.tile([P, 2 * WIDTHS[q]], F32, name=f"picked_high{q}", align_bytes=64) for q in range(EARLY)}
-        x_bf = [picked_high[2][:, WIDTHS[2] :].bitcast(BF16).rearrange("p (j i) -> p j i", i=PACK)]
-        x_bf.extend(keep.tile([P, WIDTHS[q], PACK], BF16, name=f"x_bf{q}", align_bytes=64)[:] for q in range(1, GROUPS))
+        picked_high = {q: keep.tile([P, 2 * WIDTHS[q]], F32, name=f"picked_high{q}", align_bytes=64) for q in range(2)}
+        x_bf = [keep.tile([P, w, PACK], BF16, name=f"x_bf{q}", align_bytes=64)[:] for q, w in enumerate(WIDTHS)]
         x_codes = [keep.tile([P, w], U32, name=f"x_codes{q}", align_bytes=64) for q, w in enumerate(WIDTHS)]
         x_scales = [keep.tile([P, w], U8, name=f"x_scales{q}", align_bytes=64) for q, w in enumerate(WIDTHS)]
 
@@ -128,10 +133,10 @@ def tile_list_gelu_none_kernel(
             if q >= EARLY:
                 picked_high[q] = keep.tile([P, 2 * width], F32, name=LATE_SLOT[q], align_bytes=64)
                 gather(picked_high[q][:, :width], 2, STARTS[q], width)
-            gather(picked_high[q][:, width:], 3, STARTS[q], width)
+            gather(picked_high[q][:, width : 2 * width], 3, STARTS[q], width)
 
         def weave_x(q):
-            weave_pair(q, 2, picked_high[q][:].rearrange("p (i j) -> p i j", i=2))
+            weave_pair(q, 2, picked_high[q][:, : 2 * WIDTHS[q]].rearrange("p (i j) -> p i j", i=2))
 
         def quantize_x(q):
             nc.vector.quantize_mx(
@@ -180,6 +185,24 @@ def tile_list_gelu_none_kernel(
                 stop=True,
             )
 
+        taken = []
+
+        def next_bank(shape):
+            taken.append(shape)
+            return psum.tile(shape, F32, name=f"bank{len(taken) % 8}")
+
+        warm_bank = next_bank([P, BANK])
+        for rep in range(3):
+            nc.tensor.matmul_mx(
+                out=warm_bank[:],
+                lhsT=words_raw[0][:, : P // 2].bitcast(FP4X4),
+                lhsT_scale=warm_scales[:, :P],
+                rhs=warm_codes[:].bitcast(FP8X4),
+                rhs_scale=warm_scales[:],
+                start=True,
+                stop=True,
+            )
+
         act = {}
         h_bf = {}
         h_codes = {}
@@ -193,14 +216,14 @@ def tile_list_gelu_none_kernel(
             h_codes[q, b] = keep.tile([P, width], U32, name=f"h_codes{q}_{b}", align_bytes=64)
             h_scales[q, b] = keep.tile([P, width], U8, name=f"h_scales{q}_{b}", align_bytes=64)
             for first in range(0, PACK, per_bank):
-                bank = psum.tile([P, per_bank, width], F32, name="gate_bank", bufs=3)
+                bank = next_bank([P, per_bank, width])
                 for t in range(per_bank):
                     first_product(bank[:, t, :], 0, b, first + t, q, slice(0, width))
                 nc.scalar.activation(act[q, b][:, first : first + per_bank, :], bank[:], GELU)
 
         def up(q, b, c):
             cols = slice(c * CHUNK, (c + 1) * CHUNK)
-            bank = psum.tile([P, PACK, CHUNK], F32, name="up_bank", bufs=3)
+            bank = next_bank([P, PACK, CHUNK])
             for t in range(PACK):
                 first_product(bank[:, t, :], 1, b, t, q, cols)
             nc.vector.tensor_tensor(
@@ -231,36 +254,35 @@ def tile_list_gelu_none_kernel(
                 stop=stop,
             )
 
-        def down(q, tag, bufs):
-            width = WIDTHS[q]
-            tokens = slice(STARTS[q], STARTS[q] + width)
-            per_bank = BANK // width
+        def store(q, first, count, acc, on_vector, queue):
+            tokens = slice(STARTS[q], STARTS[q] + WIDTHS[q])
+            result = keep.tile([P, count, WIDTHS[q]], F32, name=f"result{q}_{first}")
+            if on_vector:
+                nc.vector.tensor_copy(result[:], acc[:])
+            else:
+                nc.scalar.copy(result[:], acc[:])
+            queue.dma_start(out_rows[:, first : first + count, tokens], result[:])
+
+        def down(q):
+            per_bank = BANK // WIDTHS[q]
             for first in range(0, N_TILES, per_bank):
-                acc = psum.tile([P, per_bank, width], F32, name=tag, bufs=bufs)
+                acc = next_bank([P, per_bank, WIDTHS[q]])
                 for mm in range(per_bank):
                     for b in reversed(range(PASSES)):
                         down_pass(acc[:, mm, :], first + mm, q, b, b == PASSES - 1, b == 0)
-                result = keep.tile([P, per_bank, width], F32, name=f"result{q}_{first}")
-                nc.scalar.copy(result[:], acc[:])
-                nc.sync.dma_start(out_rows[:, first : first + per_bank, tokens], result[:])
+                store(q, first, per_bank, acc, False, nc.sync)
 
-        def last_down(q):
-            width = WIDTHS[q]
-            tokens = slice(STARTS[q], STARTS[q] + width)
-            accs = [psum.tile([P, 2, width], F32, name="up_bank", bufs=3) for half in range(2)]
-            for b in range(PASSES):
-                if b == PASSES - 1:
-                    quantize_h(q, b)
-                for m in range(N_TILES):
-                    down_pass(accs[m // 2][:, m % 2, :], m, q, b, b == 0 and m % 2 == 0, b == PASSES - 1 and m % 2 == 1)
-            for half in range(2):
-                result = keep.tile([P, 2, width], F32, name=f"last_result{half}")
-                if half == 0:
-                    nc.vector.tensor_copy(result[:], accs[half][:])
-                else:
-                    nc.scalar.copy(result[:], accs[half][:])
-                queue = nc.sync if half == 0 else nc.scalar
-                queue.dma_start(out_rows[:, 2 * half : 2 * half + 2, tokens], result[:])
+        accs = {}
+
+        def down_by_pass(q, b):
+            if b == 0:
+                accs[q] = [next_bank([P, 2, WIDTHS[q]]) for half in range(2)]
+            for m in range(N_TILES):
+                down_pass(accs[q][m // 2][:, m % 2, :], m, q, b, b == 0 and m % 2 == 0, b == PASSES - 1 and m % 2 == 1)
+
+        def ups(q, b):
+            for c in range(WIDTHS[q] // CHUNK):
+                up(q, b, c)
 
         last = GROUPS - 1
         for q in range(2):
@@ -268,39 +290,63 @@ def tile_list_gelu_none_kernel(
             weave_x(q)
         order_words(0)
         quantize_x(0)
-        finish_x(2)
-        weave_x(2)
         order_words(1)
         quantize_x(1)
+        finish_x(2)
         gate(0, 0)
         gate(0, 1)
-        finish_x(3)
-        up(0, 0, 0)
+        ups(0, 0)
+        ups(0, 1)
+        gate(1, 0)
+        weave_x(2)
+        weave_wd(0, 1)
         quantize_x(2)
-        up(0, 1, 0)
+        ups(1, 0)
+        weave_wd(0, 0)
+        gate(1, 1)
+        weave_wd(1, 1)
+        weave_wd(1, 0)
         quantize_h(0, 0)
+        quantize_h(0, 1)
+        quantize_wd(0, 1)
+        quantize_wd(0, 0)
+        ups(1, 1)
+        finish_x(3)
+        quantize_wd(1, 1)
+        quantize_wd(1, 0)
+        gate(2, 0)
         weave_x(3)
+        quantize_x(3)
+        ups(2, 0)
+        quantize_h(1, 0)
+        quantize_h(1, 1)
+        gate(2, 1)
+        ups(2, 1)
         finish_x(4)
-        pending = [(0, 1)]
-        for q in range(1, GROUPS):
-            for b in range(PASSES):
-                gate(q, b)
-                if q == 1:
-                    weave_wd(b, 0)
-                for c in range(WIDTHS[q] // CHUNK):
-                    up(q, b, c)
-                    if c == 0:
-                        quantize_h(*pending.pop())
-                pending.append((q, b))
-                if q == 1:
-                    quantize_x(3 + b)
-                    weave_wd(b, 1)
-                    if b == 0:
-                        weave_x(4)
-                if (q, b) in ((1, 1), (2, 0)):
-                    for half in range(2):
-                        quantize_wd(q - 1, half)
-        for q in range(last - 1):
-            down(q, "down_bank", 2)
-        down(last - 1, "gate_bank", 3)
-        last_down(last)
+        down(0)
+        down(1)
+        gate(3, 0)
+        quantize_h(2, 0)
+        weave_x(4)
+        ups(3, 0)
+        quantize_h(2, 1)
+        quantize_x(4)
+        gate(3, 1)
+        ups(3, 1)
+        down(2)
+        quantize_h(3, 0)
+        gate(4, 0)
+        gate(4, 1)
+        ups(4, 0)
+        quantize_h(3, 1)
+        ups(4, 1)
+        quantize_h(4, 0)
+        for b in range(PASSES):
+            down_by_pass(last - 1, b)
+        down_by_pass(last, 0)
+        quantize_h(last, 1)
+        down_by_pass(last, 1)
+        store(last - 1, 0, 2, accs[last - 1][0], False, nc.sync)
+        store(last - 1, 2, 2, accs[last - 1][1], False, nc.sync)
+        store(last, 0, 2, accs[last][0], True, nc.sync)
+        store(last, 2, 2, accs[last][1], False, nc.scalar)

@@ -69,7 +69,7 @@ def tile_list_gelu_none_kernel(
         warm_zero = keep.tile([P, PACK * BANK], BF16, name="warm_zero", align_bytes=64)
         warm_codes = keep.tile([P, BANK], U32, name="warm_codes", align_bytes=64)
         warm_scales = keep.tile([P, BANK], U8, name="warm_scales", align_bytes=64)
-        nc.vector.memset(warm_zero[:], 0.0)
+        nc.vector.memset(warm_zero[:].bitcast(I32), 0)
         nc.vector.quantize_mx(out=warm_codes[:].bitcast(FP8X4), scales=warm_scales[:], in_=warm_zero[:])
 
         x_planes = xT.rearrange("(p i) t -> i p t", i=PACK)
@@ -192,11 +192,11 @@ def tile_list_gelu_none_kernel(
             return psum.tile(shape, F32, name=f"bank{len(taken) % 8}")
 
         warm_bank = next_bank([P, BANK])
-        for rep in range(3):
+        for rep in range(4):
             nc.tensor.matmul_mx(
                 out=warm_bank[:],
-                lhsT=words_raw[0][:, : P // 2].bitcast(FP4X4),
-                lhsT_scale=warm_scales[:, :P],
+                lhsT=warm_codes[:, :P].bitcast(FP8X4),
+                lhsT_scale=w_scales[0][:, :P],
                 rhs=warm_codes[:].bitcast(FP8X4),
                 rhs_scale=warm_scales[:],
                 start=True,

@@ -66,12 +66,6 @@ def tile_list_gelu_none_kernel(
             order_scales(0, slice(32 * q, 32 * q + 4))
         nc.scalar.activation(warm_out[:], warm_in[:], GELU)
 
-        warm_zero = keep.tile([P, PACK * BANK], BF16, name="warm_zero", align_bytes=64)
-        warm_codes = keep.tile([P, BANK], U32, name="warm_codes", align_bytes=64)
-        warm_scales = keep.tile([P, BANK], U8, name="warm_scales", align_bytes=64)
-        nc.vector.memset(warm_zero[:].bitcast(I32), 0)
-        nc.vector.quantize_mx(out=warm_codes[:].bitcast(FP8X4), scales=warm_scales[:], in_=warm_zero[:])
-
         x_planes = xT.rearrange("(p i) t -> i p t", i=PACK)
         planes = [keep.tile([P, T], F32, name=f"plane{i}") for i in range(PACK)]
         weight = keep.tile([P, J], F32, name="weight")
@@ -190,18 +184,6 @@ def tile_list_gelu_none_kernel(
         def next_bank(shape):
             taken.append(shape)
             return psum.tile(shape, F32, name=f"bank{len(taken) % 8}")
-
-        warm_bank = next_bank([P, BANK])
-        for rep in range(4):
-            nc.tensor.matmul_mx(
-                out=warm_bank[:],
-                lhsT=warm_codes[:, :P].bitcast(FP8X4),
-                lhsT_scale=w_scales[0][:, :P],
-                rhs=warm_codes[:].bitcast(FP8X4),
-                rhs_scale=warm_scales[:],
-                start=True,
-                stop=True,
-            )
 
         act = {}
         h_bf = {}

@@ -25,9 +25,9 @@ N_TILES = N // P
 WIDTHS = (128, 256, 256, 256, 128)
 STARTS = tuple(sum(WIDTHS[:q]) for q in range(len(WIDTHS)))
 GROUPS = len(WIDTHS)
-EARLY = 2
+EARLY = 3
 HEAD = 256
-LATE_SLOT = {2: "x_bf0", 3: "act1_0", 4: "act2_0"}
+LATE_SLOT = {3: "act1_0", 4: "x_bf0"}
 WD_ON_VECTOR = ((0, 1), (1, 1))
 
 
@@ -48,22 +48,17 @@ def tile_list_gelu_none_kernel(
 
         w_scales = [keep.tile([P, R], U8, name=f"w_scales{g}", align_bytes=64) for g in range(2)]
         scales_raw = [keep.tile([P, R // 4], I32, name=f"scales_raw{g}") for g in range(2)]
-        nc.vector.memset(w_scales[0][:].bitcast(I32), 0)
-        nc.vector.memset(scales_raw[1][:], 0)
-
-        def order_scales(g, rows):
+        for g, src in enumerate((wg_scales, wu_scales)):
+            nc.vector.memset(w_scales[g][:].bitcast(I32), 0)
+            nc.scalar.dma_start(scales_raw[g][:16, :], src[0].bitcast(I32))
             nc.vector.tensor_copy(
-                w_scales[g][rows, :].bitcast(I32).rearrange("p (b t s) -> p b t s", t=PACK, s=32),
-                scales_raw[g][rows, :].rearrange("p (b s t) -> p b t s", t=PACK, s=32),
+                w_scales[g][:16, :].bitcast(I32).rearrange("p (b t s) -> p b t s", t=PACK, s=32),
+                scales_raw[g][:16, :].rearrange("p (b s t) -> p b t s", t=PACK, s=32),
             )
-
-        def load_scales(queue, g, q):
-            rows = slice(32 * q, 32 * q + 4)
-            queue.dma_start(scales_raw[g][rows, :], (wg_scales, wu_scales)[g][0, 4 * q : 4 * q + 4, :].bitcast(I32))
-
-        for q in range(3):
-            load_scales(nc.scalar, 0, q)
-            order_scales(0, slice(32 * q, 32 * q + 4))
+            for q in range(1, 4):
+                nc.scalar.dma_start(
+                    w_scales[g][32 * q : 32 * q + 4, :].bitcast(I32), w_scales[g][4 * q : 4 * q + 4, :].bitcast(I32)
+                )
         nc.scalar.activation(warm_out[:], warm_in[:], GELU)
 
         x_planes = xT.rearrange("(p i) t -> i p t", i=PACK)
@@ -79,13 +74,8 @@ def tile_list_gelu_none_kernel(
             for t in range(PACK):
                 nc.sync.dma_start(wd_raw[b][:, t, :], wd_rows[b, t])
 
-        nc.sync.dma_start(planes[1][:], x_planes[1])
-        load_scales(nc.sync, 0, 3)
-        load_scales(nc.sync, 1, 0)
-        nc.sync.dma_start(planes[2][:], x_planes[2])
-        for q in range(1, 4):
-            load_scales(nc.sync, 1, q)
-        nc.sync.dma_start(planes[3][:], x_planes[3])
+        for i in range(1, PACK):
+            nc.sync.dma_start(planes[i][:], x_planes[i])
 
         words_raw = [keep.tile([P, R // 2], I32, name=f"words_raw{g}", align_bytes=64) for g in range(2)]
         for g, src in enumerate((wg_words, wu_words)):
@@ -100,7 +90,9 @@ def tile_list_gelu_none_kernel(
 
         picked_low = keep.tile([P, 2, J], F32, name="picked_low")
         picked_high = {q: keep.tile([P, 2 * WIDTHS[q]], F32, name=f"picked_high{q}", align_bytes=64) for q in range(2)}
-        x_bf = [keep.tile([P, w, PACK], BF16, name=f"x_bf{q}", align_bytes=64)[:] for q, w in enumerate(WIDTHS)]
+        picked_high[2] = keep.tile([P, WIDTHS[2] + 2 * WIDTHS[1]], F32, name="picked_high2", align_bytes=64)
+        x_bf = {q: keep.tile([P, WIDTHS[q], PACK], BF16, name=f"x_bf{q}", align_bytes=64)[:] for q in (0, 2, 3, 4)}
+        x_bf[1] = picked_high[2][:, WIDTHS[2] :].bitcast(BF16).rearrange("p (j i) -> p j i", i=PACK)
         x_codes = [keep.tile([P, w], U32, name=f"x_codes{q}", align_bytes=64) for q, w in enumerate(WIDTHS)]
         x_scales = [keep.tile([P, w], U8, name=f"x_scales{q}", align_bytes=64) for q, w in enumerate(WIDTHS)]
 
@@ -118,9 +110,6 @@ def tile_list_gelu_none_kernel(
             weave_pair(q, 0, picked_low[:, :, cols])
         for q in range(EARLY):
             gather(picked_high[q][:, : WIDTHS[q]], 2, STARTS[q], WIDTHS[q])
-
-        order_scales(0, slice(96, 100))
-        order_scales(1, slice(0, P))
 
         def finish_x(q):
             width = WIDTHS[q]
@@ -275,6 +264,7 @@ def tile_list_gelu_none_kernel(
         order_words(1)
         quantize_x(1)
         finish_x(2)
+        finish_x(4)
         gate(0, 0)
         gate(0, 1)
         ups(0, 0)
@@ -304,7 +294,6 @@ def tile_list_gelu_none_kernel(
         quantize_h(1, 1)
         gate(2, 1)
         ups(2, 1)
-        finish_x(4)
         down(0)
         down(1)
         gate(3, 0)

@@ -14,6 +14,7 @@ U8 = mybir.dt.uint8
 FP8X4 = mybir.dt.float8_e4m3fn_x4
 FP4X4 = mybir.dt.float4_e2m1fn_x4
 MULT = mybir.AluOpType.mult
+ADD = mybir.AluOpType.add
 GELU = mybir.ActivationFunctionType.Gelu_apprx_tanh
 
 P = 128
@@ -25,10 +26,8 @@ N_TILES = N // P
 WIDTHS = (128, 256, 256, 256, 128)
 STARTS = tuple(sum(WIDTHS[:q]) for q in range(len(WIDTHS)))
 GROUPS = len(WIDTHS)
-EARLY = 3
-HEAD = 256
-LATE_SLOT = {3: "act1_0", 4: "x_bf0"}
-WD_ON_VECTOR = ((0, 1), (1, 1))
+SPREAD = (1, 1, 2, 2, 2)
+GATE_BANKS, UP_BANKS, DOWN_BANKS = 3, 3, 2
 
 
 def tile_list_gelu_none_kernel(
@@ -37,123 +36,159 @@ def tile_list_gelu_none_kernel(
     nc = tc.nc
     with ExitStack() as ctx:
         keep = ctx.enter_context(tc.tile_pool(name="keep", bufs=1))
+        laid = ctx.enter_context(tc.tile_pool(name="laid", bufs=1))
         psum = ctx.enter_context(tc.psum_pool(name="psum", bufs=1))
 
+        places = {"act1_1": 2048, "wd_bf1_2": 64, "x_codes3": 2112, "h_codes0": 3136, "wd_codes0": 4160, "act2_0": 8192, "x_codes4": 8192}
         offsets = keep.tile([P, J // 16], U16, name="offsets")
         nc.sync.dma_start(offsets[:], offs)
 
+        scales_raw = [keep.tile([P, R // 4], I32, name=f"scales_raw{g}") for g in range(2)]
+        for g in range(2):
+            nc.vector.memset(scales_raw[g][:], 0)
         warm_in = keep.tile([P, 8], F32, name="warm_in")
         warm_out = keep.tile([P, 8], F32, name="warm_out")
         nc.vector.memset(warm_in[:], 0.0)
-
-        w_scales = [keep.tile([P, R], U8, name=f"w_scales{g}", align_bytes=64) for g in range(2)]
-        scales_raw = [keep.tile([P, R // 4], I32, name=f"scales_raw{g}") for g in range(2)]
-        for g, src in enumerate((wg_scales, wu_scales)):
-            nc.vector.memset(w_scales[g][:].bitcast(I32), 0)
-            nc.scalar.dma_start(scales_raw[g][:16, :], src[0].bitcast(I32))
-            nc.vector.tensor_copy(
-                w_scales[g][:16, :].bitcast(I32).rearrange("p (b t s) -> p b t s", t=PACK, s=32),
-                scales_raw[g][:16, :].rearrange("p (b s t) -> p b t s", t=PACK, s=32),
-            )
-            for q in range(1, 4):
-                nc.scalar.dma_start(
-                    w_scales[g][32 * q : 32 * q + 4, :].bitcast(I32), w_scales[g][4 * q : 4 * q + 4, :].bitcast(I32)
-                )
         nc.scalar.activation(warm_out[:], warm_in[:], GELU)
 
+
         x_planes = xT.rearrange("(p i) t -> i p t", i=PACK)
-        planes = [keep.tile([P, T], F32, name=f"plane{i}") for i in range(PACK)]
-        weight = keep.tile([P, J], F32, name="weight")
-        nc.sync.dma_start(planes[0][:], x_planes[0])
-        nc.sync.dma_start(weight[:, :HEAD], wgt[:, :HEAD])
-        nc.sync.dma_start(weight[:, HEAD:], wgt[:, HEAD:])
+        planes = [keep.tile([P, T], F32, name=f"plane{i}", align_bytes=64) for i in range(PACK)]
+        words_raw = [keep.tile([P, R // 2], I32, name=f"words_raw{g}", align_bytes=64) for g in range(2)]
         wd_rows = wd.rearrange("(b s t e) n -> b t s (e n)", b=PASSES, t=PACK, e=4)
         wd_raw = [keep.tile([P, PACK, N], F32, name=f"wd_raw{b}") for b in range(PASSES)]
 
-        def load_wd(b):
+        def load_scales(g, src):
+            rows = src[0].bitcast(I32).rearrange("(q r) n -> r q n", r=4)
+            for r in range(4):
+                nc.sync.dma_start(scales_raw[g][r:P:32, :], rows[r])
+
+        weight = keep.tile([P, J], F32, name="weight", align_bytes=64)
+        nc.sync.dma_start(planes[0][:], x_planes[0])
+        nc.sync.dma_start(weight[:, :256], wgt[:, :256])
+        nc.sync.dma_start(weight[:, 256:], wgt[:, 256:])
+        load_scales(0, wg_scales)
+        for i in range(1, PACK):
+            nc.sync.dma_start(planes[i][:], x_planes[i])
+        nc.sync.dma_start(words_raw[0][:], wg_words[0].bitcast(I32))
+        load_scales(1, wu_scales)
+        nc.sync.dma_start(words_raw[1][:], wu_words[0].bitcast(I32))
+        for b in range(PASSES):
             for t in range(PACK):
                 nc.sync.dma_start(wd_raw[b][:, t, :], wd_rows[b, t])
 
-        for i in range(1, PACK):
-            nc.sync.dma_start(planes[i][:], x_planes[i])
+        w_scales = [keep.tile([P, R], U8, name=f"w_scales{g}", align_bytes=64) for g in range(2)]
+        roles = {"gate": (0, GATE_BANKS), "up": (GATE_BANKS, UP_BANKS), "down": (GATE_BANKS + UP_BANKS, DOWN_BANKS), "all": (0, 8)}
+        taken = {role: [] for role in roles}
 
-        words_raw = [keep.tile([P, R // 2], I32, name=f"words_raw{g}", align_bytes=64) for g in range(2)]
-        for g, src in enumerate((wg_words, wu_words)):
-            nc.sync.dma_start(words_raw[g][:], src[0].bitcast(I32))
+        def next_bank(role, shape):
+            role = "all"
+            first, count = roles[role]
+            taken[role].append(shape)
+            return psum.tile(shape, F32, name=f"bank{first + len(taken[role]) % count}")
 
-        for b in range(PASSES):
-            load_wd(b)
+        w_codes = [keep.tile([P, 2 * R], U8, name=f"w_codes{g}", align_bytes=64) for g in range(2)]
+
+        def order_scales(g, on_vector):
+            dst = w_scales[g][:].bitcast(U32).rearrange("p (b t s) -> p b t s", t=PACK, s=32)
+            src = scales_raw[g][:].bitcast(U32).rearrange("p (b s t) -> p b t s", t=PACK, s=32)
+            if on_vector:
+                nc.vector.tensor_copy(dst.bitcast(I32), src.bitcast(I32))
+            else:
+                nc.scalar.copy(dst, src)
+
+        def order_words(g, on_vector=True):
+            dst = w_codes[g][:].bitcast(U32).rearrange("p (b t s w) -> p b t s w", t=PACK, s=32, w=2)
+            src = words_raw[g][:].bitcast(U32).rearrange("p (b s t w) -> p b t s w", t=PACK, s=32, w=2)
+            if on_vector:
+                nc.vector.tensor_copy(dst.bitcast(I32), src.bitcast(I32))
+            else:
+                nc.scalar.copy(dst, src)
 
         def gather(dst, i, start, width):
             cols = offsets[:, start // 16 : (start + width) // 16]
             nc.vector.tensor_tensor(dst, planes[i][:].indirect(cols), weight[:, start : start + width], MULT)
 
         picked_low = keep.tile([P, 2, J], F32, name="picked_low")
-        picked_high = {q: keep.tile([P, 2 * WIDTHS[q]], F32, name=f"picked_high{q}", align_bytes=64) for q in range(2)}
-        picked_high[2] = keep.tile([P, WIDTHS[2] + 2 * WIDTHS[1]], F32, name="picked_high2", align_bytes=64)
-        x_bf = {q: keep.tile([P, WIDTHS[q], PACK], BF16, name=f"x_bf{q}", align_bytes=64)[:] for q in (0, 2, 3, 4)}
-        x_bf[1] = picked_high[2][:, WIDTHS[2] :].bitcast(BF16).rearrange("p (j i) -> p j i", i=PACK)
-        x_codes = [keep.tile([P, w], U32, name=f"x_codes{q}", align_bytes=64) for q, w in enumerate(WIDTHS)]
+        def place(name, shape, dtype):
+            if name in places:
+                return laid.tile(shape, dtype, name=name, align_bytes=64, offset=places[name])
+            return keep.tile(shape, dtype, name=name, align_bytes=64)
+
+        def room(name, words):
+            return place(name, [P, words], F32)
+
+        def woven(tile, first, width):
+            return tile[:, first : first + 2 * width].bitcast(BF16).rearrange("p (j i) -> p j i", i=PACK)
+
+        picked = {}
+        h_all = {}
+        x_bf = {}
+        picked[0] = room("picked0", 256)
+        picked[1] = room("picked1", 512)
+        picked[2] = room("picked2", 512)
+        x_bf[0] = woven(picked[2], 256, 128)
+        x_bf[1] = woven(room("x_bf1", 512), 0, 256)
+        x_bf[2] = woven(room("x_bf2", 512), 0, 256)
+        x_bf[3] = woven(room("x_bf3", 512), 0, 256)
+        x_bf[4] = woven(room("x_bf4", 256), 0, 128)
+
+        x_codes = [place(f"x_codes{q}", [P, w], U32) for q, w in enumerate(WIDTHS)]
         x_scales = [keep.tile([P, w], U8, name=f"x_scales{q}", align_bytes=64) for q, w in enumerate(WIDTHS)]
 
-        def weave_pair(q, first, src):
-            nc.scalar.copy(
-                x_bf[q][:, :, first : first + 2].rearrange("p (c e) i -> p c i e", e=2),
-                src.rearrange("p i (c e) -> p c i e", e=2),
-            )
+        def weave_pair(q, first, src, engine):
+            dst = x_bf[q][:, :, first : first + 2].rearrange("p (c e) i -> p c i e", e=2)
+            src = src.rearrange("p i (c e) -> p c i e", e=2)
+            if engine == "vector":
+                nc.vector.tensor_copy(dst, src)
+            elif engine == "scalar":
+                nc.scalar.copy(dst, src)
+            else:
+                nc.gpsimd.tensor_scalar(dst, src, 1.0, 0.0, MULT, ADD)
 
-        gather(picked_low[:, 0, :HEAD], 0, 0, HEAD)
-        gather(picked_low[:, 0, HEAD:], 0, HEAD, J - HEAD)
-        for q in range(GROUPS):
-            cols = slice(STARTS[q], STARTS[q] + WIDTHS[q])
-            gather(picked_low[:, 1, cols], 1, STARTS[q], WIDTHS[q])
-            weave_pair(q, 0, picked_low[:, :, cols])
-        for q in range(EARLY):
-            gather(picked_high[q][:, : WIDTHS[q]], 2, STARTS[q], WIDTHS[q])
+        def gather2(q, slot=None):
+            if slot:
+                picked[q] = room(slot, 2 * WIDTHS[q])
+            gather(picked[q][:, : WIDTHS[q]], 2, STARTS[q], WIDTHS[q])
 
-        def finish_x(q):
-            width = WIDTHS[q]
-            if q >= EARLY:
-                picked_high[q] = keep.tile([P, 2 * width], F32, name=LATE_SLOT[q], align_bytes=64)
-                gather(picked_high[q][:, :width], 2, STARTS[q], width)
-            gather(picked_high[q][:, width : 2 * width], 3, STARTS[q], width)
+        def gather3(q):
+            gather(picked[q][:, WIDTHS[q] : 2 * WIDTHS[q]], 3, STARTS[q], WIDTHS[q])
 
-        def weave_x(q):
-            weave_pair(q, 2, picked_high[q][:, : 2 * WIDTHS[q]].rearrange("p (i j) -> p i j", i=2))
+        def weave_x(q, engine="scalar"):
+            weave_pair(q, 2, picked[q][:, : 2 * WIDTHS[q]].rearrange("p (i j) -> p i j", i=2), engine)
 
         def quantize_x(q):
             nc.vector.quantize_mx(
                 out=x_codes[q][:].bitcast(FP8X4), scales=x_scales[q][:], in_=x_bf[q].rearrange("p j i -> p (j i)")
             )
 
-        w_codes = [keep.tile([P, 2 * R], U8, name=f"w_codes{g}", align_bytes=64) for g in range(2)]
-
-        def order_words(g):
-            nc.vector.tensor_copy(
-                w_codes[g][:].bitcast(I32).rearrange("p (b t s w) -> p b t s w", t=PACK, s=32, w=2),
-                words_raw[g][:].rearrange("p (b s t w) -> p b t s w", t=PACK, s=32, w=2),
-            )
-
         wd_bf = {}
-        wd_codes = [keep.tile([P, N], U32, name=f"wd_codes{b}", align_bytes=64) for b in range(PASSES)]
+        wd_codes = [place(f"wd_codes{b}", [P, N], U32) for b in range(PASSES)]
         wd_scales = [keep.tile([P, N], U8, name=f"wd_scales{b}", align_bytes=64) for b in range(PASSES)]
 
-        def weave_wd(b, half):
-            wd_bf[b, half] = keep.tile([P, N // 2, PACK], BF16, name=f"wd_bf{b}_{half}", align_bytes=64)
-            cols = slice(half * N // 2, (half + 1) * N // 2)
-            dst = wd_bf[b, half][:].rearrange("p (c e) t -> p c t e", e=4)
+        def weave_wd(b, first, count, engine, dst=None):
+            if dst is None:
+                dst = woven(room(f"wd_bf{b}_{first}", 2 * count * P), 0, count * P)
+            wd_bf[b, first] = dst
+            cols = slice(first * P, (first + count) * P)
+            if engine == "gpsimd":
+                nc.gpsimd.tensor_scalar(dst, wd_raw[b][:, :, cols].rearrange("p t n -> p n t"), 1.0, 0.0, MULT, ADD)
+                return
+            dst = dst.rearrange("p (c e) t -> p c t e", e=4)
             src = wd_raw[b][:, :, cols].rearrange("p t (c e) -> p c t e", e=4)
-            if (b, half) in WD_ON_VECTOR:
+            if engine == "vector":
                 nc.vector.tensor_copy(dst, src)
             else:
                 nc.scalar.copy(dst, src)
 
-        def quantize_wd(b, half):
-            cols = slice(half * N // 2, (half + 1) * N // 2)
+        def quantize_wd(b, first, whole=None):
+            if whole is not None:
+                wd_bf[b, first] = whole
+            cols = slice(first * P, first * P + wd_bf[b, first].shape[1])
             nc.vector.quantize_mx(
                 out=wd_codes[b][:, cols].bitcast(FP8X4),
                 scales=wd_scales[b][:, cols],
-                in_=wd_bf[b, half][:].rearrange("p n t -> p (n t)"),
+                in_=wd_bf[b, first].rearrange("p n t -> p (n t)"),
             )
 
         def first_product(dst, g, b, t, q, cols):
@@ -168,13 +203,9 @@ def tile_list_gelu_none_kernel(
                 stop=True,
             )
 
-        taken = []
-
-        def next_bank(shape):
-            taken.append(shape)
-            return psum.tile(shape, F32, name=f"bank{len(taken) % 8}")
-
         act = {}
+        codes_all = {}
+        scales_all = {}
         h_bf = {}
         h_codes = {}
         h_scales = {}
@@ -182,19 +213,26 @@ def tile_list_gelu_none_kernel(
         def gate(q, b):
             width = WIDTHS[q]
             per_bank = BANK // width
-            act[q, b] = keep.tile([P, PACK, width], F32, name=f"act{q}_{b}", align_bytes=64)
-            h_bf[q, b] = keep.tile([P, width, PACK], BF16, name=f"h_bf{q}_{b}", align_bytes=64)
-            h_codes[q, b] = keep.tile([P, width], U32, name=f"h_codes{q}_{b}", align_bytes=64)
-            h_scales[q, b] = keep.tile([P, width], U8, name=f"h_scales{q}_{b}", align_bytes=64)
+            act[q, b] = place(f"act{q}_{b}", [P, PACK, width], F32)
             for first in range(0, PACK, per_bank):
-                bank = next_bank([P, per_bank, width])
+                bank = next_bank("gate", [P, per_bank, width])
                 for t in range(per_bank):
                     first_product(bank[:, t, :], 0, b, first + t, q, slice(0, width))
                 nc.scalar.activation(act[q, b][:, first : first + per_bank, :], bank[:], GELU)
 
-        def up(q, b, c):
+        def up(q, b, c, slot=None):
+            if (b, c) == (0, 0):
+                width = WIDTHS[q]
+                if q not in h_all:
+                    h_all[q] = room(f"h_bf{q}", PASSES * 2 * width)[:]
+                codes_all[q] = place(slot or f"h_codes{q}", [P, PASSES * width], U32)
+                scales_all[q] = keep.tile([P, PASSES * width], U8, name=f"h_scales{q}", align_bytes=64)
+                for a in range(PASSES):
+                    h_bf[q, a] = woven(h_all[q], a * 2 * width, width)
+                    h_codes[q, a] = codes_all[q][:, a * width : (a + 1) * width]
+                    h_scales[q, a] = scales_all[q][:, a * width : (a + 1) * width]
             cols = slice(c * CHUNK, (c + 1) * CHUNK)
-            bank = next_bank([P, PACK, CHUNK])
+            bank = next_bank("up", [P, PACK, CHUNK])
             for t in range(PACK):
                 first_product(bank[:, t, :], 1, b, t, q, cols)
             nc.vector.tensor_tensor(
@@ -204,120 +242,149 @@ def tile_list_gelu_none_kernel(
                 MULT,
             )
 
-        def quantize_h(q, b):
+        def ups(q, b, slot=None):
+            for c in range(WIDTHS[q] // CHUNK):
+                up(q, b, c, slot)
+
+        def quantize_both(q):
             nc.vector.quantize_mx(
-                out=h_codes[q, b][:].bitcast(FP8X4),
-                scales=h_scales[q, b][:],
-                in_=h_bf[q, b][:].rearrange("p j t -> p (j t)"),
+                out=codes_all[q][:].bitcast(FP8X4), scales=scales_all[q][:], in_=h_all[q].bitcast(BF16)
+            )
+
+        def span(q, c):
+            return slice(0, WIDTHS[q]) if c is None else slice(c * CHUNK, (c + 1) * CHUNK)
+
+        def quantize_h(q, b, c=None):
+            cols = span(q, c)
+            nc.vector.quantize_mx(
+                out=h_codes[q, b][:, cols].bitcast(FP8X4),
+                scales=h_scales[q, b][:, cols],
+                in_=h_bf[q, b][:, cols, :].rearrange("p j t -> p (j t)"),
             )
 
         out_rows = out.rearrange("(m p) j -> p m j", p=P)
 
-        def down_pass(acc, m, q, b, start, stop):
+        def down_pass(acc, m, q, b, cols, start, stop):
             n_cols = slice(m * P, (m + 1) * P)
             nc.tensor.matmul_mx(
                 out=acc,
                 lhsT=wd_codes[b][:, n_cols].bitcast(FP8X4),
                 lhsT_scale=wd_scales[b][:, n_cols],
-                rhs=h_codes[q, b][:].bitcast(FP8X4),
-                rhs_scale=h_scales[q, b][:],
+                rhs=h_codes[q, b][:, cols].bitcast(FP8X4),
+                rhs_scale=h_scales[q, b][:, cols],
                 start=start,
                 stop=stop,
             )
 
-        def store(q, first, count, acc, on_vector, queue):
-            tokens = slice(STARTS[q], STARTS[q] + WIDTHS[q])
-            result = keep.tile([P, count, WIDTHS[q]], F32, name=f"result{q}_{first}")
+        def store(q, cols, first, count, acc, on_vector, queue):
+            tokens = slice(STARTS[q] + cols.start, STARTS[q] + cols.stop)
+            result = keep.tile([P, count, cols.stop - cols.start], F32, name=f"result{tokens.start}_{first}")
             if on_vector:
                 nc.vector.tensor_copy(result[:], acc[:])
             else:
                 nc.scalar.copy(result[:], acc[:])
             queue.dma_start(out_rows[:, first : first + count, tokens], result[:])
 
-        def down(q):
-            per_bank = BANK // WIDTHS[q]
-            for first in range(0, N_TILES, per_bank):
-                acc = next_bank([P, per_bank, WIDTHS[q]])
+        def down(q, c=None, part=None, role="down", on_vector=False):
+            cols = span(q, c)
+            width = cols.stop - cols.start
+            per_bank = BANK // width
+            firsts = list(range(0, N_TILES, per_bank))
+            for first in firsts if part is None else firsts[part : part + 1]:
+                acc = next_bank(role, [P, per_bank, width])
                 for mm in range(per_bank):
-                    for b in reversed(range(PASSES)):
-                        down_pass(acc[:, mm, :], first + mm, q, b, b == PASSES - 1, b == 0)
-                store(q, first, per_bank, acc, False, nc.sync)
+                    for b in range(PASSES):
+                        down_pass(acc[:, mm, :], first + mm, q, b, cols, b == 0, b == PASSES - 1)
+                store(q, cols, first, per_bank, acc, on_vector, nc.sync)
 
         accs = {}
 
-        def down_by_pass(q, b):
+        def down_by_pass(q, b, role):
             if b == 0:
-                accs[q] = [next_bank([P, 2, WIDTHS[q]]) for half in range(2)]
+                accs[q] = [next_bank(role, [P, 2, WIDTHS[q]]) for half in range(2)]
             for m in range(N_TILES):
-                down_pass(accs[q][m // 2][:, m % 2, :], m, q, b, b == 0 and m % 2 == 0, b == PASSES - 1 and m % 2 == 1)
-
-        def ups(q, b):
-            for c in range(WIDTHS[q] // CHUNK):
-                up(q, b, c)
+                acc = accs[q][m // 2][:, m % 2, :]
+                down_pass(acc, m, q, b, span(q, None), b == 0 and m % 2 == 0, b == PASSES - 1 and m % 2 == 1)
 
         last = GROUPS - 1
-        for q in range(2):
-            finish_x(q)
-            weave_x(q)
+        gather(picked_low[:, 0, :256], 0, 0, 256)
+        gather(picked_low[:, 0, 256:], 0, 256, 768)
+        order_scales(0, False)
+        for q in range(GROUPS):
+            cols = slice(STARTS[q], STARTS[q] + WIDTHS[q])
+            gather(picked_low[:, 1, cols], 1, STARTS[q], WIDTHS[q])
+            weave_pair(q, 0, picked_low[:, :, cols], "scalar")
+        for q in range(3):
+            gather2(q)
+        gather3(0)
+        weave_x(0)
+        gather3(1)
+        weave_x(1)
         order_words(0)
         quantize_x(0)
+        order_scales(1, False)
         order_words(1)
+        gather3(2)
         quantize_x(1)
-        finish_x(2)
-        finish_x(4)
         gate(0, 0)
+        weave_x(2)
         gate(0, 1)
+        gather2(3, "x_bf1")
+        gather3(3)
+        quantize_x(2)
+        gate(1, 0)
+        weave_x(3)
+        gather2(4, "x_bf2")
+        gather3(4)
+        wd_room = room("plane3", 2048)
+        weave_wd(0, 0, 4, "gpsimd", woven(wd_room, 0, 512))
+        h_all[0] = room("weight", 512)[:]
         ups(0, 0)
         ups(0, 1)
-        gate(1, 0)
-        weave_x(2)
-        weave_wd(0, 1)
-        quantize_x(2)
-        ups(1, 0)
-        weave_wd(0, 0)
         gate(1, 1)
-        weave_wd(1, 1)
-        weave_wd(1, 0)
-        quantize_h(0, 0)
-        quantize_h(0, 1)
-        quantize_wd(0, 1)
-        quantize_wd(0, 0)
+        ups(1, 0)
         ups(1, 1)
-        finish_x(3)
-        quantize_wd(1, 1)
-        quantize_wd(1, 0)
-        gate(2, 0)
-        weave_x(3)
+        weave_wd(1, 0, 2, "scalar", woven(wd_room, 1024, 256))
         quantize_x(3)
-        ups(2, 0)
-        quantize_h(1, 0)
-        quantize_h(1, 1)
-        gate(2, 1)
-        ups(2, 1)
-        down(0)
-        down(1)
-        gate(3, 0)
-        quantize_h(2, 0)
+        quantize_wd(0, 0)
+        weave_wd(1, 2, 2, "vector")
+        quantize_both(0)
+        quantize_wd(1, 0)
+        quantize_wd(1, 2)
         weave_x(4)
-        ups(3, 0)
-        quantize_h(2, 1)
+        gate(2, 0)
+        quantize_both(1)
+        gate(2, 1)
+        up(2, 0, 0)
+        down(0)
+        up(2, 0, 1)
+        gate(3, 0)
+        up(2, 1, 0)
+        down(1, part=0)
+        quantize_h(2, 0)
+        up(2, 1, 1)
         quantize_x(4)
         gate(3, 1)
-        ups(3, 1)
-        down(2)
-        quantize_h(3, 0)
+        up(3, 0, 0)
+        down(1, part=1)
+        quantize_h(2, 1)
+        up(3, 0, 1)
         gate(4, 0)
+        up(3, 1, 0)
+        down(2, part=0)
+        quantize_h(3, 0)
+        up(3, 1, 1)
         gate(4, 1)
+        down(2, part=1)
+        quantize_h(3, 1, 0)
         ups(4, 0)
-        quantize_h(3, 1)
+        down(3, c=0)
+        quantize_h(3, 1, 1)
         ups(4, 1)
+        down(3, c=1)
         quantize_h(4, 0)
-        for b in range(PASSES):
-            down_by_pass(last - 1, b)
-        down_by_pass(last, 0)
+        down_by_pass(last, 0, "gate")
         quantize_h(last, 1)
-        down_by_pass(last, 1)
-        store(last - 1, 0, 2, accs[last - 1][0], False, nc.sync)
-        store(last - 1, 2, 2, accs[last - 1][1], False, nc.sync)
-        store(last, 0, 2, accs[last][0], True, nc.sync)
-        store(last, 2, 2, accs[last][1], False, nc.scalar)
+        down_by_pass(last, 1, "gate")
+        store(last, span(last, None), 0, 2, accs[last][0], True, nc.sync)
+        store(last, span(last, None), 2, 2, accs[last][1], False, nc.scalar)

@@ -25,6 +25,7 @@ CHUNK = 128
 N_TILES = N // P
 WIDTHS = (128, 256, 256, 256, 128)
 STARTS = tuple(sum(WIDTHS[:q]) for q in range(len(WIDTHS)))
+AHEAD = STARTS[-1]
 GROUPS = len(WIDTHS)
 SPREAD = (1, 1, 2, 2, 2)
 GATE_BANKS, UP_BANKS, DOWN_BANKS = 3, 3, 2
@@ -39,7 +40,13 @@ def tile_list_gelu_none_kernel(
         laid = ctx.enter_context(tc.tile_pool(name="laid", bufs=1))
         psum = ctx.enter_context(tc.psum_pool(name="psum", bufs=1))
 
-        places = {"act1_1": 2048, "wd_bf1_2": 64, "x_codes3": 2112, "h_codes0": 3136, "wd_codes0": 4160, "act2_0": 8192, "x_codes4": 8192}
+        places = {"act1_1": 2048, "wd_late": 64, "x_codes3": 2112, "h_codes0": 3136, "wd_codes0": 4160, "act2_0": 8192, "x_codes4": 8192, "act1_0": 12288, "wd_codes1": 12288, "plane3": 16384, "wd_room": 20480, "x_bf2": 24576, "picked_low": 32768, "last_picks": 32768}
+
+        def place(name, shape, dtype):
+            if name in places:
+                return laid.tile(shape, dtype, name=name, align_bytes=64, offset=places[name])
+            return keep.tile(shape, dtype, name=name, align_bytes=64)
+
         offsets = keep.tile([P, J // 16], U16, name="offsets")
         nc.sync.dma_start(offsets[:], offs)
 
@@ -53,7 +60,7 @@ def tile_list_gelu_none_kernel(
 
 
         x_planes = xT.rearrange("(p i) t -> i p t", i=PACK)
-        planes = [keep.tile([P, T], F32, name=f"plane{i}", align_bytes=64) for i in range(PACK)]
+        planes = [place(f"plane{i}", [P, T], F32) for i in range(PACK)]
         words_raw = [keep.tile([P, R // 2], I32, name=f"words_raw{g}", align_bytes=64) for g in range(2)]
         wd_rows = wd.rearrange("(b s t e) n -> b t s (e n)", b=PASSES, t=PACK, e=4)
         wd_raw = [keep.tile([P, PACK, N], F32, name=f"wd_raw{b}") for b in range(PASSES)]
@@ -67,9 +74,10 @@ def tile_list_gelu_none_kernel(
         nc.sync.dma_start(planes[0][:], x_planes[0])
         nc.sync.dma_start(weight[:, :256], wgt[:, :256])
         nc.sync.dma_start(weight[:, 256:], wgt[:, 256:])
-        load_scales(0, wg_scales)
         for i in range(1, PACK):
             nc.sync.dma_start(planes[i][:], x_planes[i])
+            if i == 1:
+                load_scales(0, wg_scales)
         nc.sync.dma_start(words_raw[0][:], wg_words[0].bitcast(I32))
         load_scales(1, wu_scales)
         nc.sync.dma_start(words_raw[1][:], wu_words[0].bitcast(I32))
@@ -77,7 +85,7 @@ def tile_list_gelu_none_kernel(
             for t in range(PACK):
                 nc.sync.dma_start(wd_raw[b][:, t, :], wd_rows[b, t])
 
-        w_scales = [keep.tile([P, R], U8, name=f"w_scales{g}", align_bytes=64) for g in range(2)]
+        w_scales = [place(f"w_scales{g}", [P, R], U8) for g in range(2)]
         roles = {"gate": (0, GATE_BANKS), "up": (GATE_BANKS, UP_BANKS), "down": (GATE_BANKS + UP_BANKS, DOWN_BANKS), "all": (0, 8)}
         taken = {role: [] for role in roles}
 
@@ -87,7 +95,7 @@ def tile_list_gelu_none_kernel(
             taken[role].append(shape)
             return psum.tile(shape, F32, name=f"bank{first + len(taken[role]) % count}")
 
-        w_codes = [keep.tile([P, 2 * R], U8, name=f"w_codes{g}", align_bytes=64) for g in range(2)]
+        w_codes = [place(f"w_codes{g}", [P, 2 * R], U8) for g in range(2)]
 
         def order_scales(g, on_vector):
             dst = w_scales[g][:].bitcast(U32).rearrange("p (b t s) -> p b t s", t=PACK, s=32)
@@ -109,29 +117,24 @@ def tile_list_gelu_none_kernel(
             cols = offsets[:, start // 16 : (start + width) // 16]
             nc.vector.tensor_tensor(dst, planes[i][:].indirect(cols), weight[:, start : start + width], MULT)
 
-        picked_low = keep.tile([P, 2, J], F32, name="picked_low")
-        def place(name, shape, dtype):
-            if name in places:
-                return laid.tile(shape, dtype, name=name, align_bytes=64, offset=places[name])
-            return keep.tile(shape, dtype, name=name, align_bytes=64)
-
+        picked_low = place("picked_low", [P, 2, J], F32)
         def room(name, words):
             return place(name, [P, words], F32)
 
         def woven(tile, first, width):
             return tile[:, first : first + 2 * width].bitcast(BF16).rearrange("p (j i) -> p j i", i=PACK)
 
+        ahead = range(4)
         picked = {}
         h_all = {}
         x_bf = {}
-        picked[0] = room("picked0", 256)
-        picked[1] = room("picked1", 512)
-        picked[2] = room("picked2", 512)
-        x_bf[0] = woven(picked[2], 256, 128)
-        x_bf[1] = woven(room("x_bf1", 512), 0, 256)
+        early = room("early", 2 * AHEAD + 256)
+        x_bf[0] = woven(early, AHEAD + STARTS[2], 128)
+        x_bf[1] = woven(early, AHEAD + STARTS[3], 256)
         x_bf[2] = woven(room("x_bf2", 512), 0, 256)
         x_bf[3] = woven(room("x_bf3", 512), 0, 256)
         x_bf[4] = woven(room("x_bf4", 256), 0, 128)
+        picked[4] = early[:, 2 * AHEAD :]
 
         x_codes = [place(f"x_codes{q}", [P, w], U32) for q, w in enumerate(WIDTHS)]
         x_scales = [keep.tile([P, w], U8, name=f"x_scales{q}", align_bytes=64) for q, w in enumerate(WIDTHS)]
@@ -152,10 +155,18 @@ def tile_list_gelu_none_kernel(
             gather(picked[q][:, : WIDTHS[q]], 2, STARTS[q], WIDTHS[q])
 
         def gather3(q):
+            if q in ahead:
+                first = AHEAD + STARTS[q]
+                gather(early[:, first : first + WIDTHS[q]], 3, STARTS[q], WIDTHS[q])
+                return
             gather(picked[q][:, WIDTHS[q] : 2 * WIDTHS[q]], 3, STARTS[q], WIDTHS[q])
 
         def weave_x(q, engine="scalar"):
-            weave_pair(q, 2, picked[q][:, : 2 * WIDTHS[q]].rearrange("p (i j) -> p i j", i=2), engine)
+            if q in ahead:
+                pair = early[:, : 2 * AHEAD].rearrange("p (i j) -> p i j", i=2)[:, :, STARTS[q] : STARTS[q] + WIDTHS[q]]
+            else:
+                pair = picked[q][:, : 2 * WIDTHS[q]].rearrange("p (i j) -> p i j", i=2)
+            weave_pair(q, 2, pair, engine)
 
         def quantize_x(q):
             nc.vector.quantize_mx(
@@ -309,13 +320,14 @@ def tile_list_gelu_none_kernel(
         last = GROUPS - 1
         gather(picked_low[:, 0, :256], 0, 0, 256)
         gather(picked_low[:, 0, 256:], 0, 256, 768)
+        for groups in ((0, 1), (2,), (3, 4)):
+            first = STARTS[groups[0]]
+            width = sum(WIDTHS[q] for q in groups)
+            gather(picked_low[:, 1, first : first + width], 1, first, width)
+            for q in groups:
+                weave_pair(q, 0, picked_low[:, :, STARTS[q] : STARTS[q] + WIDTHS[q]], "scalar")
         order_scales(0, False)
-        for q in range(GROUPS):
-            cols = slice(STARTS[q], STARTS[q] + WIDTHS[q])
-            gather(picked_low[:, 1, cols], 1, STARTS[q], WIDTHS[q])
-            weave_pair(q, 0, picked_low[:, :, cols], "scalar")
-        for q in range(3):
-            gather2(q)
+        gather(early[:, :AHEAD], 2, 0, AHEAD)
         gather3(0)
         weave_x(0)
         gather3(1)
@@ -329,33 +341,33 @@ def tile_list_gelu_none_kernel(
         gate(0, 0)
         weave_x(2)
         gate(0, 1)
-        gather2(3, "x_bf1")
         gather3(3)
+        gather2(4)
+        gather3(4)
         quantize_x(2)
         gate(1, 0)
-        weave_x(3)
-        gather2(4, "x_bf2")
-        gather3(4)
-        wd_room = room("plane3", 2048)
+        wd_room = room("wd_room", 2048)
         weave_wd(0, 0, 4, "gpsimd", woven(wd_room, 0, 512))
+        weave_wd(1, 0, 1, "gpsimd", woven(wd_room, 1024, 128))
         h_all[0] = room("weight", 512)[:]
         ups(0, 0)
         ups(0, 1)
         gate(1, 1)
         ups(1, 0)
         ups(1, 1)
-        weave_wd(1, 0, 2, "scalar", woven(wd_room, 1024, 256))
+        weave_x(3)
+        weave_wd(1, 1, 1, "scalar", woven(wd_room, 1280, 128))
         quantize_x(3)
         quantize_wd(0, 0)
-        weave_wd(1, 2, 2, "vector")
+        weave_wd(1, 2, 2, "vector", woven(room("wd_late", 512), 0, 256))
         quantize_both(0)
-        quantize_wd(1, 0)
+        quantize_wd(1, 0, woven(wd_room, 1024, 256))
         quantize_wd(1, 2)
-        weave_x(4)
         gate(2, 0)
         quantize_both(1)
         gate(2, 1)
         up(2, 0, 0)
+        weave_x(4)
         down(0)
         up(2, 0, 1)
         gate(3, 0)

@@ -348,7 +348,6 @@ def tile_list_gelu_none_kernel(
         gate(1, 0)
         wd_room = room("wd_room", 2048)
         weave_wd(0, 0, 4, "gpsimd", woven(wd_room, 0, 512))
-        weave_wd(1, 0, 1, "gpsimd", woven(wd_room, 1024, 128))
         h_all[0] = room("weight", 512)[:]
         ups(0, 0)
         ups(0, 1)
@@ -356,7 +355,7 @@ def tile_list_gelu_none_kernel(
         ups(1, 0)
         ups(1, 1)
         weave_x(3)
-        weave_wd(1, 1, 1, "scalar", woven(wd_room, 1280, 128))
+        weave_wd(1, 0, 2, "scalar", woven(wd_room, 1024, 256))
         quantize_x(3)
         quantize_wd(0, 0)
         weave_wd(1, 2, 2, "vector", woven(room("wd_late", 512), 0, 256))

@@ -25,7 +25,7 @@ CHUNK = 128
 N_TILES = N // P
 WIDTHS = (128, 256, 256, 256, 128)
 STARTS = tuple(sum(WIDTHS[:q]) for q in range(len(WIDTHS)))
-AHEAD = STARTS[-1]
+AHEAD = J
 GROUPS = len(WIDTHS)
 SPREAD = (1, 1, 2, 2, 2)
 GATE_BANKS, UP_BANKS, DOWN_BANKS = 3, 3, 2
@@ -40,7 +40,7 @@ def tile_list_gelu_none_kernel(
         laid = ctx.enter_context(tc.tile_pool(name="laid", bufs=1))
         psum = ctx.enter_context(tc.psum_pool(name="psum", bufs=1))
 
-        places = {"act1_1": 2048, "wd_late": 64, "x_codes3": 2112, "h_codes0": 3136, "wd_codes0": 4160, "act2_0": 8192, "x_codes4": 8192, "act1_0": 12288, "wd_codes1": 12288, "plane3": 16384, "wd_room": 20480, "x_bf2": 24576, "picked_low": 32768, "last_picks": 32768}
+        places = {"act1_1": 2048, "wd_late": 64, "x_codes3": 2112, "h_codes0": 3136, "wd_codes0": 4160, "act2_0": 8192, "x_codes4": 8192, "act1_0": 12288, "wd_codes1": 12288, "plane3": 16384, "wd_room": 20480, "x_bf2": 24576}
 
         def place(name, shape, dtype):
             if name in places:
@@ -76,10 +76,9 @@ def tile_list_gelu_none_kernel(
         nc.sync.dma_start(weight[:, 256:], wgt[:, 256:])
         for i in range(1, PACK):
             nc.sync.dma_start(planes[i][:], x_planes[i])
-            if i == 1:
-                load_scales(0, wg_scales)
+            if i <= 2:
+                load_scales(i - 1, (wg_scales, wu_scales)[i - 1])
         nc.sync.dma_start(words_raw[0][:], wg_words[0].bitcast(I32))
-        load_scales(1, wu_scales)
         nc.sync.dma_start(words_raw[1][:], wu_words[0].bitcast(I32))
         for b in range(PASSES):
             for t in range(PACK):
@@ -124,17 +123,16 @@ def tile_list_gelu_none_kernel(
         def woven(tile, first, width):
             return tile[:, first : first + 2 * width].bitcast(BF16).rearrange("p (j i) -> p j i", i=PACK)
 
-        ahead = range(4)
+        ahead = range(GROUPS)
         picked = {}
         h_all = {}
         x_bf = {}
-        early = room("early", 2 * AHEAD + 256)
+        early = room("early", 2 * AHEAD + 128)
         x_bf[0] = woven(early, AHEAD + STARTS[2], 128)
         x_bf[1] = woven(early, AHEAD + STARTS[3], 256)
         x_bf[2] = woven(room("x_bf2", 512), 0, 256)
         x_bf[3] = woven(room("x_bf3", 512), 0, 256)
         x_bf[4] = woven(room("x_bf4", 256), 0, 128)
-        picked[4] = early[:, 2 * AHEAD :]
 
         x_codes = [place(f"x_codes{q}", [P, w], U32) for q, w in enumerate(WIDTHS)]
         x_scales = [keep.tile([P, w], U8, name=f"x_scales{q}", align_bytes=64) for q, w in enumerate(WIDTHS)]
@@ -230,6 +228,15 @@ def tile_list_gelu_none_kernel(
                 for t in range(per_bank):
                     first_product(bank[:, t, :], 0, b, first + t, q, slice(0, width))
                 nc.scalar.activation(act[q, b][:, first : first + per_bank, :], bank[:], GELU)
+
+        def gate_by_chunks(q, b):
+            act[q, b] = place(f"act{q}_{b}", [P, PACK, WIDTHS[q]], F32)
+            for c in range(WIDTHS[q] // CHUNK):
+                cols = slice(c * CHUNK, (c + 1) * CHUNK)
+                bank = next_bank("gate", [P, PACK, CHUNK])
+                for t in range(PACK):
+                    first_product(bank[:, t, :], 0, b, t, q, cols)
+                nc.scalar.activation(act[q, b][:, :, cols], bank[:], GELU)
 
         def up(q, b, c, slot=None):
             if (b, c) == (0, 0):
@@ -327,6 +334,7 @@ def tile_list_gelu_none_kernel(
             for q in groups:
                 weave_pair(q, 0, picked_low[:, :, STARTS[q] : STARTS[q] + WIDTHS[q]], "scalar")
         order_scales(0, False)
+        order_scales(1, False)
         gather(early[:, :AHEAD], 2, 0, AHEAD)
         gather3(0)
         weave_x(0)
@@ -334,7 +342,6 @@ def tile_list_gelu_none_kernel(
         weave_x(1)
         order_words(0)
         quantize_x(0)
-        order_scales(1, False)
         order_words(1)
         gather3(2)
         quantize_x(1)
@@ -342,7 +349,6 @@ def tile_list_gelu_none_kernel(
         weave_x(2)
         gate(0, 1)
         gather3(3)
-        gather2(4)
         gather3(4)
         quantize_x(2)
         gate(1, 0)

@@ -1,6 +1,7 @@
 from contextlib import ExitStack
 
 import concourse.mybir as mybir
+from concourse.masks import make_identity
 
 K, R, N, T, J = 512, 1024, 512, 2048, 1024
 FLOPS = 2 * K * R * J * 2 + 2 * R * N * J
@@ -25,7 +26,7 @@ CHUNK = 128
 N_TILES = N // P
 WIDTHS = (128, 256, 256, 256, 128)
 STARTS = tuple(sum(WIDTHS[:q]) for q in range(len(WIDTHS)))
-AHEAD = J
+AHEAD = STARTS[-1]
 GROUPS = len(WIDTHS)
 SPREAD = (1, 1, 2, 2, 2)
 GATE_BANKS, UP_BANKS, DOWN_BANKS = 3, 3, 2
@@ -40,7 +41,7 @@ def tile_list_gelu_none_kernel(
         laid = ctx.enter_context(tc.tile_pool(name="laid", bufs=1))
         psum = ctx.enter_context(tc.psum_pool(name="psum", bufs=1))
 
-        places = {"act1_1": 2048, "wd_late": 64, "x_codes3": 2112, "h_codes0": 3136, "wd_codes0": 4160, "act2_0": 8192, "x_codes4": 8192, "act1_0": 12288, "wd_codes1": 12288, "plane3": 16384, "wd_room": 20480, "x_bf2": 24576}
+        places = {"act1_1": 2048, "wd_late": 64, "x_codes3": 2112, "h_codes0": 3136, "wd_codes0": 4160, "act2_0": 8192, "x_codes4": 8192, "act1_0": 12288, "wd_codes1": 12288, "plane3": 16384, "wd_room": 20480, "x_bf2": 24576, "picked_low": 32768, "w_scales0": 32768, "w_scales1": 33792}
 
         def place(name, shape, dtype):
             if name in places:
@@ -52,11 +53,15 @@ def tile_list_gelu_none_kernel(
 
         scales_raw = [keep.tile([P, R // 4], I32, name=f"scales_raw{g}") for g in range(2)]
         for g in range(2):
-            nc.vector.memset(scales_raw[g][:], 0)
+            nc.gpsimd.memset(scales_raw[g][:], 0)
         warm_in = keep.tile([P, 8], F32, name="warm_in")
         warm_out = keep.tile([P, 8], F32, name="warm_out")
+        wgt_rows = keep.tile([P, CHUNK], F32, name="wgt_rows")
+        nc.sync.dma_start(wgt_rows[:], wgt.rearrange("(a e) j -> e a j", e=8)[0])
         nc.vector.memset(warm_in[:], 0.0)
         nc.scalar.activation(warm_out[:], warm_in[:], GELU)
+        identity = keep.tile([P, P], F32, name="identity")
+        make_identity(nc, identity[:])
 
 
         x_planes = xT.rearrange("(p i) t -> i p t", i=PACK)
@@ -70,21 +75,18 @@ def tile_list_gelu_none_kernel(
             for r in range(4):
                 nc.sync.dma_start(scales_raw[g][r:P:32, :], rows[r])
 
-        weight = keep.tile([P, J], F32, name="weight", align_bytes=64)
         nc.sync.dma_start(planes[0][:], x_planes[0])
-        nc.sync.dma_start(weight[:, :256], wgt[:, :256])
-        nc.sync.dma_start(weight[:, 256:], wgt[:, 256:])
         for i in range(1, PACK):
             nc.sync.dma_start(planes[i][:], x_planes[i])
             if i <= 2:
                 load_scales(i - 1, (wg_scales, wu_scales)[i - 1])
         nc.sync.dma_start(words_raw[0][:], wg_words[0].bitcast(I32))
-        nc.sync.dma_start(words_raw[1][:], wu_words[0].bitcast(I32))
         for b in range(PASSES):
             for t in range(PACK):
                 nc.sync.dma_start(wd_raw[b][:, t, :], wd_rows[b, t])
+                if (b, t) == (0, 0):
+                    nc.sync.dma_start(words_raw[1][:], wu_words[0].bitcast(I32))
 
-        w_scales = [place(f"w_scales{g}", [P, R], U8) for g in range(2)]
         roles = {"gate": (0, GATE_BANKS), "up": (GATE_BANKS, UP_BANKS), "down": (GATE_BANKS + UP_BANKS, DOWN_BANKS), "all": (0, 8)}
         taken = {role: [] for role in roles}
 
@@ -94,6 +96,21 @@ def tile_list_gelu_none_kernel(
             taken[role].append(shape)
             return psum.tile(shape, F32, name=f"bank{first + len(taken[role]) % count}")
 
+        weight = keep.tile([P, J], F32, name="weight", align_bytes=64)
+        turned = psum.tile([P, P], F32, name="bank7")
+        nc.tensor.transpose(turned[:], wgt_rows[:], identity[:])
+        done = 0
+        for s, count in enumerate(SPREAD):
+            wide = keep.tile([P, count, 16, 8], F32, name=f"wide{s}")
+            src = turned[:].rearrange("e (a c) -> e c a", c=8)[:, done : done + count, :]
+            nc.vector.tensor_copy(wide[:], src.unsqueeze(3).to_broadcast([P, count, 16, 8]))
+            back = psum.tile([P, count, CHUNK], F32, name=f"bank{s}")
+            for c in range(count):
+                nc.tensor.transpose(back[:, c, :], wide[:, c, :, :].rearrange("e a q -> e (a q)"), identity[:])
+            nc.scalar.copy(weight[:, done * CHUNK : (done + count) * CHUNK], back[:].rearrange("p c e -> p (c e)"))
+            done = done + count
+
+        w_scales = [place(f"w_scales{g}", [P, R], U8) for g in range(2)]
         w_codes = [place(f"w_codes{g}", [P, 2 * R], U8) for g in range(2)]
 
         def order_scales(g, on_vector):
@@ -123,16 +140,17 @@ def tile_list_gelu_none_kernel(
         def woven(tile, first, width):
             return tile[:, first : first + 2 * width].bitcast(BF16).rearrange("p (j i) -> p j i", i=PACK)
 
-        ahead = range(GROUPS)
+        ahead = range(4)
         picked = {}
         h_all = {}
         x_bf = {}
-        early = room("early", 2 * AHEAD + 128)
+        early = room("early", 2 * AHEAD + 256)
         x_bf[0] = woven(early, AHEAD + STARTS[2], 128)
         x_bf[1] = woven(early, AHEAD + STARTS[3], 256)
         x_bf[2] = woven(room("x_bf2", 512), 0, 256)
         x_bf[3] = woven(room("x_bf3", 512), 0, 256)
         x_bf[4] = woven(room("x_bf4", 256), 0, 128)
+        picked[4] = early[:, 2 * AHEAD :]
 
         x_codes = [place(f"x_codes{q}", [P, w], U32) for q, w in enumerate(WIDTHS)]
         x_scales = [keep.tile([P, w], U8, name=f"x_scales{q}", align_bytes=64) for q, w in enumerate(WIDTHS)]
@@ -325,8 +343,10 @@ def tile_list_gelu_none_kernel(
                 down_pass(acc, m, q, b, span(q, None), b == 0 and m % 2 == 0, b == PASSES - 1 and m % 2 == 1)
 
         last = GROUPS - 1
-        gather(picked_low[:, 0, :256], 0, 0, 256)
-        gather(picked_low[:, 0, 256:], 0, 256, 768)
+        gather(picked_low[:, 0, :128], 0, 0, 128)
+        gather(picked_low[:, 0, 128:256], 0, 128, 128)
+        gather(picked_low[:, 0, 256:512], 0, 256, 256)
+        gather(picked_low[:, 0, 512:], 0, 512, 512)
         for groups in ((0, 1), (2,), (3, 4)):
             first = STARTS[groups[0]]
             width = sum(WIDTHS[q] for q in groups)
@@ -342,22 +362,23 @@ def tile_list_gelu_none_kernel(
         weave_x(1)
         order_words(0)
         quantize_x(0)
-        order_words(1)
         gather3(2)
+        order_words(1)
         quantize_x(1)
         gate(0, 0)
         weave_x(2)
         gate(0, 1)
         gather3(3)
+        gather2(4)
         gather3(4)
         quantize_x(2)
-        gate(1, 0)
+        gate_by_chunks(1, 0)
         wd_room = room("wd_room", 2048)
         weave_wd(0, 0, 4, "gpsimd", woven(wd_room, 0, 512))
         h_all[0] = room("weight", 512)[:]
         ups(0, 0)
         ups(0, 1)
-        gate(1, 1)
+        gate_by_chunks(1, 1)
         ups(1, 0)
         ups(1, 1)
         weave_x(3)

@@ -22,14 +22,12 @@ P = 128
 PACK = 4
 PASSES = R // (P * PACK)
 BANK = 512
+BANKS = 8
 CHUNK = 128
 N_TILES = N // P
 WIDTHS = (128, 256, 256, 256, 128)
 STARTS = tuple(sum(WIDTHS[:q]) for q in range(len(WIDTHS)))
-AHEAD = STARTS[-1]
-GROUPS = len(WIDTHS)
-SPREAD = (1, 1, 2, 2, 2)
-GATE_BANKS, UP_BANKS, DOWN_BANKS = 3, 3, 2
+A, B, C, D, E = range(len(WIDTHS))
 
 
 def tile_list_gelu_none_kernel(
@@ -41,123 +39,47 @@ def tile_list_gelu_none_kernel(
         laid = ctx.enter_context(tc.tile_pool(name="laid", bufs=1))
         psum = ctx.enter_context(tc.psum_pool(name="psum", bufs=1))
 
-        places = {"act1_1": 2048, "wd_late": 64, "x_codes3": 2112, "h_codes0": 3136, "wd_codes0": 4160, "act2_0": 8192, "x_codes4": 8192, "act1_0": 12288, "wd_codes1": 12288, "plane3": 16384, "wd_room": 20480, "x_bf2": 24576, "picked_low": 32768, "w_scales0": 32768, "w_scales1": 33792}
+        places = {"plane3": 0, "x_bf2": 8192, "wd_bf0": 4096, "act2_0_0": 12288, "h_codes0": 11328, "x_codes3": 12352, "h_codes1": 13888, "h_bf1": 16384, "wd_bf1": 16384, "w_scales0": 20480, "w_scales1": 21504, "wide4": 20480}
 
         def place(name, shape, dtype):
             if name in places:
                 return laid.tile(shape, dtype, name=name, align_bytes=64, offset=places[name])
             return keep.tile(shape, dtype, name=name, align_bytes=64)
 
-        offsets = keep.tile([P, J // 16], U16, name="offsets")
-        nc.sync.dma_start(offsets[:], offs)
+        turns = []
 
+        def next_bank(shape):
+            turns.append(shape)
+            return psum.tile(shape, F32, name=f"bank{len(turns) % BANKS}")
+
+        offsets = keep.tile([P, J // 16], U16, name="offsets")
+        wgt_rows = keep.tile([P, CHUNK], F32, name="wgt_rows")
         scales_raw = [keep.tile([P, R // 4], I32, name=f"scales_raw{g}") for g in range(2)]
-        for g in range(2):
-            nc.gpsimd.memset(scales_raw[g][:], 0)
+        words_raw = [place(f"words_raw{g}", [P, R // 2], I32) for g in range(2)]
+        planes = [place(f"plane{i}", [P, T], F32) for i in range(PACK)]
+        wd_raw = [keep.tile([P, PACK, N], F32, name=f"wd_raw{b}") for b in range(PASSES)]
+        x_planes = xT.rearrange("(p i) t -> i p t", i=PACK)
+        wd_rows = wd.rearrange("(b s t e) n -> b t s (e n)", b=PASSES, t=PACK, e=4)
         warm_in = keep.tile([P, 8], F32, name="warm_in")
         warm_out = keep.tile([P, 8], F32, name="warm_out")
-        wgt_rows = keep.tile([P, CHUNK], F32, name="wgt_rows")
-        nc.sync.dma_start(wgt_rows[:], wgt.rearrange("(a e) j -> e a j", e=8)[0])
-        nc.vector.memset(warm_in[:], 0.0)
-        nc.scalar.activation(warm_out[:], warm_in[:], GELU)
         identity = keep.tile([P, P], F32, name="identity")
-        make_identity(nc, identity[:])
+        weight = place("weight", [P, J], F32)
 
-
-        x_planes = xT.rearrange("(p i) t -> i p t", i=PACK)
-        planes = [place(f"plane{i}", [P, T], F32) for i in range(PACK)]
-        words_raw = [keep.tile([P, R // 2], I32, name=f"words_raw{g}", align_bytes=64) for g in range(2)]
-        wd_rows = wd.rearrange("(b s t e) n -> b t s (e n)", b=PASSES, t=PACK, e=4)
-        wd_raw = [keep.tile([P, PACK, N], F32, name=f"wd_raw{b}") for b in range(PASSES)]
-
-        def load_scales(g, src):
-            rows = src[0].bitcast(I32).rearrange("(q r) n -> r q n", r=4)
+        def load_scales(g):
+            rows = (wg_scales, wu_scales)[g][0].bitcast(I32).rearrange("(q r) n -> r q n", r=4)
             for r in range(4):
                 nc.sync.dma_start(scales_raw[g][r:P:32, :], rows[r])
 
-        nc.sync.dma_start(planes[0][:], x_planes[0])
-        for i in range(1, PACK):
+        def load_words(g):
+            nc.sync.dma_start(words_raw[g][:], (wg_words, wu_words)[g][0].bitcast(I32))
+
+        def load_plane(i):
             nc.sync.dma_start(planes[i][:], x_planes[i])
-            if i <= 2:
-                load_scales(i - 1, (wg_scales, wu_scales)[i - 1])
-        nc.sync.dma_start(words_raw[0][:], wg_words[0].bitcast(I32))
-        for b in range(PASSES):
-            for t in range(PACK):
-                nc.sync.dma_start(wd_raw[b][:, t, :], wd_rows[b, t])
-                if (b, t) == (0, 0):
-                    nc.sync.dma_start(words_raw[1][:], wu_words[0].bitcast(I32))
 
-        roles = {"gate": (0, GATE_BANKS), "up": (GATE_BANKS, UP_BANKS), "down": (GATE_BANKS + UP_BANKS, DOWN_BANKS), "all": (0, 8)}
-        taken = {role: [] for role in roles}
+        def load_wd(b, t):
+            nc.sync.dma_start(wd_raw[b][:, t, :], wd_rows[b, t])
 
-        def next_bank(role, shape):
-            role = "all"
-            first, count = roles[role]
-            taken[role].append(shape)
-            return psum.tile(shape, F32, name=f"bank{first + len(taken[role]) % count}")
-
-        weight = keep.tile([P, J], F32, name="weight", align_bytes=64)
-        turned = psum.tile([P, P], F32, name="bank7")
-        nc.tensor.transpose(turned[:], wgt_rows[:], identity[:])
-        done = 0
-        for s, count in enumerate(SPREAD):
-            wide = keep.tile([P, count, 16, 8], F32, name=f"wide{s}")
-            src = turned[:].rearrange("e (a c) -> e c a", c=8)[:, done : done + count, :]
-            nc.vector.tensor_copy(wide[:], src.unsqueeze(3).to_broadcast([P, count, 16, 8]))
-            back = psum.tile([P, count, CHUNK], F32, name=f"bank{s}")
-            for c in range(count):
-                nc.tensor.transpose(back[:, c, :], wide[:, c, :, :].rearrange("e a q -> e (a q)"), identity[:])
-            nc.scalar.copy(weight[:, done * CHUNK : (done + count) * CHUNK], back[:].rearrange("p c e -> p (c e)"))
-            done = done + count
-
-        w_scales = [place(f"w_scales{g}", [P, R], U8) for g in range(2)]
-        w_codes = [place(f"w_codes{g}", [P, 2 * R], U8) for g in range(2)]
-
-        def order_scales(g, on_vector):
-            dst = w_scales[g][:].bitcast(U32).rearrange("p (b t s) -> p b t s", t=PACK, s=32)
-            src = scales_raw[g][:].bitcast(U32).rearrange("p (b s t) -> p b t s", t=PACK, s=32)
-            if on_vector:
-                nc.vector.tensor_copy(dst.bitcast(I32), src.bitcast(I32))
-            else:
-                nc.scalar.copy(dst, src)
-
-        def order_words(g, on_vector=True):
-            dst = w_codes[g][:].bitcast(U32).rearrange("p (b t s w) -> p b t s w", t=PACK, s=32, w=2)
-            src = words_raw[g][:].bitcast(U32).rearrange("p (b s t w) -> p b t s w", t=PACK, s=32, w=2)
-            if on_vector:
-                nc.vector.tensor_copy(dst.bitcast(I32), src.bitcast(I32))
-            else:
-                nc.scalar.copy(dst, src)
-
-        def gather(dst, i, start, width):
-            cols = offsets[:, start // 16 : (start + width) // 16]
-            nc.vector.tensor_tensor(dst, planes[i][:].indirect(cols), weight[:, start : start + width], MULT)
-
-        picked_low = place("picked_low", [P, 2, J], F32)
-        def room(name, words):
-            return place(name, [P, words], F32)
-
-        def woven(tile, first, width):
-            return tile[:, first : first + 2 * width].bitcast(BF16).rearrange("p (j i) -> p j i", i=PACK)
-
-        ahead = range(4)
-        picked = {}
-        h_all = {}
-        x_bf = {}
-        early = room("early", 2 * AHEAD + 256)
-        x_bf[0] = woven(early, AHEAD + STARTS[2], 128)
-        x_bf[1] = woven(early, AHEAD + STARTS[3], 256)
-        x_bf[2] = woven(room("x_bf2", 512), 0, 256)
-        x_bf[3] = woven(room("x_bf3", 512), 0, 256)
-        x_bf[4] = woven(room("x_bf4", 256), 0, 128)
-        picked[4] = early[:, 2 * AHEAD :]
-
-        x_codes = [place(f"x_codes{q}", [P, w], U32) for q, w in enumerate(WIDTHS)]
-        x_scales = [keep.tile([P, w], U8, name=f"x_scales{q}", align_bytes=64) for q, w in enumerate(WIDTHS)]
-
-        def weave_pair(q, first, src, engine):
-            dst = x_bf[q][:, :, first : first + 2].rearrange("p (c e) i -> p c i e", e=2)
-            src = src.rearrange("p i (c e) -> p c i e", e=2)
+        def copy(engine, dst, src):
             if engine == "vector":
                 nc.vector.tensor_copy(dst, src)
             elif engine == "scalar":
@@ -165,58 +87,115 @@ def tile_list_gelu_none_kernel(
             else:
                 nc.gpsimd.tensor_scalar(dst, src, 1.0, 0.0, MULT, ADD)
 
-        def gather2(q, slot=None):
-            if slot:
-                picked[q] = room(slot, 2 * WIDTHS[q])
-            gather(picked[q][:, : WIDTHS[q]], 2, STARTS[q], WIDTHS[q])
+        def turn_rows():
+            turned = next_bank([P, P])
+            nc.tensor.transpose(turned[:], wgt_rows[:], identity[:])
+            return turned
 
-        def gather3(q):
-            if q in ahead:
-                first = AHEAD + STARTS[q]
-                gather(early[:, first : first + WIDTHS[q]], 3, STARTS[q], WIDTHS[q])
-                return
-            gather(picked[q][:, WIDTHS[q] : 2 * WIDTHS[q]], 3, STARTS[q], WIDTHS[q])
+        wide = {}
 
-        def weave_x(q, engine="scalar"):
-            if q in ahead:
-                pair = early[:, : 2 * AHEAD].rearrange("p (i j) -> p i j", i=2)[:, :, STARTS[q] : STARTS[q] + WIDTHS[q]]
-            else:
-                pair = picked[q][:, : 2 * WIDTHS[q]].rearrange("p (i j) -> p i j", i=2)
-            weave_pair(q, 2, pair, engine)
+        def widen(turned, first, count, engine):
+            wide[first] = place(f"wide{first}", [P, count, 16, 8], F32)
+            src = turned[:].rearrange("e (a c) -> e c a", c=8)[:, first : first + count, :]
+            copy(engine, wide[first][:], src.unsqueeze(3).to_broadcast([P, count, 16, 8]))
 
-        def quantize_x(q):
-            nc.vector.quantize_mx(
-                out=x_codes[q][:].bitcast(FP8X4), scales=x_scales[q][:], in_=x_bf[q].rearrange("p j i -> p (j i)")
-            )
+        def turn_back(first, count, engine):
+            back = next_bank([P, count, CHUNK])
+            for c in range(count):
+                nc.tensor.transpose(back[:, c, :], wide[first][:, c, :, :].rearrange("e a q -> e (a q)"), identity[:])
+            copy(engine, weight[:, first * CHUNK : (first + count) * CHUNK], back[:].rearrange("p c e -> p (c e)"))
 
-        wd_bf = {}
-        wd_codes = [place(f"wd_codes{b}", [P, N], U32) for b in range(PASSES)]
-        wd_scales = [keep.tile([P, N], U8, name=f"wd_scales{b}", align_bytes=64) for b in range(PASSES)]
+        w_scales = [place(f"w_scales{g}", [P, R], U8) for g in range(2)]
+        w_codes = [place(f"w_codes{g}", [P, 2 * R], U8) for g in range(2)]
 
-        def weave_wd(b, first, count, engine, dst=None):
-            if dst is None:
-                dst = woven(room(f"wd_bf{b}_{first}", 2 * count * P), 0, count * P)
-            wd_bf[b, first] = dst
-            cols = slice(first * P, (first + count) * P)
-            if engine == "gpsimd":
-                nc.gpsimd.tensor_scalar(dst, wd_raw[b][:, :, cols].rearrange("p t n -> p n t"), 1.0, 0.0, MULT, ADD)
-                return
-            dst = dst.rearrange("p (c e) t -> p c t e", e=4)
-            src = wd_raw[b][:, :, cols].rearrange("p t (c e) -> p c t e", e=4)
+        def move(engine, dst, src):
             if engine == "vector":
-                nc.vector.tensor_copy(dst, src)
+                nc.vector.tensor_copy(dst.bitcast(I32), src.bitcast(I32))
             else:
                 nc.scalar.copy(dst, src)
 
-        def quantize_wd(b, first, whole=None):
-            if whole is not None:
-                wd_bf[b, first] = whole
-            cols = slice(first * P, first * P + wd_bf[b, first].shape[1])
+        def order_scales(g, engine):
+            dst = w_scales[g][:].bitcast(U32).rearrange("p (b t s) -> p b t s", t=PACK, s=32)
+            src = scales_raw[g][:].bitcast(U32).rearrange("p (b s t) -> p b t s", t=PACK, s=32)
+            move(engine, dst, src)
+
+        def order_words(g, engine):
+            dst = w_codes[g][:].bitcast(U32).rearrange("p (b t s w) -> p b t s w", t=PACK, s=32, w=2)
+            src = words_raw[g][:].bitcast(U32).rearrange("p (b s t w) -> p b t s w", t=PACK, s=32, w=2)
+            move(engine, dst, src)
+
+        def woven(tile, first, width):
+            return tile[:, first : first + 2 * width].bitcast(BF16).rearrange("p (j i) -> p j i", i=PACK)
+
+        low = place("low", [P, 2 * J], F32)
+        high = place("high", [P, 2 * J + CHUNK], F32)
+
+        def gather(i, start, width):
+            dst = (low, high)[i // 2][:, (i % 2) * J + start : (i % 2) * J + start + width]
+            cols = offsets[:, start // 16 : (start + width) // 16]
+            nc.vector.tensor_tensor(dst, planes[i][:].indirect(cols), weight[:, start : start + width], MULT)
+
+        X_PARTS = ((0, 128, 384), (128, 256, 640), (384, 256, None), (640, 384, None))
+        x_bf = {}
+        x_codes = {}
+        x_scales = {}
+        for part, (start, width, where) in enumerate(X_PARTS):
+            if where is None:
+                x_bf[part] = woven(place(f"x_bf{part}", [P, 2 * width], F32), 0, width)
+            else:
+                x_bf[part] = woven(high, J + where, width)
+
+        def weave_x(part, pair, engine="scalar"):
+            start, width, where = X_PARTS[part]
+            src = (low, high)[pair][:, : 2 * J].rearrange("p (i j) -> p i j", i=2)[:, :, start : start + width]
+            dst = x_bf[part][:, :, 2 * pair : 2 * pair + 2].rearrange("p (c e) i -> p c i e", e=2)
+            copy(engine, dst, src.rearrange("p i (c e) -> p c i e", e=2))
+
+        def quantize_x(part):
+            start, width, where = X_PARTS[part]
+            codes = place(f"x_codes{part}", [P, width], U32)
+            scales = keep.tile([P, width], U8, name=f"x_scales{part}", align_bytes=64)
+            nc.vector.quantize_mx(out=codes[:].bitcast(FP8X4), scales=scales[:], in_=x_bf[part].rearrange("p j i -> p (j i)"))
+            for q in range(len(WIDTHS)):
+                if start <= STARTS[q] < start + width:
+                    cols = slice(STARTS[q] - start, STARTS[q] - start + WIDTHS[q])
+                    x_codes[q] = codes[:, cols]
+                    x_scales[q] = scales[:, cols]
+
+        WD_PARTS = ((0, 3), (3, 1))
+        wd_bf = {}
+        wd_codes = {}
+        wd_scales = {}
+
+        def weave_wd(part, b, engine="gpsimd"):
+            first, count = WD_PARTS[part]
+            if part not in wd_bf:
+                wd_bf[part] = place(f"wd_bf{part}", [P, PASSES * 2 * count * P], F32)
+            dst = woven(wd_bf[part], b * 2 * count * P, count * P)
+            cols = slice(first * P, (first + count) * P)
+            if engine == "gpsimd":
+                copy(engine, dst, wd_raw[b][:, :, cols].rearrange("p t n -> p n t"))
+            else:
+                src = wd_raw[b][:, :, cols].rearrange("p t (c e) -> p c t e", e=4)
+                copy(engine, dst.rearrange("p (c e) t -> p c t e", e=4), src)
+
+        def quantize_wd(part, first=0, passes=PASSES):
+            width = WD_PARTS[part][1] * P
+            if part not in wd_codes:
+                wd_codes[part] = place(f"wd_codes{part}", [P, PASSES * width], U32)
+                wd_scales[part] = keep.tile([P, PASSES * width], U8, name=f"wd_scales{part}", align_bytes=64)
+            cols = slice(first * width, (first + passes) * width)
             nc.vector.quantize_mx(
-                out=wd_codes[b][:, cols].bitcast(FP8X4),
-                scales=wd_scales[b][:, cols],
-                in_=wd_bf[b, first].rearrange("p n t -> p (n t)"),
+                out=wd_codes[part][:, cols].bitcast(FP8X4),
+                scales=wd_scales[part][:, cols],
+                in_=wd_bf[part][:, 2 * cols.start : 2 * cols.stop].bitcast(BF16),
             )
+
+        def wd_tile(m, b):
+            for part, (first, count) in enumerate(WD_PARTS):
+                if first <= m < first + count:
+                    cols = slice((b * count + m - first) * P, (b * count + m - first + 1) * P)
+                    return wd_codes[part][:, cols], wd_scales[part][:, cols]
 
         def first_product(dst, g, b, t, q, cols):
             s = b * PACK + t
@@ -231,198 +210,208 @@ def tile_list_gelu_none_kernel(
             )
 
         act = {}
-        codes_all = {}
-        scales_all = {}
-        h_bf = {}
+        h_all = {}
         h_codes = {}
         h_scales = {}
 
-        def gate(q, b):
+        def gate_chunk(q, b, c):
+            tile = place(f"act{q}_{b}_{c}", [P, PACK, CHUNK], F32)
+            act[q, b, c] = tile[:]
+            bank = next_bank([P, PACK, CHUNK])
+            for t in range(PACK):
+                first_product(bank[:, t, :], 0, b, t, q, slice(c * CHUNK, (c + 1) * CHUNK))
+            nc.scalar.activation(tile[:], bank[:], GELU)
+
+        wide_act = {}
+
+        def gate_half(q, b, half):
+            if half == 0:
+                wide_act[q, b] = place(f"act{q}_{b}", [P, PACK, 2 * CHUNK], F32)
+                for c in range(2):
+                    act[q, b, c] = wide_act[q, b][:, :, c * CHUNK : (c + 1) * CHUNK]
+            bank = next_bank([P, 2, 2 * CHUNK])
+            for t in range(2):
+                first_product(bank[:, t, :], 0, b, 2 * half + t, q, slice(0, 2 * CHUNK))
+            nc.scalar.activation(wide_act[q, b][:, 2 * half : 2 * half + 2, :], bank[:], GELU)
+
+        def gate_wide(q, b):
+            gate_half(q, b, 0)
+            gate_half(q, b, 1)
+
+        def up(q, b, c):
             width = WIDTHS[q]
-            per_bank = BANK // width
-            act[q, b] = place(f"act{q}_{b}", [P, PACK, width], F32)
-            for first in range(0, PACK, per_bank):
-                bank = next_bank("gate", [P, per_bank, width])
-                for t in range(per_bank):
-                    first_product(bank[:, t, :], 0, b, first + t, q, slice(0, width))
-                nc.scalar.activation(act[q, b][:, first : first + per_bank, :], bank[:], GELU)
-
-        def gate_by_chunks(q, b):
-            act[q, b] = place(f"act{q}_{b}", [P, PACK, WIDTHS[q]], F32)
-            for c in range(WIDTHS[q] // CHUNK):
-                cols = slice(c * CHUNK, (c + 1) * CHUNK)
-                bank = next_bank("gate", [P, PACK, CHUNK])
-                for t in range(PACK):
-                    first_product(bank[:, t, :], 0, b, t, q, cols)
-                nc.scalar.activation(act[q, b][:, :, cols], bank[:], GELU)
-
-        def up(q, b, c, slot=None):
-            if (b, c) == (0, 0):
-                width = WIDTHS[q]
-                if q not in h_all:
-                    h_all[q] = room(f"h_bf{q}", PASSES * 2 * width)[:]
-                codes_all[q] = place(slot or f"h_codes{q}", [P, PASSES * width], U32)
-                scales_all[q] = keep.tile([P, PASSES * width], U8, name=f"h_scales{q}", align_bytes=64)
-                for a in range(PASSES):
-                    h_bf[q, a] = woven(h_all[q], a * 2 * width, width)
-                    h_codes[q, a] = codes_all[q][:, a * width : (a + 1) * width]
-                    h_scales[q, a] = scales_all[q][:, a * width : (a + 1) * width]
+            if q not in h_all:
+                h_all[q] = place(f"h_bf{q}", [P, PASSES * 2 * width], F32)
             cols = slice(c * CHUNK, (c + 1) * CHUNK)
-            bank = next_bank("up", [P, PACK, CHUNK])
+            bank = next_bank([P, PACK, CHUNK])
             for t in range(PACK):
                 first_product(bank[:, t, :], 1, b, t, q, cols)
             nc.vector.tensor_tensor(
-                h_bf[q, b][:, cols, :].rearrange("p (c e) t -> p c t e", e=2),
+                woven(h_all[q], b * 2 * width, width)[:, cols, :].rearrange("p (c e) t -> p c t e", e=2),
                 bank[:].rearrange("p t (c e) -> p c t e", e=2),
-                act[q, b][:, :, cols].rearrange("p t (c e) -> p c t e", e=2),
+                act[q, b, c].rearrange("p t (c e) -> p c t e", e=2),
                 MULT,
             )
 
-        def ups(q, b, slot=None):
-            for c in range(WIDTHS[q] // CHUNK):
-                up(q, b, c, slot)
-
-        def quantize_both(q):
+        def quantize_h(q, first=0, count=PASSES):
+            width = WIDTHS[q]
+            if q not in h_codes:
+                h_codes[q] = place(f"h_codes{q}", [P, PASSES * width], U32)
+                h_scales[q] = keep.tile([P, PASSES * width], U8, name=f"h_scales{q}", align_bytes=64)
+            cols = slice(first * width, (first + count) * width)
             nc.vector.quantize_mx(
-                out=codes_all[q][:].bitcast(FP8X4), scales=scales_all[q][:], in_=h_all[q].bitcast(BF16)
-            )
-
-        def span(q, c):
-            return slice(0, WIDTHS[q]) if c is None else slice(c * CHUNK, (c + 1) * CHUNK)
-
-        def quantize_h(q, b, c=None):
-            cols = span(q, c)
-            nc.vector.quantize_mx(
-                out=h_codes[q, b][:, cols].bitcast(FP8X4),
-                scales=h_scales[q, b][:, cols],
-                in_=h_bf[q, b][:, cols, :].rearrange("p j t -> p (j t)"),
+                out=h_codes[q][:, cols].bitcast(FP8X4),
+                scales=h_scales[q][:, cols],
+                in_=h_all[q][:, 2 * cols.start : 2 * cols.stop].bitcast(BF16),
             )
 
         out_rows = out.rearrange("(m p) j -> p m j", p=P)
 
-        def down_pass(acc, m, q, b, cols, start, stop):
-            n_cols = slice(m * P, (m + 1) * P)
+        def down_pass(acc, m, q, b, start, stop):
+            codes, scales = wd_tile(m, b)
+            cols = slice(b * WIDTHS[q], (b + 1) * WIDTHS[q])
             nc.tensor.matmul_mx(
                 out=acc,
-                lhsT=wd_codes[b][:, n_cols].bitcast(FP8X4),
-                lhsT_scale=wd_scales[b][:, n_cols],
-                rhs=h_codes[q, b][:, cols].bitcast(FP8X4),
-                rhs_scale=h_scales[q, b][:, cols],
+                lhsT=codes.bitcast(FP8X4),
+                lhsT_scale=scales,
+                rhs=h_codes[q][:, cols].bitcast(FP8X4),
+                rhs_scale=h_scales[q][:, cols],
                 start=start,
                 stop=stop,
             )
 
-        def store(q, cols, first, count, acc, on_vector, queue):
-            tokens = slice(STARTS[q] + cols.start, STARTS[q] + cols.stop)
-            result = keep.tile([P, count, cols.stop - cols.start], F32, name=f"result{tokens.start}_{first}")
-            if on_vector:
-                nc.vector.tensor_copy(result[:], acc[:])
-            else:
-                nc.scalar.copy(result[:], acc[:])
+        def store(q, first, count, acc, engine, queue):
+            tokens = slice(STARTS[q], STARTS[q] + WIDTHS[q])
+            result = keep.tile([P, count, WIDTHS[q]], F32, name=f"result{q}_{first}")
+            copy(engine, result[:], acc[:])
             queue.dma_start(out_rows[:, first : first + count, tokens], result[:])
 
-        def down(q, c=None, part=None, role="down", on_vector=False):
-            cols = span(q, c)
-            width = cols.stop - cols.start
-            per_bank = BANK // width
-            firsts = list(range(0, N_TILES, per_bank))
-            for first in firsts if part is None else firsts[part : part + 1]:
-                acc = next_bank(role, [P, per_bank, width])
-                for mm in range(per_bank):
-                    for b in range(PASSES):
-                        down_pass(acc[:, mm, :], first + mm, q, b, cols, b == 0, b == PASSES - 1)
-                store(q, cols, first, per_bank, acc, on_vector, nc.sync)
+        def down(q, part=0, engine="scalar"):
+            count = BANK // WIDTHS[q]
+            acc = next_bank([P, count, WIDTHS[q]])
+            for mm in range(count):
+                for b in range(PASSES):
+                    down_pass(acc[:, mm, :], part * count + mm, q, b, b == 0, b == PASSES - 1)
+            store(q, part * count, count, acc, engine, nc.sync)
 
-        accs = {}
-
-        def down_by_pass(q, b, role):
-            if b == 0:
-                accs[q] = [next_bank(role, [P, 2, WIDTHS[q]]) for half in range(2)]
-            for m in range(N_TILES):
-                acc = accs[q][m // 2][:, m % 2, :]
-                down_pass(acc, m, q, b, span(q, None), b == 0 and m % 2 == 0, b == PASSES - 1 and m % 2 == 1)
-
-        last = GROUPS - 1
-        gather(picked_low[:, 0, :128], 0, 0, 128)
-        gather(picked_low[:, 0, 128:256], 0, 128, 128)
-        gather(picked_low[:, 0, 256:512], 0, 256, 256)
-        gather(picked_low[:, 0, 512:], 0, 512, 512)
-        for groups in ((0, 1), (2,), (3, 4)):
-            first = STARTS[groups[0]]
+        def down_tile(m, groups, engine="scalar"):
             width = sum(WIDTHS[q] for q in groups)
-            gather(picked_low[:, 1, first : first + width], 1, first, width)
+            start = STARTS[groups[0]]
+            acc = next_bank([P, width])
             for q in groups:
-                weave_pair(q, 0, picked_low[:, :, STARTS[q] : STARTS[q] + WIDTHS[q]], "scalar")
-        order_scales(0, False)
-        order_scales(1, False)
-        gather(early[:, :AHEAD], 2, 0, AHEAD)
-        gather3(0)
-        weave_x(0)
-        gather3(1)
-        weave_x(1)
-        order_words(0)
+                for b in range(PASSES):
+                    down_pass(acc[:, STARTS[q] - start : STARTS[q] - start + WIDTHS[q]], m, q, b, b == 0, b == PASSES - 1)
+            result = keep.tile([P, width], F32, name=f"result_tile{m}_{groups[0]}")
+            copy(engine, result[:], acc[:])
+            nc.sync.dma_start(out_rows[:, m, start : start + width], result[:])
+
+        accs = []
+
+        def down_last(b):
+            if b == 0:
+                accs.extend(next_bank([P, 2, WIDTHS[E]]) for half in range(2))
+            for m in range(N_TILES):
+                down_pass(accs[m // 2][:, m % 2, :], m, E, b, b == 0 and m % 2 == 0, b == PASSES - 1 and m % 2 == 1)
+
+        nc.sync.dma_start(offsets[:], offs)
+        nc.sync.dma_start(wgt_rows[:], wgt.rearrange("(a e) j -> e a j", e=8)[0])
+        for g in range(2):
+            nc.gpsimd.memset(scales_raw[g][:], 0)
+        nc.vector.memset(warm_in[:], 0.0)
+        nc.scalar.activation(warm_out[:], warm_in[:], GELU)
+        make_identity(nc, identity[:])
+        load_plane(0)
+        load_scales(0)
+        load_plane(1)
+        load_scales(1)
+        load_plane(2)
+        load_plane(3)
+        load_words(0)
+        load_words(1)
+        for b in range(PASSES):
+            for t in range(PACK):
+                load_wd(b, t)
+        turned = turn_rows()
+        for first, count in ((0, 1), (1, 3), (4, 4)):
+            widen(turned, first, count, "vector")
+            turn_back(first, count, "scalar")
+        order_scales(0, "scalar")
+        order_scales(1, "scalar")
+        gather(0, 0, 128)
+        gather(0, 128, 384)
+        gather(0, 512, 512)
+        gather(1, 0, 384)
+        weave_x(0, 0)
+        weave_x(1, 0)
+        gather(1, 384, 640)
+        weave_x(2, 0)
+        weave_x(3, 0)
+        gather(2, 0, J)
+        gather(3, 0, 128)
+        weave_x(0, 1)
+        gather(3, 128, 256)
+        weave_x(1, 1)
+        order_words(0, "vector")
         quantize_x(0)
-        gather3(2)
-        order_words(1)
+        order_words(1, "scalar")
+        gather(3, 384, 256)
+        weave_x(2, 1)
+        gate_chunk(A, 0, 0)
         quantize_x(1)
-        gate(0, 0)
-        weave_x(2)
-        gate(0, 1)
-        gather3(3)
-        gather2(4)
-        gather3(4)
+        gate_chunk(A, 1, 0)
+        gather(3, 640, 384)
         quantize_x(2)
-        gate_by_chunks(1, 0)
-        wd_room = room("wd_room", 2048)
-        weave_wd(0, 0, 4, "gpsimd", woven(wd_room, 0, 512))
-        h_all[0] = room("weight", 512)[:]
-        ups(0, 0)
-        ups(0, 1)
-        gate_by_chunks(1, 1)
-        ups(1, 0)
-        ups(1, 1)
-        weave_x(3)
-        weave_wd(1, 0, 2, "scalar", woven(wd_room, 1024, 256))
+        weave_wd(0, 0)
+        weave_wd(0, 1)
+        gate_chunk(B, 0, 0)
+        up(A, 0, 0)
+        gate_chunk(B, 0, 1)
+        up(A, 1, 0)
+        gate_chunk(B, 1, 0)
+        up(B, 0, 0)
+        gate_chunk(B, 1, 1)
+        up(B, 0, 1)
+        gate_chunk(C, 0, 0)
+        up(B, 1, 0)
+        gate_chunk(C, 0, 1)
+        up(B, 1, 1)
+        weave_x(3, 1)
+        up(C, 0, 0)
+        gate_wide(C, 1)
+        up(C, 0, 1)
+        quantize_h(A)
+        quantize_wd(0, 0, 1)
         quantize_x(3)
-        quantize_wd(0, 0)
-        weave_wd(1, 2, 2, "vector", woven(room("wd_late", 512), 0, 256))
-        quantize_both(0)
-        quantize_wd(1, 0, woven(wd_room, 1024, 256))
-        quantize_wd(1, 2)
-        gate(2, 0)
-        quantize_both(1)
-        gate(2, 1)
-        up(2, 0, 0)
-        weave_x(4)
-        down(0)
-        up(2, 0, 1)
-        gate(3, 0)
-        up(2, 1, 0)
-        down(1, part=0)
-        quantize_h(2, 0)
-        up(2, 1, 1)
-        quantize_x(4)
-        gate(3, 1)
-        up(3, 0, 0)
-        down(1, part=1)
-        quantize_h(2, 1)
-        up(3, 0, 1)
-        gate(4, 0)
-        up(3, 1, 0)
-        down(2, part=0)
-        quantize_h(3, 0)
-        up(3, 1, 1)
-        gate(4, 1)
-        down(2, part=1)
-        quantize_h(3, 1, 0)
-        ups(4, 0)
-        down(3, c=0)
-        quantize_h(3, 1, 1)
-        ups(4, 1)
-        down(3, c=1)
-        quantize_h(4, 0)
-        down_by_pass(last, 0, "gate")
-        quantize_h(last, 1)
-        down_by_pass(last, 1, "gate")
-        store(last, span(last, None), 0, 2, accs[last][0], True, nc.sync)
-        store(last, span(last, None), 2, 2, accs[last][1], False, nc.scalar)
+        quantize_wd(0, 1, 1)
+        quantize_h(B)
+        weave_wd(1, 0)
+        weave_wd(1, 1)
+        gate_wide(D, 0)
+        up(C, 1, 0)
+        up(C, 1, 1)
+        down_tile(0, (A, B))
+        gate_wide(D, 1)
+        up(D, 0, 0)
+        down_tile(1, (A, B))
+        up(D, 0, 1)
+        quantize_wd(1)
+        quantize_h(C)
+        gate_chunk(E, 0, 0)
+        down_tile(2, (A, B))
+        up(D, 1, 0)
+        gate_chunk(E, 1, 0)
+        down_tile(3, (A, B))
+        up(D, 1, 1)
+        down(C, 0)
+        up(E, 0, 0)
+        down(C, 1)
+        quantize_h(D)
+        up(E, 1, 0)
+        quantize_h(E, 0, 1)
+        quantize_h(E, 1, 1)
+        down(D, 0)
+        down(D, 1)
+        down_last(0)
+        down_last(1)
+        store(E, 0, 2, accs[0], "vector", nc.sync)
+        store(E, 2, 2, accs[1], "scalar", nc.scalar)

@@ -39,7 +39,7 @@ def tile_list_gelu_none_kernel(
         laid = ctx.enter_context(tc.tile_pool(name="laid", bufs=1))
         psum = ctx.enter_context(tc.psum_pool(name="psum", bufs=1))
 
-        places = {"plane3": 0, "x_bf2": 8192, "wd_bf0": 4096, "act2_0_0": 12288, "h_codes0": 11328, "x_codes3": 12352, "h_codes1": 13888, "h_bf1": 16384, "wd_bf1": 16384, "w_scales0": 20480, "w_scales1": 21504, "wide4": 20480}
+        places = {"plane3": 0, "x_bf2": 8192, "wd_bf0": 6144, "x_bf3": 10240, "h_bf1": 13312, "wd_bf1": 9728, "act1_1_1": 20480, "h_scales0": 20480, "wd_scales0": 20736, "x_scales3": 21248, "wide4": 40960, "w_scales0": 40960, "low": 45056, "w_scales1": 45056, "h_bf4": 24576, "result_chunk3_1": 24576}
 
         def place(name, shape, dtype):
             if name in places:
@@ -48,16 +48,18 @@ def tile_list_gelu_none_kernel(
 
         turns = []
 
-        def next_bank(shape):
-            turns.append(shape)
-            return psum.tile(shape, F32, name=f"bank{len(turns) % BANKS}")
+        def next_bank(shape, at=None):
+            if at is None:
+                turns.append(shape)
+                at = len(turns) % BANKS
+            return psum.tile(shape, F32, name=f"bank{at}")
 
         offsets = keep.tile([P, J // 16], U16, name="offsets")
         wgt_rows = keep.tile([P, CHUNK], F32, name="wgt_rows")
         scales_raw = [keep.tile([P, R // 4], I32, name=f"scales_raw{g}") for g in range(2)]
         words_raw = [place(f"words_raw{g}", [P, R // 2], I32) for g in range(2)]
         planes = [place(f"plane{i}", [P, T], F32) for i in range(PACK)]
-        wd_raw = [keep.tile([P, PACK, N], F32, name=f"wd_raw{b}") for b in range(PASSES)]
+        wd_raw = keep.tile([P, PASSES, PACK, N], F32, name="wd_raw")
         x_planes = xT.rearrange("(p i) t -> i p t", i=PACK)
         wd_rows = wd.rearrange("(b s t e) n -> b t s (e n)", b=PASSES, t=PACK, e=4)
         warm_in = keep.tile([P, 8], F32, name="warm_in")
@@ -77,7 +79,7 @@ def tile_list_gelu_none_kernel(
             nc.sync.dma_start(planes[i][:], x_planes[i])
 
         def load_wd(b, t):
-            nc.sync.dma_start(wd_raw[b][:, t, :], wd_rows[b, t])
+            nc.sync.dma_start(wd_raw[:, b, t, :], wd_rows[b, t])
 
         def copy(engine, dst, src):
             if engine == "vector":
@@ -154,7 +156,7 @@ def tile_list_gelu_none_kernel(
         def quantize_x(part):
             start, width, where = X_PARTS[part]
             codes = place(f"x_codes{part}", [P, width], U32)
-            scales = keep.tile([P, width], U8, name=f"x_scales{part}", align_bytes=64)
+            scales = place(f"x_scales{part}", [P, width], U8)
             nc.vector.quantize_mx(out=codes[:].bitcast(FP8X4), scales=scales[:], in_=x_bf[part].rearrange("p j i -> p (j i)"))
             for q in range(len(WIDTHS)):
                 if start <= STARTS[q] < start + width:
@@ -162,39 +164,40 @@ def tile_list_gelu_none_kernel(
                     x_codes[q] = codes[:, cols]
                     x_scales[q] = scales[:, cols]
 
-        WD_PARTS = ((0, 3), (3, 1))
+        WD_PARTS = ((0, 2), (2, 2))
         wd_bf = {}
         wd_codes = {}
         wd_scales = {}
 
-        def weave_wd(part, b, engine="gpsimd"):
+        def weave_wd(part, tiles=None, passes=slice(0, PASSES), engine="gpsimd"):
             first, count = WD_PARTS[part]
             if part not in wd_bf:
-                wd_bf[part] = place(f"wd_bf{part}", [P, PASSES * 2 * count * P], F32)
-            dst = woven(wd_bf[part], b * 2 * count * P, count * P)
-            cols = slice(first * P, (first + count) * P)
-            if engine == "gpsimd":
-                copy(engine, dst, wd_raw[b][:, :, cols].rearrange("p t n -> p n t"))
+                wd_bf[part] = place(f"wd_bf{part}", [P, count * PASSES * 2 * P], F32)
+            tiles = tiles or slice(0, count)
+            dst = wd_bf[part][:].bitcast(BF16).rearrange("p (m b n t) -> p m b n t", b=PASSES, n=P, t=PACK)
+            dst = dst[:, tiles, passes, :, :]
+            src = wd_raw[:].rearrange("p b t (m n) -> p m b n t", n=P)[:, first + tiles.start : first + tiles.stop, passes, :, :]
+            if tiles.stop - tiles.start == 1:
+                dst, src = dst[:, 0], src[:, 0]
             else:
-                src = wd_raw[b][:, :, cols].rearrange("p t (c e) -> p c t e", e=4)
-                copy(engine, dst.rearrange("p (c e) t -> p c t e", e=4), src)
+                dst, src = dst[:, :, 0], src[:, :, 0]
+            if engine != "gpsimd":
+                dst = dst.rearrange("p a (c e) t -> p a c t e", e=4)
+                src = src.rearrange("p a (c e) t -> p a c t e", e=4)
+            copy(engine, dst, src)
 
-        def quantize_wd(part, first=0, passes=PASSES):
-            width = WD_PARTS[part][1] * P
-            if part not in wd_codes:
-                wd_codes[part] = place(f"wd_codes{part}", [P, PASSES * width], U32)
-                wd_scales[part] = keep.tile([P, PASSES * width], U8, name=f"wd_scales{part}", align_bytes=64)
-            cols = slice(first * width, (first + passes) * width)
+        def quantize_wd(part):
+            width = WD_PARTS[part][1] * PASSES * P
+            wd_codes[part] = place(f"wd_codes{part}", [P, width], U32)
+            wd_scales[part] = place(f"wd_scales{part}", [P, width], U8)
             nc.vector.quantize_mx(
-                out=wd_codes[part][:, cols].bitcast(FP8X4),
-                scales=wd_scales[part][:, cols],
-                in_=wd_bf[part][:, 2 * cols.start : 2 * cols.stop].bitcast(BF16),
+                out=wd_codes[part][:].bitcast(FP8X4), scales=wd_scales[part][:], in_=wd_bf[part][:].bitcast(BF16)
             )
 
         def wd_tile(m, b):
             for part, (first, count) in enumerate(WD_PARTS):
                 if first <= m < first + count:
-                    cols = slice((b * count + m - first) * P, (b * count + m - first + 1) * P)
+                    cols = slice(((m - first) * PASSES + b) * P, ((m - first) * PASSES + b + 1) * P)
                     return wd_codes[part][:, cols], wd_scales[part][:, cols]
 
         def first_product(dst, g, b, t, q, cols):
@@ -214,22 +217,22 @@ def tile_list_gelu_none_kernel(
         h_codes = {}
         h_scales = {}
 
-        def gate_chunk(q, b, c):
+        def gate_chunk(q, b, c, at=None):
             tile = place(f"act{q}_{b}_{c}", [P, PACK, CHUNK], F32)
             act[q, b, c] = tile[:]
-            bank = next_bank([P, PACK, CHUNK])
+            bank = next_bank([P, PACK, CHUNK], at)
             for t in range(PACK):
                 first_product(bank[:, t, :], 0, b, t, q, slice(c * CHUNK, (c + 1) * CHUNK))
             nc.scalar.activation(tile[:], bank[:], GELU)
 
         wide_act = {}
 
-        def gate_half(q, b, half):
+        def gate_half(q, b, half, at=None):
             if half == 0:
                 wide_act[q, b] = place(f"act{q}_{b}", [P, PACK, 2 * CHUNK], F32)
                 for c in range(2):
                     act[q, b, c] = wide_act[q, b][:, :, c * CHUNK : (c + 1) * CHUNK]
-            bank = next_bank([P, 2, 2 * CHUNK])
+            bank = next_bank([P, 2, 2 * CHUNK], at)
             for t in range(2):
                 first_product(bank[:, t, :], 0, b, 2 * half + t, q, slice(0, 2 * CHUNK))
             nc.scalar.activation(wide_act[q, b][:, 2 * half : 2 * half + 2, :], bank[:], GELU)
@@ -238,12 +241,12 @@ def tile_list_gelu_none_kernel(
             gate_half(q, b, 0)
             gate_half(q, b, 1)
 
-        def up(q, b, c):
+        def up(q, b, c, at=None):
             width = WIDTHS[q]
             if q not in h_all:
                 h_all[q] = place(f"h_bf{q}", [P, PASSES * 2 * width], F32)
             cols = slice(c * CHUNK, (c + 1) * CHUNK)
-            bank = next_bank([P, PACK, CHUNK])
+            bank = next_bank([P, PACK, CHUNK], at)
             for t in range(PACK):
                 first_product(bank[:, t, :], 1, b, t, q, cols)
             nc.vector.tensor_tensor(
@@ -257,13 +260,51 @@ def tile_list_gelu_none_kernel(
             width = WIDTHS[q]
             if q not in h_codes:
                 h_codes[q] = place(f"h_codes{q}", [P, PASSES * width], U32)
-                h_scales[q] = keep.tile([P, PASSES * width], U8, name=f"h_scales{q}", align_bytes=64)
+                h_scales[q] = place(f"h_scales{q}", [P, PASSES * width], U8)
             cols = slice(first * width, (first + count) * width)
             nc.vector.quantize_mx(
                 out=h_codes[q][:, cols].bitcast(FP8X4),
                 scales=h_scales[q][:, cols],
                 in_=h_all[q][:, 2 * cols.start : 2 * cols.stop].bitcast(BF16),
             )
+
+        def up_chunk(q, b, c, at=None):
+            if (q, c) not in h_all:
+                h_all[q, c] = place(f"h_bf{q}_{c}", [P, PASSES * 2 * CHUNK], F32)
+            bank = next_bank([P, PACK, CHUNK], at)
+            for t in range(PACK):
+                first_product(bank[:, t, :], 1, b, t, q, slice(c * CHUNK, (c + 1) * CHUNK))
+            nc.vector.tensor_tensor(
+                woven(h_all[q, c], b * 2 * CHUNK, CHUNK).rearrange("p (c e) t -> p c t e", e=2),
+                bank[:].rearrange("p t (c e) -> p c t e", e=2),
+                act[q, b, c].rearrange("p t (c e) -> p c t e", e=2),
+                MULT,
+            )
+
+        def quantize_chunk(q, c):
+            h_codes[q, c] = place(f"h_codes{q}_{c}", [P, PASSES * CHUNK], U32)
+            h_scales[q, c] = place(f"h_scales{q}_{c}", [P, PASSES * CHUNK], U8)
+            nc.vector.quantize_mx(out=h_codes[q, c][:].bitcast(FP8X4), scales=h_scales[q, c][:], in_=h_all[q, c][:].bitcast(BF16))
+
+        def down_chunk(q, c, engine="scalar", at=None):
+            acc = next_bank([P, N_TILES, CHUNK], at)
+            for m in range(N_TILES):
+                for b in range(PASSES):
+                    codes, scales = wd_tile(m, b)
+                    cols = slice(b * CHUNK, (b + 1) * CHUNK)
+                    nc.tensor.matmul_mx(
+                        out=acc[:, m, :],
+                        lhsT=codes.bitcast(FP8X4),
+                        lhsT_scale=scales,
+                        rhs=h_codes[q, c][:, cols].bitcast(FP8X4),
+                        rhs_scale=h_scales[q, c][:, cols],
+                        start=b == 0,
+                        stop=b == PASSES - 1,
+                    )
+            result = place(f"result_chunk{q}_{c}", [P, N_TILES, CHUNK], F32)
+            copy(engine, result[:], acc[:])
+            start = STARTS[q] + c * CHUNK
+            nc.sync.dma_start(out_rows[:, :, start : start + CHUNK], result[:])
 
         out_rows = out.rearrange("(m p) j -> p m j", p=P)
 
@@ -286,18 +327,18 @@ def tile_list_gelu_none_kernel(
             copy(engine, result[:], acc[:])
             queue.dma_start(out_rows[:, first : first + count, tokens], result[:])
 
-        def down(q, part=0, engine="scalar"):
+        def down(q, part=0, engine="scalar", at=None):
             count = BANK // WIDTHS[q]
-            acc = next_bank([P, count, WIDTHS[q]])
+            acc = next_bank([P, count, WIDTHS[q]], at)
             for mm in range(count):
                 for b in range(PASSES):
                     down_pass(acc[:, mm, :], part * count + mm, q, b, b == 0, b == PASSES - 1)
             store(q, part * count, count, acc, engine, nc.sync)
 
-        def down_tile(m, groups, engine="scalar"):
+        def down_tile(m, groups, engine="scalar", at=None):
             width = sum(WIDTHS[q] for q in groups)
             start = STARTS[groups[0]]
-            acc = next_bank([P, width])
+            acc = next_bank([P, width], at)
             for q in groups:
                 for b in range(PASSES):
                     down_pass(acc[:, STARTS[q] - start : STARTS[q] - start + WIDTHS[q]], m, q, b, b == 0, b == PASSES - 1)
@@ -305,11 +346,42 @@ def tile_list_gelu_none_kernel(
             copy(engine, result[:], acc[:])
             nc.sync.dma_start(out_rows[:, m, start : start + width], result[:])
 
+        held = {}
+
+        def down_by_pass(q, b, engines=("scalar", "scalar"), at=(None, None)):
+            if b == 0:
+                held[q] = [next_bank([P, 2, WIDTHS[q]], at[half]) for half in range(2)]
+            for m in range(N_TILES):
+                down_pass(held[q][m // 2][:, m % 2, :], m, q, b, b == 0 and m % 2 == 0, b == PASSES - 1 and m % 2 == 1)
+                if b == PASSES - 1 and m % 2 == 1:
+                    store(q, m - 1, 2, held[q][m // 2], engines[m // 2], nc.sync)
+
+        def warm_operand():
+            ones = keep.tile([P, PACK * BANK], BF16, name="ones", align_bytes=64)
+            nc.vector.memset(ones[:], 1.0)
+            codes = keep.tile([P, BANK], U32, name="ones_codes", align_bytes=64)
+            scales = keep.tile([P, BANK], U8, name="ones_scales", align_bytes=64)
+            nc.vector.quantize_mx(out=codes[:].bitcast(FP8X4), scales=scales[:], in_=ones[:])
+            return codes, scales
+
+        def warm_up(operand, count, at=None):
+            bank = next_bank([P, BANK], at)
+            for k in range(count):
+                nc.tensor.matmul_mx(
+                    out=bank[:],
+                    lhsT=words_raw[0][:].bitcast(U8)[:, : 2 * P].bitcast(FP4X4),
+                    lhsT_scale=w_scales[0][:, :P],
+                    rhs=operand[0][:].bitcast(FP8X4),
+                    rhs_scale=operand[1][:],
+                    start=True,
+                    stop=True,
+                )
+
         accs = []
 
-        def down_last(b):
+        def down_last(b, at=(None, None)):
             if b == 0:
-                accs.extend(next_bank([P, 2, WIDTHS[E]]) for half in range(2))
+                accs.extend(next_bank([P, 2, WIDTHS[E]], at[half]) for half in range(2))
             for m in range(N_TILES):
                 down_pass(accs[m // 2][:, m % 2, :], m, E, b, b == 0 and m % 2 == 0, b == PASSES - 1 and m % 2 == 1)
 
@@ -321,10 +393,10 @@ def tile_list_gelu_none_kernel(
         nc.scalar.activation(warm_out[:], warm_in[:], GELU)
         make_identity(nc, identity[:])
         load_plane(0)
-        load_scales(0)
         load_plane(1)
-        load_scales(1)
+        load_scales(0)
         load_plane(2)
+        load_scales(1)
         load_plane(3)
         load_words(0)
         load_words(1)
@@ -336,7 +408,6 @@ def tile_list_gelu_none_kernel(
             widen(turned, first, count, "vector")
             turn_back(first, count, "scalar")
         order_scales(0, "scalar")
-        order_scales(1, "scalar")
         gather(0, 0, 128)
         gather(0, 128, 384)
         gather(0, 512, 512)
@@ -346,6 +417,7 @@ def tile_list_gelu_none_kernel(
         gather(1, 384, 640)
         weave_x(2, 0)
         weave_x(3, 0)
+        order_scales(1, "scalar")
         gather(2, 0, J)
         gather(3, 0, 128)
         weave_x(0, 1)
@@ -361,56 +433,56 @@ def tile_list_gelu_none_kernel(
         gate_chunk(A, 1, 0)
         gather(3, 640, 384)
         quantize_x(2)
-        weave_wd(0, 0)
-        weave_wd(0, 1)
-        gate_chunk(B, 0, 0)
+        weave_wd(0, passes=slice(0, 1))
+        weave_wd(0, passes=slice(1, 2))
         up(A, 0, 0)
-        gate_chunk(B, 0, 1)
+        gate_chunk(B, 0, 0)
         up(A, 1, 0)
-        gate_chunk(B, 1, 0)
+        gate_chunk(B, 0, 1)
         up(B, 0, 0)
-        gate_chunk(B, 1, 1)
+        gate_chunk(B, 1, 0)
         up(B, 0, 1)
-        gate_chunk(C, 0, 0)
+        gate_chunk(B, 1, 1)
         up(B, 1, 0)
-        gate_chunk(C, 0, 1)
         up(B, 1, 1)
         weave_x(3, 1)
+        gate_wide(C, 0)
+        quantize_h(A)
+        quantize_wd(0)
+        quantize_x(3)
+        quantize_h(B)
+        weave_wd(1, tiles=slice(0, 1))
         up(C, 0, 0)
         gate_wide(C, 1)
         up(C, 0, 1)
-        quantize_h(A)
-        quantize_wd(0, 0, 1)
-        quantize_x(3)
-        quantize_wd(0, 1, 1)
-        quantize_h(B)
-        weave_wd(1, 0)
-        weave_wd(1, 1)
-        gate_wide(D, 0)
         up(C, 1, 0)
+        weave_wd(1, tiles=slice(1, 2), engine="scalar")
         up(C, 1, 1)
-        down_tile(0, (A, B))
-        gate_wide(D, 1)
-        up(D, 0, 0)
-        down_tile(1, (A, B))
-        up(D, 0, 1)
+        gate_wide(D, 0)
         quantize_wd(1)
         quantize_h(C)
+        gate_chunk(D, 1, 0)
+        up_chunk(D, 0, 0)
+        down_tile(0, (A, B))
+        up_chunk(D, 1, 0)
+        gate_chunk(D, 1, 1)
+        down_tile(1, (A, B))
+        up_chunk(D, 0, 1)
+        quantize_chunk(D, 0)
         gate_chunk(E, 0, 0)
+        up_chunk(D, 1, 1)
         down_tile(2, (A, B))
-        up(D, 1, 0)
         gate_chunk(E, 1, 0)
-        down_tile(3, (A, B))
-        up(D, 1, 1)
-        down(C, 0)
         up(E, 0, 0)
-        down(C, 1)
-        quantize_h(D)
+        down_tile(3, (A, B))
+        quantize_chunk(D, 1)
         up(E, 1, 0)
+        down(C, 0)
+        down(C, 1)
+        down_chunk(D, 0)
         quantize_h(E, 0, 1)
         quantize_h(E, 1, 1)
-        down(D, 0)
-        down(D, 1)
+        down_chunk(D, 1, "vector")
         down_last(0)
         down_last(1)
         store(E, 0, 2, accs[0], "vector", nc.sync)

@@ -147,10 +147,11 @@ def tile_list_gelu_none_kernel(
             else:
                 x_bf[part] = woven(high, J + where, width)
 
-        def weave_x(part, pair, engine="scalar"):
+        def weave_x(part, pair, engine="scalar", skip=0, count=None):
             start, width, where = X_PARTS[part]
-            src = (low, high)[pair][:, : 2 * J].rearrange("p (i j) -> p i j", i=2)[:, :, start : start + width]
-            dst = x_bf[part][:, :, 2 * pair : 2 * pair + 2].rearrange("p (c e) i -> p c i e", e=2)
+            count = count or width - skip
+            src = (low, high)[pair][:, : 2 * J].rearrange("p (i j) -> p i j", i=2)[:, :, start + skip : start + skip + count]
+            dst = x_bf[part][:, skip : skip + count, 2 * pair : 2 * pair + 2].rearrange("p (c e) i -> p c i e", e=2)
             copy(engine, dst, src.rearrange("p i (c e) -> p c i e", e=2))
 
         def quantize_x(part):
@@ -212,18 +213,21 @@ def tile_list_gelu_none_kernel(
                 stop=True,
             )
 
+        IN_HIGH = (B, 1, 0)
         act = {}
         h_all = {}
         h_codes = {}
         h_scales = {}
 
         def gate_chunk(q, b, c, at=None):
-            tile = place(f"act{q}_{b}_{c}", [P, PACK, CHUNK], F32)
-            act[q, b, c] = tile[:]
+            if (q, b, c) == IN_HIGH:
+                act[q, b, c] = high[:, J : J + PACK * CHUNK].rearrange("p (t j) -> p t j", t=PACK)
+            else:
+                act[q, b, c] = place(f"act{q}_{b}_{c}", [P, PACK, CHUNK], F32)[:]
             bank = next_bank([P, PACK, CHUNK], at)
             for t in range(PACK):
                 first_product(bank[:, t, :], 0, b, t, q, slice(c * CHUNK, (c + 1) * CHUNK))
-            nc.scalar.activation(tile[:], bank[:], GELU)
+            nc.scalar.activation(act[q, b, c], bank[:], GELU)
 
         wide_act = {}
 
@@ -357,11 +361,11 @@ def tile_list_gelu_none_kernel(
                     store(q, m - 1, 2, held[q][m // 2], engines[m // 2], nc.sync)
 
         def warm_operand():
-            ones = keep.tile([P, PACK * BANK], BF16, name="ones", align_bytes=64)
+            ones = keep.tile([P, 2 * BANK], F32, name="ones", align_bytes=64)
             nc.vector.memset(ones[:], 1.0)
             codes = keep.tile([P, BANK], U32, name="ones_codes", align_bytes=64)
             scales = keep.tile([P, BANK], U8, name="ones_scales", align_bytes=64)
-            nc.vector.quantize_mx(out=codes[:].bitcast(FP8X4), scales=scales[:], in_=ones[:])
+            nc.vector.quantize_mx(out=codes[:].bitcast(FP8X4), scales=scales[:], in_=ones[:].bitcast(BF16))
             return codes, scales
 
         def warm_up(operand, count, at=None):
@@ -385,14 +389,15 @@ def tile_list_gelu_none_kernel(
             for m in range(N_TILES):
                 down_pass(accs[m // 2][:, m % 2, :], m, E, b, b == 0 and m % 2 == 0, b == PASSES - 1 and m % 2 == 1)
 
-        nc.sync.dma_start(offsets[:], offs)
         nc.sync.dma_start(wgt_rows[:], wgt.rearrange("(a e) j -> e a j", e=8)[0])
         for g in range(2):
             nc.gpsimd.memset(scales_raw[g][:], 0)
         nc.vector.memset(warm_in[:], 0.0)
         nc.scalar.activation(warm_out[:], warm_in[:], GELU)
         make_identity(nc, identity[:])
+        ones = warm_operand()
         load_plane(0)
+        nc.sync.dma_start(offsets[:], offs)
         load_plane(1)
         load_scales(0)
         load_plane(2)
@@ -419,6 +424,7 @@ def tile_list_gelu_none_kernel(
         weave_x(3, 0)
         order_scales(1, "scalar")
         gather(2, 0, J)
+        warm_up(ones, 3, 7)
         gather(3, 0, 128)
         weave_x(0, 1)
         gather(3, 128, 256)
@@ -427,9 +433,10 @@ def tile_list_gelu_none_kernel(
         quantize_x(0)
         order_words(1, "scalar")
         gather(3, 384, 256)
-        weave_x(2, 1)
+        weave_x(2, 1, count=128)
         gate_chunk(A, 0, 0)
         quantize_x(1)
+        weave_x(2, 1, "vector", skip=128)
         gate_chunk(A, 1, 0)
         gather(3, 640, 384)
         quantize_x(2)
@@ -462,27 +469,27 @@ def tile_list_gelu_none_kernel(
         quantize_wd(1)
         quantize_h(C)
         gate_chunk(D, 1, 0)
-        up_chunk(D, 0, 0)
         down_tile(0, (A, B))
-        up_chunk(D, 1, 0)
+        up_chunk(D, 0, 0)
         gate_chunk(D, 1, 1)
         down_tile(1, (A, B))
-        up_chunk(D, 0, 1)
-        quantize_chunk(D, 0)
+        up_chunk(D, 1, 0)
         gate_chunk(E, 0, 0)
-        up_chunk(D, 1, 1)
+        up_chunk(D, 0, 1)
         down_tile(2, (A, B))
+        quantize_chunk(D, 0)
+        up_chunk(D, 1, 1)
         gate_chunk(E, 1, 0)
-        up(E, 0, 0)
         down_tile(3, (A, B))
+        up(E, 0, 0)
+        down(C, 0)
         quantize_chunk(D, 1)
         up(E, 1, 0)
-        down(C, 0)
         down(C, 1)
         down_chunk(D, 0)
         quantize_h(E, 0, 1)
         quantize_h(E, 1, 1)
-        down_chunk(D, 1, "vector")
+        down_chunk(D, 1)
         down_last(0)
         down_last(1)
         store(E, 0, 2, accs[0], "vector", nc.sync)

@@ -39,7 +39,7 @@ def tile_list_gelu_none_kernel(
         laid = ctx.enter_context(tc.tile_pool(name="laid", bufs=1))
         psum = ctx.enter_context(tc.psum_pool(name="psum", bufs=1))
 
-        places = {"plane3": 0, "x_bf2": 8192, "wd_bf0": 6144, "x_bf3": 10240, "h_bf1": 13312, "wd_bf1": 9728, "act1_1_1": 20480, "h_scales0": 20480, "wd_scales0": 20736, "x_scales3": 21248, "wide4": 40960, "w_scales0": 40960, "low": 45056, "w_scales1": 45056, "h_bf4": 24576, "result_chunk3_1": 24576}
+        places = {"act1_1_1": 20480, "h_scales0": 20480, "wd_scales0": 20736, "x_scales3": 21248, "wide4": 40960, "w_scales0": 40960, "low": 45056, "w_scales1": 45056, "act2_1": 28672, "wd_scales1": 28672, "h_scales2": 29184}
 
         def place(name, shape, dtype):
             if name in places:
@@ -138,11 +138,15 @@ def tile_list_gelu_none_kernel(
             nc.vector.tensor_tensor(dst, planes[i][:].indirect(cols), weight[:, start : start + width], MULT)
 
         X_PARTS = ((0, 128, 384), (128, 256, 640), (384, 256, None), (640, 384, None))
+        room = place("room", [P, 2048], F32)
+        IN_ROOM = {2: 768, 3: 0}
         x_bf = {}
         x_codes = {}
         x_scales = {}
         for part, (start, width, where) in enumerate(X_PARTS):
-            if where is None:
+            if part in IN_ROOM:
+                x_bf[part] = woven(room, IN_ROOM[part], width)
+            elif where is None:
                 x_bf[part] = woven(place(f"x_bf{part}", [P, 2 * width], F32), 0, width)
             else:
                 x_bf[part] = woven(high, J + where, width)
@@ -165,41 +169,30 @@ def tile_list_gelu_none_kernel(
                     x_codes[q] = codes[:, cols]
                     x_scales[q] = scales[:, cols]
 
-        WD_PARTS = ((0, 2), (2, 2))
-        wd_bf = {}
+        WD_AT = {(0, 0): 1024, (1, 0): 1280, (0, 1): 1536, (1, 1): 1792, (2, 1): 0, (3, 1): 256, (3, 0): 512, (2, 0): 768}
         wd_codes = {}
         wd_scales = {}
 
-        def weave_wd(part, tiles=None, passes=slice(0, PASSES), engine="gpsimd"):
-            first, count = WD_PARTS[part]
-            if part not in wd_bf:
-                wd_bf[part] = place(f"wd_bf{part}", [P, count * PASSES * 2 * P], F32)
-            tiles = tiles or slice(0, count)
-            dst = wd_bf[part][:].bitcast(BF16).rearrange("p (m b n t) -> p m b n t", b=PASSES, n=P, t=PACK)
-            dst = dst[:, tiles, passes, :, :]
-            src = wd_raw[:].rearrange("p b t (m n) -> p m b n t", n=P)[:, first + tiles.start : first + tiles.stop, passes, :, :]
-            if tiles.stop - tiles.start == 1:
-                dst, src = dst[:, 0], src[:, 0]
+        def weave_wd(m, b, tiles, engine="gpsimd"):
+            dst = woven(room, WD_AT[m, b], tiles * P)
+            src = wd_raw[:, b, :, m * P : (m + tiles) * P]
+            run = 2 if engine == "gpsimd" else 4
+            if run == 1:
+                copy(engine, dst, src.rearrange("p t n -> p n t"))
             else:
-                dst, src = dst[:, :, 0], src[:, :, 0]
-            if engine != "gpsimd":
-                dst = dst.rearrange("p a (c e) t -> p a c t e", e=4)
-                src = src.rearrange("p a (c e) t -> p a c t e", e=4)
-            copy(engine, dst, src)
+                copy(engine, dst.rearrange("p (c e) t -> p c t e", e=run), src.rearrange("p t (c e) -> p c t e", e=run))
 
-        def quantize_wd(part):
-            width = WD_PARTS[part][1] * PASSES * P
-            wd_codes[part] = place(f"wd_codes{part}", [P, width], U32)
-            wd_scales[part] = place(f"wd_scales{part}", [P, width], U8)
+        def quantize_wd(half):
+            wd_codes[half] = place(f"wd_codes{half}", [P, 4 * P], U32)
+            wd_scales[half] = place(f"wd_scales{half}", [P, 4 * P], U8)
+            first = 1024 * (1 - half)
             nc.vector.quantize_mx(
-                out=wd_codes[part][:].bitcast(FP8X4), scales=wd_scales[part][:], in_=wd_bf[part][:].bitcast(BF16)
+                out=wd_codes[half][:].bitcast(FP8X4), scales=wd_scales[half][:], in_=room[:, first : first + 1024].bitcast(BF16)
             )
 
         def wd_tile(m, b):
-            for part, (first, count) in enumerate(WD_PARTS):
-                if first <= m < first + count:
-                    cols = slice(((m - first) * PASSES + b) * P, ((m - first) * PASSES + b + 1) * P)
-                    return wd_codes[part][:, cols], wd_scales[part][:, cols]
+            first = WD_AT[m, b] % 1024 // 2
+            return wd_codes[m // 2][:, first : first + P], wd_scales[m // 2][:, first : first + P]
 
         def first_product(dst, g, b, t, q, cols):
             s = b * PACK + t
@@ -440,8 +433,9 @@ def tile_list_gelu_none_kernel(
         gate_chunk(A, 1, 0)
         gather(3, 640, 384)
         quantize_x(2)
-        weave_wd(0, passes=slice(0, 1))
-        weave_wd(0, passes=slice(1, 2))
+        weave_wd(0, 0, 2)
+        weave_wd(2, 0, 1)
+        weave_wd(0, 1, 2)
         up(A, 0, 0)
         gate_chunk(B, 0, 0)
         up(A, 1, 0)
@@ -456,30 +450,30 @@ def tile_list_gelu_none_kernel(
         gate_wide(C, 0)
         quantize_h(A)
         quantize_wd(0)
-        quantize_x(3)
         quantize_h(B)
-        weave_wd(1, tiles=slice(0, 1))
+        quantize_x(3)
+        weave_wd(2, 1, 2)
+        weave_wd(3, 0, 1)
         up(C, 0, 0)
         gate_wide(C, 1)
         up(C, 0, 1)
         up(C, 1, 0)
-        weave_wd(1, tiles=slice(1, 2), engine="scalar")
         up(C, 1, 1)
         gate_wide(D, 0)
+        up_chunk(D, 0, 0)
         quantize_wd(1)
         quantize_h(C)
-        gate_chunk(D, 1, 0)
         down_tile(0, (A, B))
-        up_chunk(D, 0, 0)
-        gate_chunk(D, 1, 1)
+        gate_chunk(D, 1, 0)
         down_tile(1, (A, B))
+        gate_chunk(D, 1, 1)
         up_chunk(D, 1, 0)
         gate_chunk(E, 0, 0)
         up_chunk(D, 0, 1)
         down_tile(2, (A, B))
         quantize_chunk(D, 0)
-        up_chunk(D, 1, 1)
         gate_chunk(E, 1, 0)
+        up_chunk(D, 1, 1)
         down_tile(3, (A, B))
         up(E, 0, 0)
         down(C, 0)

@@ -388,7 +388,6 @@ def tile_list_gelu_none_kernel(
         nc.vector.memset(warm_in[:], 0.0)
         nc.scalar.activation(warm_out[:], warm_in[:], GELU)
         make_identity(nc, identity[:])
-        ones = warm_operand()
         load_plane(0)
         nc.sync.dma_start(offsets[:], offs)
         load_plane(1)
@@ -417,7 +416,6 @@ def tile_list_gelu_none_kernel(
         weave_x(3, 0)
         order_scales(1, "scalar")
         gather(2, 0, J)
-        warm_up(ones, 3, 7)
         gather(3, 0, 128)
         weave_x(0, 1)
         gather(3, 128, 256)

from contextlib import ExitStack

import concourse.mybir as mybir
from concourse.masks import make_identity

K, R, N, T, J = 512, 1024, 512, 2048, 1024
FLOPS = 2 * K * R * J * 2 + 2 * R * N * J

F32 = mybir.dt.float32
BF16 = mybir.dt.bfloat16
I32 = mybir.dt.int32
U32 = mybir.dt.uint32
U16 = mybir.dt.uint16
U8 = mybir.dt.uint8
FP8X4 = mybir.dt.float8_e4m3fn_x4
FP4X4 = mybir.dt.float4_e2m1fn_x4
MULT = mybir.AluOpType.mult
ADD = mybir.AluOpType.add
GELU = mybir.ActivationFunctionType.Gelu_apprx_tanh

P = 128
PACK = 4
PASSES = R // (P * PACK)
BANK = 512
BANKS = 8
CHUNK = 128
N_TILES = N // P
WIDTHS = (128, 256, 256, 256, 128)
STARTS = tuple(sum(WIDTHS[:q]) for q in range(len(WIDTHS)))
A, B, C, D, E = range(len(WIDTHS))


def tile_list_gelu_none_kernel(
    tc, xT, wgt, wg_words, wg_scales, wu_words, wu_scales, wd, offs, out
):
    nc = tc.nc
    with ExitStack() as ctx:
        keep = ctx.enter_context(tc.tile_pool(name="keep", bufs=1))
        laid = ctx.enter_context(tc.tile_pool(name="laid", bufs=1))
        psum = ctx.enter_context(tc.psum_pool(name="psum", bufs=1))

        places = {"act1_1_1": 20480, "h_scales0": 20480, "wd_scales0": 20736, "x_scales3": 21248, "wide4": 40960, "w_scales0": 40960, "low": 45056, "w_scales1": 45056, "act2_1": 28672, "wd_scales1": 28672, "h_scales2": 29184}

        def place(name, shape, dtype):
            if name in places:
                return laid.tile(shape, dtype, name=name, align_bytes=64, offset=places[name])
            return keep.tile(shape, dtype, name=name, align_bytes=64)

        turns = []

        def next_bank(shape, at=None):
            if at is None:
                turns.append(shape)
                at = len(turns) % BANKS
            return psum.tile(shape, F32, name=f"bank{at}")

        offsets = keep.tile([P, J // 16], U16, name="offsets")
        wgt_rows = keep.tile([P, CHUNK], F32, name="wgt_rows")
        scales_raw = [keep.tile([P, R // 4], I32, name=f"scales_raw{g}") for g in range(2)]
        words_raw = [place(f"words_raw{g}", [P, R // 2], I32) for g in range(2)]
        planes = [place(f"plane{i}", [P, T], F32) for i in range(PACK)]
        wd_raw = keep.tile([P, PASSES, PACK, N], F32, name="wd_raw")
        x_planes = xT.rearrange("(p i) t -> i p t", i=PACK)
        wd_rows = wd.rearrange("(b s t e) n -> b t s (e n)", b=PASSES, t=PACK, e=4)
        warm_in = keep.tile([P, 8], F32, name="warm_in")
        warm_out = keep.tile([P, 8], F32, name="warm_out")
        identity = keep.tile([P, P], F32, name="identity")
        weight = place("weight", [P, J], F32)

        def load_scales(g):
            rows = (wg_scales, wu_scales)[g][0].bitcast(I32).rearrange("(q r) n -> r q n", r=4)
            for r in range(4):
                nc.sync.dma_start(scales_raw[g][r:P:32, :], rows[r])

        def load_words(g):
            nc.sync.dma_start(words_raw[g][:], (wg_words, wu_words)[g][0].bitcast(I32))

        def load_plane(i):
            nc.sync.dma_start(planes[i][:], x_planes[i])

        def load_wd(b, t):
            nc.sync.dma_start(wd_raw[:, b, t, :], wd_rows[b, t])

        def copy(engine, dst, src):
            if engine == "vector":
                nc.vector.tensor_copy(dst, src)
            elif engine == "scalar":
                nc.scalar.copy(dst, src)
            else:
                nc.gpsimd.tensor_scalar(dst, src, 1.0, 0.0, MULT, ADD)

        def turn_rows():
            turned = next_bank([P, P])
            nc.tensor.transpose(turned[:], wgt_rows[:], identity[:])
            return turned

        wide = {}

        def widen(turned, first, count, engine):
            wide[first] = place(f"wide{first}", [P, count, 16, 8], F32)
            src = turned[:].rearrange("e (a c) -> e c a", c=8)[:, first : first + count, :]
            copy(engine, wide[first][:], src.unsqueeze(3).to_broadcast([P, count, 16, 8]))

        def turn_back(first, count, engine):
            back = next_bank([P, count, CHUNK])
            for c in range(count):
                nc.tensor.transpose(back[:, c, :], wide[first][:, c, :, :].rearrange("e a q -> e (a q)"), identity[:])
            copy(engine, weight[:, first * CHUNK : (first + count) * CHUNK], back[:].rearrange("p c e -> p (c e)"))

        w_scales = [place(f"w_scales{g}", [P, R], U8) for g in range(2)]
        w_codes = [place(f"w_codes{g}", [P, 2 * R], U8) for g in range(2)]

        def move(engine, dst, src):
            if engine == "vector":
                nc.vector.tensor_copy(dst.bitcast(I32), src.bitcast(I32))
            else:
                nc.scalar.copy(dst, src)

        def order_scales(g, engine):
            dst = w_scales[g][:].bitcast(U32).rearrange("p (b t s) -> p b t s", t=PACK, s=32)
            src = scales_raw[g][:].bitcast(U32).rearrange("p (b s t) -> p b t s", t=PACK, s=32)
            move(engine, dst, src)

        def order_words(g, engine):
            dst = w_codes[g][:].bitcast(U32).rearrange("p (b t s w) -> p b t s w", t=PACK, s=32, w=2)
            src = words_raw[g][:].bitcast(U32).rearrange("p (b s t w) -> p b t s w", t=PACK, s=32, w=2)
            move(engine, dst, src)

        def woven(tile, first, width):
            return tile[:, first : first + 2 * width].bitcast(BF16).rearrange("p (j i) -> p j i", i=PACK)

        low = place("low", [P, 2 * J], F32)
        high = place("high", [P, 2 * J + CHUNK], F32)

        def gather(i, start, width):
            dst = (low, high)[i // 2][:, (i % 2) * J + start : (i % 2) * J + start + width]
            cols = offsets[:, start // 16 : (start + width) // 16]
            nc.vector.tensor_tensor(dst, planes[i][:].indirect(cols), weight[:, start : start + width], MULT)

        X_PARTS = ((0, 128, 384), (128, 256, 640), (384, 256, None), (640, 384, None))
        room = place("room", [P, 2048], F32)
        IN_ROOM = {2: 768, 3: 0}
        x_bf = {}
        x_codes = {}
        x_scales = {}
        for part, (start, width, where) in enumerate(X_PARTS):
            if part in IN_ROOM:
                x_bf[part] = woven(room, IN_ROOM[part], width)
            elif where is None:
                x_bf[part] = woven(place(f"x_bf{part}", [P, 2 * width], F32), 0, width)
            else:
                x_bf[part] = woven(high, J + where, width)

        def weave_x(part, pair, engine="scalar", skip=0, count=None):
            start, width, where = X_PARTS[part]
            count = count or width - skip
            src = (low, high)[pair][:, : 2 * J].rearrange("p (i j) -> p i j", i=2)[:, :, start + skip : start + skip + count]
            dst = x_bf[part][:, skip : skip + count, 2 * pair : 2 * pair + 2].rearrange("p (c e) i -> p c i e", e=2)
            copy(engine, dst, src.rearrange("p i (c e) -> p c i e", e=2))

        def quantize_x(part):
            start, width, where = X_PARTS[part]
            codes = place(f"x_codes{part}", [P, width], U32)
            scales = place(f"x_scales{part}", [P, width], U8)
            nc.vector.quantize_mx(out=codes[:].bitcast(FP8X4), scales=scales[:], in_=x_bf[part].rearrange("p j i -> p (j i)"))
            for q in range(len(WIDTHS)):
                if start <= STARTS[q] < start + width:
                    cols = slice(STARTS[q] - start, STARTS[q] - start + WIDTHS[q])
                    x_codes[q] = codes[:, cols]
                    x_scales[q] = scales[:, cols]

        WD_AT = {(0, 0): 1024, (1, 0): 1280, (0, 1): 1536, (1, 1): 1792, (2, 1): 0, (3, 1): 256, (3, 0): 512, (2, 0): 768}
        wd_codes = {}
        wd_scales = {}

        def weave_wd(m, b, tiles, engine="gpsimd"):
            dst = woven(room, WD_AT[m, b], tiles * P)
            src = wd_raw[:, b, :, m * P : (m + tiles) * P]
            run = 2 if engine == "gpsimd" else 4
            if run == 1:
                copy(engine, dst, src.rearrange("p t n -> p n t"))
            else:
                copy(engine, dst.rearrange("p (c e) t -> p c t e", e=run), src.rearrange("p t (c e) -> p c t e", e=run))

        def quantize_wd(half):
            wd_codes[half] = place(f"wd_codes{half}", [P, 4 * P], U32)
            wd_scales[half] = place(f"wd_scales{half}", [P, 4 * P], U8)
            first = 1024 * (1 - half)
            nc.vector.quantize_mx(
                out=wd_codes[half][:].bitcast(FP8X4), scales=wd_scales[half][:], in_=room[:, first : first + 1024].bitcast(BF16)
            )

        def wd_tile(m, b):
            first = WD_AT[m, b] % 1024 // 2
            return wd_codes[m // 2][:, first : first + P], wd_scales[m // 2][:, first : first + P]

        def first_product(dst, g, b, t, q, cols):
            s = b * PACK + t
            nc.tensor.matmul_mx(
                out=dst,
                lhsT=w_codes[g][:, 2 * P * s : 2 * P * (s + 1)].bitcast(FP4X4),
                lhsT_scale=w_scales[g][:, P * s : P * (s + 1)],
                rhs=x_codes[q][:, cols].bitcast(FP8X4),
                rhs_scale=x_scales[q][:, cols],
                start=True,
                stop=True,
            )

        IN_HIGH = (B, 1, 0)
        act = {}
        h_all = {}
        h_codes = {}
        h_scales = {}

        def gate_chunk(q, b, c, at=None):
            if (q, b, c) == IN_HIGH:
                act[q, b, c] = high[:, J : J + PACK * CHUNK].rearrange("p (t j) -> p t j", t=PACK)
            else:
                act[q, b, c] = place(f"act{q}_{b}_{c}", [P, PACK, CHUNK], F32)[:]
            bank = next_bank([P, PACK, CHUNK], at)
            for t in range(PACK):
                first_product(bank[:, t, :], 0, b, t, q, slice(c * CHUNK, (c + 1) * CHUNK))
            nc.scalar.activation(act[q, b, c], bank[:], GELU)

        wide_act = {}

        def gate_half(q, b, half, at=None):
            if half == 0:
                wide_act[q, b] = place(f"act{q}_{b}", [P, PACK, 2 * CHUNK], F32)
                for c in range(2):
                    act[q, b, c] = wide_act[q, b][:, :, c * CHUNK : (c + 1) * CHUNK]
            bank = next_bank([P, 2, 2 * CHUNK], at)
            for t in range(2):
                first_product(bank[:, t, :], 0, b, 2 * half + t, q, slice(0, 2 * CHUNK))
            nc.scalar.activation(wide_act[q, b][:, 2 * half : 2 * half + 2, :], bank[:], GELU)

        def gate_wide(q, b):
            gate_half(q, b, 0)
            gate_half(q, b, 1)

        def up(q, b, c, at=None):
            width = WIDTHS[q]
            if q not in h_all:
                h_all[q] = place(f"h_bf{q}", [P, PASSES * 2 * width], F32)
            cols = slice(c * CHUNK, (c + 1) * CHUNK)
            bank = next_bank([P, PACK, CHUNK], at)
            for t in range(PACK):
                first_product(bank[:, t, :], 1, b, t, q, cols)
            nc.vector.tensor_tensor(
                woven(h_all[q], b * 2 * width, width)[:, cols, :].rearrange("p (c e) t -> p c t e", e=2),
                bank[:].rearrange("p t (c e) -> p c t e", e=2),
                act[q, b, c].rearrange("p t (c e) -> p c t e", e=2),
                MULT,
            )

        def quantize_h(q, first=0, count=PASSES):
            width = WIDTHS[q]
            if q not in h_codes:
                h_codes[q] = place(f"h_codes{q}", [P, PASSES * width], U32)
                h_scales[q] = place(f"h_scales{q}", [P, PASSES * width], U8)
            cols = slice(first * width, (first + count) * width)
            nc.vector.quantize_mx(
                out=h_codes[q][:, cols].bitcast(FP8X4),
                scales=h_scales[q][:, cols],
                in_=h_all[q][:, 2 * cols.start : 2 * cols.stop].bitcast(BF16),
            )

        def up_chunk(q, b, c, at=None):
            if (q, c) not in h_all:
                h_all[q, c] = place(f"h_bf{q}_{c}", [P, PASSES * 2 * CHUNK], F32)
            bank = next_bank([P, PACK, CHUNK], at)
            for t in range(PACK):
                first_product(bank[:, t, :], 1, b, t, q, slice(c * CHUNK, (c + 1) * CHUNK))
            nc.vector.tensor_tensor(
                woven(h_all[q, c], b * 2 * CHUNK, CHUNK).rearrange("p (c e) t -> p c t e", e=2),
                bank[:].rearrange("p t (c e) -> p c t e", e=2),
                act[q, b, c].rearrange("p t (c e) -> p c t e", e=2),
                MULT,
            )

        def quantize_chunk(q, c):
            h_codes[q, c] = place(f"h_codes{q}_{c}", [P, PASSES * CHUNK], U32)
            h_scales[q, c] = place(f"h_scales{q}_{c}", [P, PASSES * CHUNK], U8)
            nc.vector.quantize_mx(out=h_codes[q, c][:].bitcast(FP8X4), scales=h_scales[q, c][:], in_=h_all[q, c][:].bitcast(BF16))

        def down_chunk(q, c, engine="scalar", at=None):
            acc = next_bank([P, N_TILES, CHUNK], at)
            for m in range(N_TILES):
                for b in range(PASSES):
                    codes, scales = wd_tile(m, b)
                    cols = slice(b * CHUNK, (b + 1) * CHUNK)
                    nc.tensor.matmul_mx(
                        out=acc[:, m, :],
                        lhsT=codes.bitcast(FP8X4),
                        lhsT_scale=scales,
                        rhs=h_codes[q, c][:, cols].bitcast(FP8X4),
                        rhs_scale=h_scales[q, c][:, cols],
                        start=b == 0,
                        stop=b == PASSES - 1,
                    )
            result = place(f"result_chunk{q}_{c}", [P, N_TILES, CHUNK], F32)
            copy(engine, result[:], acc[:])
            start = STARTS[q] + c * CHUNK
            nc.sync.dma_start(out_rows[:, :, start : start + CHUNK], result[:])

        out_rows = out.rearrange("(m p) j -> p m j", p=P)

        def down_pass(acc, m, q, b, start, stop):
            codes, scales = wd_tile(m, b)
            cols = slice(b * WIDTHS[q], (b + 1) * WIDTHS[q])
            nc.tensor.matmul_mx(
                out=acc,
                lhsT=codes.bitcast(FP8X4),
                lhsT_scale=scales,
                rhs=h_codes[q][:, cols].bitcast(FP8X4),
                rhs_scale=h_scales[q][:, cols],
                start=start,
                stop=stop,
            )

        def store(q, first, count, acc, engine, queue):
            tokens = slice(STARTS[q], STARTS[q] + WIDTHS[q])
            result = keep.tile([P, count, WIDTHS[q]], F32, name=f"result{q}_{first}")
            copy(engine, result[:], acc[:])
            queue.dma_start(out_rows[:, first : first + count, tokens], result[:])

        def down(q, part=0, engine="scalar", at=None):
            count = BANK // WIDTHS[q]
            acc = next_bank([P, count, WIDTHS[q]], at)
            for mm in range(count):
                for b in range(PASSES):
                    down_pass(acc[:, mm, :], part * count + mm, q, b, b == 0, b == PASSES - 1)
            store(q, part * count, count, acc, engine, nc.sync)

        def down_tile(m, groups, engine="scalar", at=None):
            width = sum(WIDTHS[q] for q in groups)
            start = STARTS[groups[0]]
            acc = next_bank([P, width], at)
            for q in groups:
                for b in range(PASSES):
                    down_pass(acc[:, STARTS[q] - start : STARTS[q] - start + WIDTHS[q]], m, q, b, b == 0, b == PASSES - 1)
            result = keep.tile([P, width], F32, name=f"result_tile{m}_{groups[0]}")
            copy(engine, result[:], acc[:])
            nc.sync.dma_start(out_rows[:, m, start : start + width], result[:])

        held = {}

        def down_by_pass(q, b, engines=("scalar", "scalar"), at=(None, None)):
            if b == 0:
                held[q] = [next_bank([P, 2, WIDTHS[q]], at[half]) for half in range(2)]
            for m in range(N_TILES):
                down_pass(held[q][m // 2][:, m % 2, :], m, q, b, b == 0 and m % 2 == 0, b == PASSES - 1 and m % 2 == 1)
                if b == PASSES - 1 and m % 2 == 1:
                    store(q, m - 1, 2, held[q][m // 2], engines[m // 2], nc.sync)

        def warm_operand():
            ones = keep.tile([P, 2 * BANK], F32, name="ones", align_bytes=64)
            nc.vector.memset(ones[:], 1.0)
            codes = keep.tile([P, BANK], U32, name="ones_codes", align_bytes=64)
            scales = keep.tile([P, BANK], U8, name="ones_scales", align_bytes=64)
            nc.vector.quantize_mx(out=codes[:].bitcast(FP8X4), scales=scales[:], in_=ones[:].bitcast(BF16))
            return codes, scales

        def warm_up(operand, count, at=None):
            bank = next_bank([P, BANK], at)
            for k in range(count):
                nc.tensor.matmul_mx(
                    out=bank[:],
                    lhsT=words_raw[0][:].bitcast(U8)[:, : 2 * P].bitcast(FP4X4),
                    lhsT_scale=w_scales[0][:, :P],
                    rhs=operand[0][:].bitcast(FP8X4),
                    rhs_scale=operand[1][:],
                    start=True,
                    stop=True,
                )

        accs = []

        def down_last(b, at=(None, None)):
            if b == 0:
                accs.extend(next_bank([P, 2, WIDTHS[E]], at[half]) for half in range(2))
            for m in range(N_TILES):
                down_pass(accs[m // 2][:, m % 2, :], m, E, b, b == 0 and m % 2 == 0, b == PASSES - 1 and m % 2 == 1)

        nc.sync.dma_start(wgt_rows[:], wgt.rearrange("(a e) j -> e a j", e=8)[0])
        for g in range(2):
            nc.gpsimd.memset(scales_raw[g][:], 0)
        nc.vector.memset(warm_in[:], 0.0)
        nc.scalar.activation(warm_out[:], warm_in[:], GELU)
        make_identity(nc, identity[:])
        load_plane(0)
        nc.sync.dma_start(offsets[:], offs)
        load_plane(1)
        load_scales(0)
        load_plane(2)
        load_scales(1)
        load_plane(3)
        load_words(0)
        load_words(1)
        for b in range(PASSES):
            for t in range(PACK):
                load_wd(b, t)
        turned = turn_rows()
        for first, count in ((0, 1), (1, 3), (4, 4)):
            widen(turned, first, count, "vector")
            turn_back(first, count, "scalar")
        order_scales(0, "scalar")
        gather(0, 0, 128)
        gather(0, 128, 384)
        gather(0, 512, 512)
        gather(1, 0, 384)
        weave_x(0, 0)
        weave_x(1, 0)
        gather(1, 384, 640)
        weave_x(2, 0)
        weave_x(3, 0)
        order_scales(1, "scalar")
        gather(2, 0, J)
        gather(3, 0, 128)
        weave_x(0, 1)
        gather(3, 128, 256)
        weave_x(1, 1)
        order_words(0, "vector")
        quantize_x(0)
        order_words(1, "scalar")
        gather(3, 384, 256)
        weave_x(2, 1, count=128)
        gate_chunk(A, 0, 0)
        quantize_x(1)
        weave_x(2, 1, "vector", skip=128)
        gate_chunk(A, 1, 0)
        gather(3, 640, 384)
        quantize_x(2)
        weave_wd(0, 0, 2)
        weave_wd(2, 0, 1)
        weave_wd(0, 1, 2)
        up(A, 0, 0)
        gate_chunk(B, 0, 0)
        up(A, 1, 0)
        gate_chunk(B, 0, 1)
        up(B, 0, 0)
        gate_chunk(B, 1, 0)
        up(B, 0, 1)
        gate_chunk(B, 1, 1)
        up(B, 1, 0)
        up(B, 1, 1)
        weave_x(3, 1)
        gate_wide(C, 0)
        quantize_h(A)
        quantize_wd(0)
        quantize_h(B)
        quantize_x(3)
        weave_wd(2, 1, 2)
        weave_wd(3, 0, 1)
        up(C, 0, 0)
        gate_wide(C, 1)
        up(C, 0, 1)
        up(C, 1, 0)
        up(C, 1, 1)
        gate_wide(D, 0)
        up_chunk(D, 0, 0)
        quantize_wd(1)
        quantize_h(C)
        down_tile(0, (A, B))
        gate_chunk(D, 1, 0)
        down_tile(1, (A, B))
        gate_chunk(D, 1, 1)
        up_chunk(D, 1, 0)
        gate_chunk(E, 0, 0)
        up_chunk(D, 0, 1)
        down_tile(2, (A, B))
        quantize_chunk(D, 0)
        gate_chunk(E, 1, 0)
        up_chunk(D, 1, 1)
        down_tile(3, (A, B))
        up(E, 0, 0)
        down(C, 0)
        quantize_chunk(D, 1)
        up(E, 1, 0)
        down(C, 1)
        down_chunk(D, 0)
        quantize_h(E, 0, 1)
        quantize_h(E, 1, 1)
        down_chunk(D, 1)
        down_last(0)
        down_last(1)
        store(E, 0, 2, accs[0], "vector", nc.sync)
        store(E, 2, 2, accs[1], "scalar", nc.scalar)
